import numpy as np, ml_dtypes
CORES = [40,41,42,43,44,45,46,47]
N = 8
BF = ml_dtypes.bfloat16
V, L, A, T = 4096, 192, 1024, 4
H = L // 2; B = V - T * H
def draw0(rng):
    ax = np.clip(np.floor(rng.random((N, 8, 1, V)) * 300 - 22 + 140 * (rng.random((N, 8, 16, V)) - 0.5)), 0, 255).astype(np.int64)
    zp = np.clip(np.floor(rng.random((N, 8, 1, A)) * 170 + 40 + 160 * (rng.random((N, 8, 16, A)) - 0.5)), 0, 255).astype(np.int64)
    p = np.clip(np.floor(rng.random((N, 8, 1, L)) * 130 + 60 + 160 * (rng.random((N, 8, 16, L)) - 0.5)), 0, 255).astype(np.int64)
    near = (rng.random((N, 8, 1, H)) < 0.6) & (rng.random((N, 8, 16, H)) > 0.15)
    p[..., 1::2] = np.where(near, p[..., ::2], p[..., 1::2])
    rt = rng.integers(0, V, (N, 8, 16, A)); ex = rng.integers(0, V, (N, 8, 16, L))
    ex[..., 1::2] = np.where(rng.random((N, 8, 16, H)) < 0.2, ex[:, :, ::-1, ::2], ex[..., 1::2])
    return ax, rt, zp, ex, p, rng.integers(0, 4096, (N, 8, 16)), rng.integers(0, 4096, (N, 8, 16))
def pack(ax, rt, zp, ex, p, wt, km):
    b = lambda a: np.ascontiguousarray(a.reshape(N, 128, -1)).astype(np.float32).astype(BF)
    w = lambda a: np.ascontiguousarray(a.reshape(N, 128, -1)).astype(np.int32)
    return {"ax": b(ax), "rt": w(rt), "zp": b(zp), "ex": w(ex), "p0": b(p), "wt": w(wt), "km": w(km)}
def setup_inputs(rng):
    return pack(*draw0(rng))
def setup_inputs_spread(rng):
    def uneven(n): return np.minimum(np.floor(np.exp2(1 + 7.3 * rng.random((N, 8, 1, n))) * rng.random((N, 8, 16, n))), 255).astype(np.int64)
    ax, zp, p = uneven(V), uneven(A), uneven(L)
    p[..., 1::2] = np.where(rng.random((N, 8, 1, H)) < 0.4, p[..., ::2], p[..., 1::2])
    rt = np.minimum(np.floor(V * rng.random((N, 8, 16, A)) ** (0.5 + 3 * rng.random((N, 8, 1, A)))), V - 1).astype(np.int64)
    ex = np.minimum(np.floor(V * rng.random((N, 8, 16, L)) ** (0.5 + 3 * rng.random((N, 8, 1, L)))), V - 1).astype(np.int64)
    wt = np.minimum(np.floor(np.exp2(12.1 * rng.random((N, 8, 16)))) - 1, 4095).astype(np.int64)
    km = np.minimum(np.floor(np.exp2(12.1 * rng.random((N, 8, 16)))) - 1, 4095).astype(np.int64)
    return pack(ax, rt, zp, ex, p, wt, km)
def setup_inputs_ends(rng):
    den = np.array([0.0, 0.1, 0.25, 0.5, 0.75, 1.0])
    ax = 255 * (rng.random((N, 8, 16, V)) < rng.choice(den, (N, 8, 1, V))); zp = 255 * (rng.random((N, 8, 16, A)) < rng.choice(den, (N, 8, 1, A)))
    p = 255 * (rng.random((N, 8, 16, L)) < rng.choice(np.array([0.0, 0.25, 0.5, 0.75, 0.9, 1.0]), (N, 8, 1, L)))
    p[..., 1::2] = np.where(rng.random((N, 8, 1, H)) < 0.5, p[..., ::2], p[..., 1::2])
    for g, (a, b) in enumerate(((0.0, 0.4), (0.2, 1.0), (0.3, 0.7), (0.4, 0.0), (0.5, 0.3), (0.7, 0.2), (1.0, 0.3), (0.3, 0.5))):
        ax[:, g, :, 0] = 255 * (rng.random((N, 16)) < a); ax[:, g, :, V - 1] = 255 * (rng.random((N, 16)) < b)
    def names(n): return np.where(rng.random((N, 8, 16, n)) < 0.85, (V - 1) * rng.integers(0, 2, (N, 8, 16, n)), rng.integers(0, V, (N, 8, 16, n)))
    rt, ex = names(A), names(L)
    wt = 4095 * rng.integers(0, 2, (N, 8, 16)); km = 4095 * rng.integers(0, 2, (N, 8, 16))
    wt[:, 7] = 4095; wt[:, 5:7, 15] = 4095; wt[:, 0, 0] = 0; wt[:, 0, 1] = 4095
    for m, k in ((0, 0), (1, 4095), (3, 8), (9, 3856), (15, 3841)): km[:, 5:, m] = k
    one = np.zeros(16, np.int64); one[15] = 1
    for i in (0, 1, L - 2, L - 1): p[:, 5:, :, i] = one
    for i in (2, 3, L - 4, L - 3): p[:, 7, :, i] = 255; p[:, 6, :, i] = 0
    p[N - 1, 7, :, L - 2:] = 255
    for h in (3840, 3841, 4095, 4080, 3832): zp[:, 5:, :, (h * A) >> 12] = 255
    zp[:, 6, :, (4080 * A) >> 12] = 0; zp[:, 6, :, (4095 * A) >> 12] = 0; zp[:, 5, :, (4095 * A) >> 12] = 0
    for h in (8, 4088, 24, 264, 136): zp[:, 7, :, (h * A) >> 12] = 0
    zp[:, 6, :, 0] = 255
    return pack(ax, rt, zp, ex, p, wt, km)
def setup_inputs_corners(rng):
    ax, rt, zp, ex, p, wt, km = draw0(rng)
    cnt = rng.integers(0, 17, (N, 8, 1, V)); cnt[..., :17] = np.arange(17)
    hi = ((np.arange(16)[:, None] + rng.integers(0, 16, (N, 8, 1, V))) & 15) < cnt
    ax = np.where(hi, rng.integers(139, 256, ax.shape), rng.integers(0, 111, ax.shape))
    p = rng.integers(111, 140, p.shape); p[..., 1::2] = np.where(rng.random((N, 8, 1, H)) < 0.5, p[..., ::2], p[..., 1::2])
    sets = ((0, 1, 2, 3), (9, 10, 12, 16), (3, 4), (4, 5, 6, 7, 8), (8, 9), tuple(range(17)), (8,), ())
    full = int(rng.integers(0, N))
    for q in range(N):
        for g in range(8):
            s = 0 if q == full else (q + g) & 7
            cand = np.flatnonzero(np.isin(cnt[q, g, 0], np.array(sets[s], np.int64))) if s < 7 else np.array([0, B - 1, B, B + H - 1, B + H, V - 2, V - 1])
            if s == 6: cand = cand[:1]
            rt[q, g] = cand[rng.integers(0, len(cand), (16, A))]
    nm = (rng.integers(0, V, (N, 8, 1, H)) + (2 * rng.integers(0, V // 2, (N, 8, 1, H)) + 1) * np.arange(32)[:, None]) & (V - 1)
    ea, eb = nm[:, :, :16], nm[:, :, 16:]; rep = np.broadcast_to(nm[:, :, :1], ea.shape)
    kd = (np.arange(H)[None, None, None, :] + np.arange(8)[None, :, None, None] + np.arange(N)[:, None, None, None]) % 6
    lone = eb.copy(); lone[:, :, 0] = ea[:, :, 15]
    ex[..., ::2] = np.where(kd >= 4, rep, ea)
    ex[..., 1::2] = np.where(kd == 0, ea, np.where(kd == 1, ea[:, :, ::-1], np.where(kd == 3, lone, np.where(kd == 4, rep, eb))))
    ch = rng.integers(0, 3, (N, 8, 1, A)); ch[:, 1] = 0
    zp = np.take_along_axis(rng.integers(0, 256, (N, 8, 16, 3)), ch, 3)
    km[:, 2] = rng.integers(0, 4096, (N, 1)); km[:, 3, ::2] = 0; km[:, 3, 1::2] = 4095; wt[:, 4] = 0; wt[:, 6, 1:] = 0; wt[:, 6, 0] = 4095
    return pack(ax, rt, zp, ex, p, wt, km)
def setup_inputs_alike(rng):
    ax, rt, zp, ex, p, wt, km = draw0(rng)
    p[:, ::2] = p[:, ::2, :, :1]
    p[:, 1::2] = np.take_along_axis(p[:, 1::2, :, :4], rng.integers(0, 4, (N, 4, 1, L)), 3)
    rt = np.take_along_axis(rt[..., :8], rng.integers(0, 8, (N, 8, 1, A)), 3)
    rt[:, 3] = rng.choice(np.array([0, V - 1, B, B - 1]), (N, 16, A))
    ex[:, ::2] = rng.choice(np.array([0, 5, B - 1, B, B + H, V - 1]), (N, 4, 16, L))
    zp[:, 4:] = np.take_along_axis(zp[:, 4:, :, :16], rng.integers(0, 16, (N, 4, 1, A)), 3)
    wt[:, 5, :14] = rng.integers(3200, 4096, (N, 14)); wt[:, 5, 14] = 256; wt[:, 5, 15] = 1
    aim = np.array([0, 4095, 4075, 4077, 4087])[np.arange(H // 2) % 5]
    big = rng.integers(200, 256, (N, 14, H // 2))
    rest = (4096 + aim - np.sum(wt[:, 5, :14, None] * big, axis=1)) & 8191
    p[:, 5, :14, 2::4] = big; p[:, 5, 14, 2::4] = rest >> 8; p[:, 5, 15, 2::4] = rest & 255; p[:, 5, :, 3::4] = 0
    for k, v in ((5, V - 3), (6, V - 5), (7, V - 7)):
        rt[:, 5, k] = v; ax[:, 5, :, v] = 0; ax[:, 5, :4, v] = 255; ax[:, 5, 14:, v] = 255
    for v, u in ((V - 3, 4075), (V - 5, 4077), (V - 7, 4087), (V - 3, 4095), (V - 3, 4096)): ax[:, 5, :, (((v * u) >> 5) + v) & (V - 1)] = 255
    return pack(ax, rt, zp, ex, p, wt, km)
def check_inputs(d):
    bad = []
    for k, hi in (("ax", 255), ("rt", V - 1), ("zp", 255), ("ex", V - 1), ("p0", 255), ("wt", 4095), ("km", 4095)):
        v = np.asarray(d[k]).astype(np.float64)
        if not (np.min(v) >= 0 and np.max(v) <= hi): bad.append("range of " + k)
        elif np.any(v != np.floor(v)): bad.append("whole numbers of " + k)
    return bad
def pick(x, e):
    n = e.shape[3]
    return np.take_along_axis(x, e.reshape(N, 8, 1, 16 * n), 3).reshape(N, 8, 16, 16, n)
def reference(ax, rt, zp, ex, p0, wt, km):
    x = ax.astype(np.float32).astype(np.int64).reshape(N, 8, 16, V)
    r = np.zeros((N, 8, 16, A + T * L), np.int64); z = np.zeros((N, 8, 16, A + T * L), np.int64)
    r[..., :A] = rt.reshape(N, 8, 16, A); z[..., :A] = zp.astype(np.float32).astype(np.int64).reshape(N, 8, 16, A)
    e0 = ex.astype(np.int64).reshape(N, 8, 16, L); p = p0.astype(np.float32).astype(np.int64).reshape(N, 8, 16, L)
    w = wt.astype(np.int64).reshape(N, 8, 16, 1); k = km.astype(np.int64).reshape(N, 8, 16, 1); odd = np.zeros(N, np.int64)
    for t in range(T):
        n = A + L * t
        u = np.repeat(np.add.reduce(w * p, axis=2)[:, :, ::2] & 4095, 2, axis=2)[:, :, None, :]
        c = (((((u * u) >> 5) & 4095) + ((k * u) & 4095)) & 4095) * n >> 12
        score = np.sum(np.abs(pick(z, c) - p[:, :, :, None, :]), axis=2)
        a = np.minimum.reduce(score * 4096 + c, axis=2) & 4095
        e = np.take_along_axis(r, a[:, :, None, :], 3)
        v = np.sum(pick(x, e) >= p[:, :, :, None, :], axis=2)
        barred = v < 4 + odd[:, None, None, None]
        e2 = (((e * u) >> 5) + e + 77 * t) & (V - 1)
        v2 = np.sum(pick(x, e2) >= p[:, :, :, None, :], axis=2)
        f = np.where(barred, e0, np.where((v < 9) & (v2 >= v), e2, e))
        odd = np.sum(barred, axis=(1, 2, 3)) & 1
        fa, fb = f[..., ::2].copy(), f[..., 1::2].copy()
        same = fa[:, :, :, None, :] == fb[:, :, None, :, :]
        ca, cb = np.any(same, axis=3), np.any(same, axis=2)
        rec = np.maximum.reduce(np.where(ca[:, :, None], pick(x, fa), 0), axis=3)
        new = B + H * t + np.arange(H)
        f[..., ::2] = np.where(ca, new, fa); f[..., 1::2] = np.where(cb, new, fb)
        src = (np.arange(N) - 1 - t % 3) % N
        f, p = f[src], p[src]
        r[..., n:n + L] = f
        if t < T - 1: z[..., n:n + L] = p
        x[..., B + H * t:B + H * t + H] = rec[src]
        p = (p + 255 - np.take_along_axis(x, f[:, :, :1], 3)) >> 1
    return {"yr": r[..., A:].reshape(N, 128, T * L).astype(np.float32), "yp": p.reshape(N, 128, L).astype(np.float32)}

@@ -1,0 +1,595 @@
+from concourse.mybir import dt, AluOpType as A, ActivationFunctionType as F
+
+V, L, A0, TT = 4096, 192, 1024, 4
+H = L // 2
+XW = V + 512
+RW = A0 + TT * L
+CFG = {
+    "CH": ((0, 48), (48, 96)),
+    "ZP": ("SVS", "SSV"),
+    "VP": (("VVS", "VVS"), ("VVS", "SSV")),
+    "RG": ("S", "B"),
+    "PS": (6, 4),
+    "ORD": "h0 p0 h1 p1 s z0 E0 z1 E1 v00 v01 c0 v10 m0 v11 c1 m1",
+    "SLACK": 15.0, "SPL": 1, "PR": {},
+}
+DT = {"i": "int32", "u": "uint16", "f": "float32", "b": "bfloat16", "h": "float16"}
+ARENA = {"i": 4096, "u": 1024, "f": 2560, "b": 24576, "h": 5120}
+SCRATCH = {
+    "X": ("sbuf", [128, XW], "bfloat16"), "Xh": ("sbuf", [128, V], "bfloat16"), "Z": ("sbuf", [128, RW], "bfloat16"),
+    "R": ("sbuf", [128, RW], "float32"), "ri": ("sbuf", [128, A0], "int32"), "exi": ("sbuf", [128, L], "int32"),
+    "wi": ("sbuf", [128, 1], "int32"), "ki": ("sbuf", [128, 1], "int32"),
+    "pn": ("sbuf", [128, TT * L], "bfloat16"), "fnat": ("sbuf", [128, TT * L], "float32"), "yo": ("sbuf", [128, L], "float32"),
+    "f0s": ("sbuf", [128, TT * 16], "uint16"), "f0l": ("sbuf", [128, TT * 16], "uint16"),
+    "qs": ("sbuf", [128, TT * H], "bfloat16"), "ql": ("sbuf", [128, TT * H], "bfloat16"),
+}
+for _k in ARENA:
+    SCRATCH["ar_" + _k] = ("sbuf", [128, ARENA[_k]], DT[_k])
+PS = ("d0", "d1", "d2", "d3", "v1", "v2", "sc", "cm")
+for _n in PS:
+    SCRATCH[_n] = ("psum", [128, 512], "float32")
+LOADS = ("p0", "wt", "km", "zp", "rt", "ax", "ex")
+SEMAPHORES = ["cV", "cS", "cP", "cG", "sent", "stored"] + ["ld_" + n for n in LOADS] + ["ar_%s%d" % (k, t) for t in range(TT) for k in "pfqz"]
+RATE = {"V": 1.0, "S": 1.0, "P": 0.5, "G": 1.0}
+EST = {"gather": 1.56, "wake": 90.0, "dma": 2200.0, "send": 2300.0}
+WHERE = {}
+TOP = {}
+
+
+def need(kind, **names):
+    q = {"i": 8, "f": 8, "b": 16, "u": 16, "h": 16}[kind]
+    for n, w in names.items():
+        WHERE[n] = (kind, TOP.get(kind, 0))
+        TOP[kind] = TOP.get(kind, 0) + -(-w // q) * q
+
+
+def ap(T, n, lo, hi, st=1):
+    if n in WHERE:
+        k, o = WHERE[n]
+        n, lo, hi = "ar_" + k, lo + o, hi + o
+    return T[n][:, lo:hi:st] if st > 1 else T[n][:, lo:hi]
+
+
+def is32(n):
+    return WHERE[n][0] == "f" if n in WHERE else SCRATCH[n][2] == "float32"
+
+
+def rg_(b, lo, hi, st=1):
+    return (b, lo, hi, st, lo % st)
+
+
+def build():
+    WHERE.clear()
+    TOP.clear()
+    CH = CFG["CH"]
+    GC = EST["gather"]
+    NC = range(len(CH))
+    ops = []
+
+    def op(eng, cyc, w, r, fn, kind="c", name="", fix=0.0):
+        w, r = [x if len(x) == 5 else rg_(*x) for x in w], [x if len(x) == 5 else rg_(*x) for x in r]
+        ops.append({"e": eng, "c": cyc * 0.83 * RATE.get(eng, 1.0) + fix, "w": w, "r": r, "f": fn, "k": kind, "n": name})
+
+    def v(n, w, r, fn, name="", half=False, fix=0.0):
+        op("V", max(64, n * (0.5 if half else 1)), w, r, fn, name=name, fix=fix)
+
+    def s(n, w, r, fn, name="", fix=0.0):
+        op("S", max(64, n), w, r, fn, name=name, fix=fix)
+
+    def vm(buf, lo, hi, val, st=1):
+        v(hi - lo, [(buf, lo, hi)], [], lambda T, g: g.vector.memset(ap(T, buf, lo, hi, st), val), "memset", half=True)
+
+    def gsel(out, inp, n, pat, cmp_, base, cm, at=0):
+        op("G", 2 * n, [(out, at, at + n)], [(inp, 0, n)], lambda T, g: g.affine_select(ap(T, out, at, at + n), ap(T, inp, 0, n), pat, cmp_, 0.0, base, cm), fix=170, name="sel")
+
+    def giota(out, n, pat, base, cm, fl=True):
+        op("G", 2 * n, [(out, 0, n)], [], (lambda T, g: g.iota(ap(T, out, 0, n), pat, base, cm, allow_small_or_imprecise_dtypes=True)) if fl else (lambda T, g: g.iota(ap(T, out, 0, n), pat, base, cm)), fix=130, name="iota")
+
+    def vs(out, ol, oh, inp, il, ih, s1, op0, s2=None, op1=None, half=False, ost=1, ist=1, name="", scol=None):
+        def fn(T, g):
+            sc = ap(T, scol[0], scol[1], scol[1] + 1) if scol else s1
+            o, i = ap(T, out, ol, oh, ost), ap(T, inp, il, ih, ist)
+            if op1 is None:
+                return g.vector.tensor_scalar(o, i, sc, None, op0)
+            return g.vector.tensor_scalar(o, i, sc, s2, op0, op1)
+        v(-(-(ih - il) // ist), [(out, ol, oh, ost)], [(inp, il, ih, ist)] + ([(scol[0], scol[1], scol[1] + 1)] if scol else []), fn, name, half)
+
+    def vc(out, ol, oh, inp, il, ih, half=False, ost=1, ist=1, name=""):
+        v(-(-(ih - il) // ist), [(out, ol, oh, ost)], [(inp, il, ih, ist)], lambda T, g: g.vector.tensor_copy(ap(T, out, ol, oh, ost), ap(T, inp, il, ih, ist)), name, half)
+
+    def vt(out, ol, oh, a, al, ah, b, bl, bh, o_, name=""):
+        n = ah - al
+        v(n if (a in PS or b in PS) else 2 * n, [(out, ol, oh)], [(a, al, ah), (b, bl, bh)],
+          lambda T, g: g.vector.tensor_tensor(ap(T, out, ol, oh), ap(T, a, al, ah), ap(T, b, bl, bh), o_), name)
+
+    def act(out, ol, oh, inp, il, ih, fn_, ost=1, ist=1, bias=0.0, scale=1.0, bcol=None, acc=None, name=""):
+        def fn(T, g):
+            kw = {"scale": scale, "bias": ap(T, bcol, 0, 1) if bcol else bias}
+            if acc:
+                kw["accum_out"] = ap(T, acc[0], acc[1], acc[1] + 1)
+            return g.scalar.activation(ap(T, out, ol, oh, ost), ap(T, inp, il, ih, ist), fn_, **kw)
+        s(-(-(ih - il) // ist), [(out, ol, oh, ost)] + ([(acc[0], acc[1], acc[1] + 1)] if acc else []), [(inp, il, ih, ist)] + ([(bcol, 0, 1)] if bcol else []), fn, name)
+
+    def gather_v(out, ol, oh, win, wh, off, fl, fh, name, in1=None, o_=None):
+        def fn(T, g):
+            ind = T[win][:, 0:wh].indirect(ap(T, off, fl, fh))
+            if in1 is None:
+                return g.vector.tensor_copy(ap(T, out, ol, oh), ind)
+            return g.vector.tensor_tensor(ap(T, out, ol, oh), ind, ap(T, *in1), o_)
+        v((oh - ol) * GC, [(out, ol, oh)], [(win, 0, wh), (off, fl, fh)] + ([in1] if in1 else []), fn, name, fix=50)
+
+    def gather_s(out, ol, oh, win, wh, off, fl, fh, name):
+        s((oh - ol) * GC, [(out, ol, oh)], [(win, 0, wh), (off, fl, fh)],
+          lambda T, g: g.scalar.activation(ap(T, out, ol, oh), T[win][:, 0:wh].indirect(ap(T, off, fl, fh)), F.Copy), name, fix=65)
+
+    def groups(grs, name):
+        cost, w, r = 0, [], []
+        for prs, out, ol, oh, ost in grs:
+            w.append((out, ol, oh, ost))
+            for x in prs:
+                n = -(-(x[5] - x[4]) // x[6])
+                cost += max(min(64, x[2] - x[1]), n) * (4 if is32(x[3]) else 1)
+                r += [(x[0], x[1], x[2], 1), x[3:7]]
+
+        def fn(T, g):
+            ins = None
+            for prs, out, ol, oh, ost in grs:
+                for y, x in enumerate(prs):
+                    ins = g.tensor.matmul(ap(T, out, ol, oh, ost), ap(T, x[0], x[1], x[2]), ap(T, x[3], x[4], x[5], x[6]), y == 0, y == len(prs) - 1)
+            return ins
+        op("P", cost, w, sorted(set(r)), fn, name=name)
+
+    bank = [0]
+
+    def dbank():
+        bank[0] = (bank[0] + 1) % 4
+        return "d%d" % bank[0]
+
+    need("b", ones=144, tmpa=144, tmpb=144, BB=128, W8=144, W4=144, I1=128, IN=128, I8=128, IB=128, IC=128, BG=128, smax=1536, p=L, prep=L * 16)
+    need("f", ones32=128, cf=8, id32=128, up32=128, dn32=128, iot=16, iom=L, ion=H, M16=16, smin=L, pc=L, bar=1, cb=8)
+    need("h", WH=128, WL=128, J1=128, JN=128, BS=2048, Q=512, N16=TT * H, E16=L, p16=L, mk=H)
+    need("i", ci=8, cj=8)
+    for c in NC:
+        np_ = CH[c][1] - CH[c][0]
+        nl, C = 2 * np_, str(c)
+        need("i", **{x + C: w for x, w in (("si", np_), ("ul", nl), ("uu", np_), ("uv", np_), ("ku", np_), ("li", 12), ("t1", nl), ("t3", nl), ("fe", nl), ("f", nl), ("ff", nl))})
+        need("u", **{x + C: w for x, w in (("cl", np_), ("al", 12), ("el", nl), ("e2l", nl), ("lu", np_))})
+        need("f", **{x + C: w for x, w in (("kt", nl), ("ks", nl), ("ef", nl), ("k1", nl), ("rl", np_))})
+        need("h", **{x + C: w for x, w in (("c16", nl), ("lh", 12), ("f16", nl), ("F16", nl), ("FT", nl))})
+        need("b", **{x + C: w for x, w in (("gz", 16 * np_), ("dz", 16 * nl), ("g1", 16 * nl), ("g2", 16 * nl), ("x1", 16 * nl), ("bb", nl), ("eq", 16 * np_), ("rs", 16 * np_))})
+
+    for q, nm, buf, wid in (("Y", "p0", "pn", L), ("Y", "wt", "wi", 1), ("Y", "km", "ki", 1), ("SD", "zp", "Z", A0), ("Y", "ax", "X", V), ("SD", "rt", "ri", A0), ("Y", "ex", "exi", L)):
+        op(q, 0, [(buf, 0, wid)], [], (lambda T, q_, nm=nm, buf=buf, wid=wid: q_.dma_start(T[buf][:, 0:wid], T[nm][:, :])), kind="load", name=nm)
+    vm("ones", 0, 144, 1.0)
+    vm("ones32", 0, 128, 1.0)
+    gsel("tmpa", "ones", 128, [[-16, 8], [0, 16]], A.is_ge, 0, 1)
+    gsel("BB", "tmpa", 128, [[16, 8], [0, 16]], A.is_ge, 15, -1)
+    vs("ci", 0, 1, "wi", 0, 1, 63, A.bitwise_and)
+    vc("cf", 0, 1, "ci", 0, 1)
+    vt("cf", 1, 2, "wi", 0, 1, "ci", 0, 1, A.subtract)
+    vc("cf", 2, 3, "ki", 0, 1)
+    vs("WH", 0, 128, "BB", 0, 128, None, A.mult, scol=("cf", 1), half=True)
+    vs("WL", 0, 128, "BB", 0, 128, None, A.mult, scol=("cf", 0), half=True)
+    vs("mk", 0, H, "ones", 0, H, -1024.0, A.mult, half=True)
+    gsel("id32", "ones32", 128, [[-1, 128]], A.is_equal, 0, 1)
+    vc("I1", 0, 128, "id32", 0, 128)
+    vs("IN", 0, 128, "id32", 0, 128, -1.0, A.mult)
+    for c, (j0, j1) in enumerate(CH):
+        m = j1 - j0
+        for b in (0, 1):
+            vs("p16", 2 * j0 + b * m, 2 * j0 + b * m + m, "pn", 2 * j0 + b, 2 * j1, 1024.0, A.add, half=True, ist=2)
+        vs("p", 2 * j0, 2 * j1, "p16", 2 * j0, 2 * j1, -1024.0, A.add, half=True, name="p")
+    act("cb", 0, 4, "ones32", 0, 4, F.Sigmoid, name="table")
+
+    def setup():
+        gsel("tmpb", "ones", 144, [[-16, 9], [-1000, 16]], A.is_ge, 16, 1)
+        gsel("tmpa", "tmpb", 144, [[16, 9], [0, 16]], A.is_ge, -1, -1)
+        vs("W4", 0, 144, "tmpa", 0, 144, 4096.0, A.mult, half=True)
+        vs("J1", 0, 128, "id32", 0, 128, 1.0, A.mult)
+        giota("iom", L, [[0, L // 16], [1, 16]], 0, 0)
+        vs("smin", 0, L, "iom", 0, L, 0.0, A.is_equal, 33554432.0, A.mult)
+        giota("cj", 1, [[1, 1]], 0, 1, fl=False)
+        vs("ci", 1, 2, "cj", 0, 1, 4, A.logical_shift_right, 1, A.bitwise_and)
+        vc("cf", 4, 5, "ci", 1, 2)
+        vs("cf", 5, 6, "ci", 1, 2, -1.0, A.mult, 1.0, A.add)
+        gsel("up32", "ones32", 128, [[-1, 128]], A.is_equal, 16, 1)
+        gsel("dn32", "ones32", 128, [[-1, 128]], A.is_equal, -16, 1)
+        vs("Q", 0, 128, "id32", 0, 128, None, A.mult, scol=("cf", 5))
+        vs("Q", 384, 512, "id32", 0, 128, None, A.mult, scol=("cf", 4))
+        vs("Q", 128, 256, "up32", 0, 128, None, A.mult, scol=("cf", 5))
+        vs("Q", 256, 384, "dn32", 0, 128, None, A.mult, scol=("cf", 4))
+        vc("R", 0, A0, "ri", 0, A0, name="R")
+        vm("X", V, XW, 0.0)
+        vm("bar", 0, 1, -1280.0)
+        vs("W8", 0, 144, "tmpa", 0, 144, 8192.0, A.mult, half=True)
+        vs("BG", 0, 128, "BB", 0, 128, -4352.0, A.mult, half=True)
+        vs("IB", 0, 128, "I1", 0, 128, 1048576.0, A.mult, half=True)
+        vs("IC", 0, 128, "I1", 0, 128, -129024.0, A.mult, half=True)
+        for c, (j0, j1) in enumerate(CH):
+            m = j1 - j0
+            for b in (0, 1):
+                vs("E16", 2 * j0 + b * m, 2 * j0 + b * m + m, "exi", 2 * j0 + b, 2 * j1, -2048.0, A.add, ist=2)
+        vs("I8", 0, 128, "I1", 0, 128, 8192.0, A.mult, half=True)
+        vs("JN", 0, 128, "id32", 0, 128, -1.0, A.mult)
+        vs("ci", 2, 3, "cj", 0, 1, 15, A.bitwise_and)
+        vc("cf", 3, 4, "ci", 2, 3)
+        giota("iot", 16, [[1, 16]], 0, 0)
+        vs("M16", 0, 16, "iot", 0, 16, None, A.is_equal, scol=("cf", 3))
+        for k in range(16):
+            vs("BS", 128 * k, 128 * k + 128, "BB", 0, 128, None, A.mult, scol=("M16", k), half=True)
+        giota("ion", H, [[1, H]], -384, 0)
+        for t in range(TT):
+            vs("N16", H * t, H * t + H, "ion", 0, H, float(H * t), A.add)
+        vm("smax", 0, 1536, 1.0)
+        vm("smax", 0, 1536, 0.0, st=16)
+        for k in range(4):
+            vs("Xh", 1024 * k, 1024 * k + 1024, "X", 1024 * k, 1024 * k + 1024, -0.5, A.mult, half=True, name="Xh")
+
+    def hash_(t, c):
+        n, (j0, j1), C = A0 + L * t, CH[c], str(c)
+        a, m, o = 2 * j0, j1 - j0, 416 + j0
+        groups([([(x, 0, 128, "mk", 0, m, 1) for x in ("WH", "WL")] + [(x, 0, 128, "p16", a, a + m, 1) for x in ("WH", "WL")], "sc", o, o + m, 1)], "u")
+        vc("si" + C, 0, m, "sc", o, o + m, name="si")
+        vs("ul" + C, 0, m, "si" + C, 0, m, 4095, A.bitwise_and, name="u")
+        vt("uu" + C, 0, m, "ul" + C, 0, m, "ul" + C, 0, m, A.mult, "uu")
+        vs("ku" + C, 0, m, "ul" + C, 0, m, None, A.mult, scol=("cf", 2), name="ku")
+        vs("uv" + C, 0, m, "uu" + C, 0, m, 5, A.arith_shift_right, 4095, A.bitwise_and, name="uv")
+        vt("uu" + C, 0, m, "ku" + C, 0, m, "uv" + C, 0, m, A.add, "hh")
+        vs("si" + C, 0, m, "uu" + C, 0, m, 4095, A.bitwise_and, name="hm")
+        vs("cl" + C, 0, m, "si" + C, 0, m, n / 4096.0, A.mult, -0.5 + 2.0 ** -13, A.add, name="cl")
+        for b in (0, 1):
+            vc("c16" + C, b * m, b * m + m, "cl" + C, 0, m, half=True, name="c16")
+        vc("ul" + C, m, 2 * m, "ul" + C, 0, m, name="uB")
+
+    def prep(c):
+        j0, j1 = CH[c]
+        for k in range(16):
+            if k < CFG["PS"][c]:
+                act("prep", 32 * j0 + k, 32 * j1, "p", 2 * j0, 2 * j1, F.Copy, ost=16, name="prep")
+            else:
+                vc("prep", 32 * j0 + k, 32 * j1, "p", 2 * j0, 2 * j1, half=True, ost=16, name="prep")
+
+    def zstage(t, c):
+        n, (j0, j1), C = A0 + L * t, CH[c], str(c)
+        b, m, path = 2 * j0, j1 - j0, CFG["ZP"][c]
+        for x, pa in enumerate(path):
+            j = 16 * x
+            if pa == "S":
+                gather_s("gz" + C, 16 * j, 16 * j + 256, "Z", n, "cl" + C, j, j + 16, "Zg")
+                d = dbank()
+                groups([([("I1", 0, 128, "gz" + C, 16 * j, 16 * j + 256, 1), ("IN", 0, 128, "prep", 16 * (b + h * m + j), 16 * (b + h * m + j) + 256, 1)], d, 256 * h, 256 * h + 256, 1) for h in (0, 1)], "Zsub")
+            for h in (0, 1):
+                l = 16 * (h * m + j)
+                if pa == "S":
+                    act("dz" + C, l, l + 256, d, 256 * h, 256 * h + 256, F.Abs, name="Zabs")
+                else:
+                    gather_v("g1" + C, l, l + 256, "Z", n, "cl" + C, j, j + 16, "Zfused", in1=("prep", 16 * b + l, 16 * b + l + 256), o_=A.subtract)
+                    act("dz" + C, l, l + 256, "g1" + C, l, l + 256, F.Abs, name="Zabs")
+
+    def relay(src, so, st, out, o0, q):
+        return [([("Q", 256 * hi + 128 * gl, 256 * hi + 128 * gl + 128, src, so + st * gl, st * q, 2 * st) for gl in (0, 1)], out, o0 + hi, o0 + q, 2) for hi in (0, 1)]
+
+    def elect(t, c):
+        n, (j0, j1), C = A0 + L * t, CH[c], str(c)
+        m, o = j1 - j0, 2 * j0
+        nl = 2 * m
+        q = nl // 16
+        r0 = 208 + 16 * c
+        groups([([("W4", 16 - k, 144 - k, "dz" + C, k, nl * 16, 16) for k in range(16)] + [("J1", 0, 128, "c16" + C, 0, nl, 1)], "sc", o, o + nl, 1)], "score")
+        v(nl, [("kt" + C, 0, nl)], [("sc", o, o + nl)], lambda T, g: g.vector.transpose(ap(T, "kt" + C, 0, nl), ap(T, "sc", o, o + nl)), "kT")
+        v(nl, [("ks" + C, 0, nl)], [("kt" + C, 0, nl), ("smin", 0, nl)],
+          lambda T, g: g.vector.tensor_tensor_scan(ap(T, "ks" + C, 0, nl), ap(T, "smin", 0, nl), ap(T, "kt" + C, 0, nl), 33554432.0, A.max, A.min), "kmin")
+        vc("li" + C, 0, q, "ks" + C, 15, nl, ist=16, name="li")
+        vs("li" + C, 0, q, "li" + C, 0, q, 4095, A.bitwise_and, name="lm")
+        vc("lh" + C, 0, q, "li" + C, 0, q, name="lh")
+        groups(relay("lh" + C, 0, 1, "sc", r0, q), "relay")
+        vc("al" + C, 0, q, "sc", r0, r0 + q, name="al")
+        gather_v("el" + C, 0, nl, "R", n, "al" + C, 0, q, "eL")
+        gather_v("t1" + C, 0, nl, "R", n, "al" + C, 0, q, "eu", in1=("ul" + C, 0, nl), o_=A.mult)
+        gather_s("ef" + C, 0, nl, "R", n, "al" + C, 0, q, "ef")
+        e7 = "ef" + C
+        if t:
+            e7 = "kt" + C
+            act(e7, 0, nl, "ef" + C, 0, nl, F.Identity, bias=float(77 * t), name="e77")
+        vs("t1" + C, 0, nl, "t1" + C, 0, nl, 5, A.arith_shift_right, name="t2")
+        vt("t3" + C, 0, nl, "t1" + C, 0, nl, e7, 0, nl, A.add, "t3")
+        vs("t3" + C, 0, nl, "t3" + C, 0, nl, 4095, A.bitwise_and, name="e2")
+        vc("e2l" + C, 0, nl, "t3" + C, 0, nl, name="e2L")
+
+    def vstage(t, c, w):
+        (j0, j1), C = CH[c], str(c)
+        b, lst, gb = 2 * j0, ("el", "e2l")[w] + C, ("g1", "g2")[w] + C
+        path = CFG["VP"][c][w]
+        x = 0
+        while x < len(path):
+            if path[x] == "V":
+                y = x
+                while y < len(path) and path[y] == "V" and (y == x or not CFG["SPL"]):
+                    y += 1
+                gather_v(gb, 512 * x, 512 * y, "X", XW, lst, 32 * x, 32 * y, "votes", in1=("prep", 16 * b + 512 * x, 16 * b + 512 * y), o_=A.is_ge)
+                x = y
+            else:
+                gather_s("x1" + C, 512 * x, 512 * x + 512, "X", XW, lst, 32 * x, 32 * x + 32, "votesS")
+                d = dbank()
+                groups([([("I1", 0, 128, "x1" + C, 512 * x, 512 * x + 512, 1), ("IN", 0, 128, "prep", 16 * b + 512 * x, 16 * b + 512 * x + 512, 1)], d, 0, 512, 1)], "vsub")
+                act(gb, 512 * x, 512 * x + 512, d, 0, 512, F.Sigmoid, bias=128.0, scale=256.0, name="vsig")
+                x += 1
+
+    def choice(t, c):
+        (j0, j1), C = CH[c], str(c)
+        b = 2 * j0
+        nl = 2 * (j1 - j0)
+        o, o2 = b, 192 + b
+        groups([([("BG", 0, 128, "ones", 0, nl, 1)] + [("W8", 16 - k, 144 - k, "g1" + C, k, nl * 16, 16) for k in range(16)], "v1", o, o + nl, 1)], "v1sum")
+        act("bb" + C, 0, nl, "v1", o, o + nl, F.Sigmoid, scale=-1.0 / 32, bcol="bar", acc=("cb", c), name="barred")
+        vt("k1" + C, 0, nl, "v1", o, o + nl, "ef" + C, 0, nl, A.add, "k1")
+        groups([([("J1", 0, 128, "E16", b, b + nl, 1), ("IC", 0, 128, "ones", 0, nl, 1), ("IB", 0, 128, "bb" + C, 0, nl, 1)], "v1", o2, o2 + nl, 1)], "k3")
+        groups([([("W8", 16 - k, 144 - k, "g2" + C, k, nl * 16, 16) for k in range(16)], "v2", o, o + nl, 1)], "v2sum")
+        act("v2", o2, o2 + nl, "v2", o, o + nl, F.Relu, bias=65536.0, scale=-1.0, name="r")
+        vt("v2", o2, o2 + nl, "t3" + C, 0, nl, "v2", o2, o2 + nl, A.subtract, "k2")
+        vt("k1" + C, 0, nl, "v2", o2, o2 + nl, "k1" + C, 0, nl, A.max, "max")
+        vt("fe" + C, 0, nl, "v1", o2, o2 + nl, "k1" + C, 0, nl, A.max, "max")
+        vs("f" + C, 0, nl, "fe" + C, 0, nl, 4095, A.bitwise_and, name="f")
+        vs("f16" + C, 0, nl, "f" + C, 0, nl, -2048.0, A.add, name="f16")
+
+    def parity():
+        groups([([("ones32", 0, 128, "cb", c, c + 1, 1) for c in NC], "cm", 500, 501, 1)], "par")
+        vc("ci", 4, 5, "cm", 500, 501)
+        vs("ci", 5, 6, "ci", 4, 5, 1, A.bitwise_and)
+        vs("bar", 0, 1, "ci", 5, 6, 256.0, A.mult, -1280.0, A.add)
+
+    def common(t, c):
+        (j0, j1), C = CH[c], str(c)
+        m = j1 - j0
+        nl = 2 * m
+        per = 16 if m <= 32 else 8
+        for h in range(16 // per):
+            d = dbank()
+            groups([([("BS", 128 * k, 128 * k + 128, "f16" + C, m, nl, 1), ("JN", 0, 128, "f16" + C, 0, m, 1)], d, m * (k - per * h), m * (k - per * h) + m, 1) for k in range(per * h, per * h + per)], "bcast")
+            vs("eq" + C, m * per * h, m * per * h + m * per, d, 0, m * per, 0.0, A.is_equal, name="eq")
+        nn = ("J1", 0, 128, "N16", H * t + j0, H * t + j1, 1)
+        groups([([nn] + [("I8", 0, 128, "eq" + C, m * k, m * k + m, 1) for k in range(16)], "cm", j0, j1, 1)], "ca")
+        act("rl" + C, 0, m, "cm", j0, j1, F.Relu, scale=-1.0, bias=4096.0, name="rl")
+        vt("rl" + C, 0, m, "f" + C, 0, m, "rl" + C, 0, m, A.max, "ls")
+        vc("lu" + C, 0, m, "rl" + C, 0, m, name="lu")
+        b0 = 256 + j0
+        groups([([nn] + [("W8", 16 - k, 144 - k, "eq" + C, m * k, m * k + m, 1) for k in range(16)], "sc", b0, b0 + m, 1)], "cb")
+        way = CFG["RG"][c]
+        if way == "B":
+            gather_s("gz" + C, 0, m * 8, "X", XW, "lu" + C, 0, m // 2, "rg")
+            gather_v("gz" + C, m * 8, m * 16, "X", XW, "lu" + C, m // 2, m, "rg")
+        elif way == "S":
+            gather_s("gz" + C, 0, m * 16, "X", XW, "lu" + C, 0, m, "rg")
+        else:
+            gather_v("gz" + C, 0, m * 16, "X", XW, "lu" + C, 0, m, "rg")
+        vt("fe" + C, 0, m, "cm", j0, j1, "f" + C, 0, m, A.max, "fx")
+        vt("fe" + C, m, nl, "sc", b0, b0 + m, "f" + C, m, nl, A.max, "fx")
+        vs("ff" + C, 0, nl, "fe" + C, 0, nl, 4095, A.bitwise_and, name="F")
+        vs("F16" + C, 0, nl, "ff" + C, 0, nl, -2048.0, A.add, name="F16")
+        v(nl, [("FT" + C, 0, nl)], [("F16" + C, 0, nl)], lambda T, g: g.vector.transpose(ap(T, "FT" + C, 0, nl), ap(T, "F16" + C, 0, nl)), "FT", half=True)
+        f0, q, l0 = 300 + 16 * c, nl // 16, 16 * t + j0 // 8
+        groups(relay("FT" + C, 0, 16, "cm", f0, q), "relayF")
+        vs("f0s", l0, l0 + q, "cm", f0, f0 + q, 2048.0, A.add, name="f0s")
+        for bb in (0, 1):
+            vc("fnat", L * t + 2 * j0 + bb, L * t + 2 * j1, "ff" + C, m * bb, m * bb + m, ost=2, name="fnat")
+        v(m * 16, [("rs" + C, 0, m * 16)], [("gz" + C, 0, m * 16), ("smax", 0, m * 16)],
+          lambda T, g: g.vector.tensor_tensor_scan(ap(T, "rs" + C, 0, m * 16), ap(T, "smax", 0, m * 16), ap(T, "gz" + C, 0, m * 16), 0.0, A.mult, A.max), "rscan", half=True)
+        vc("qs", H * t + j0, H * t + j1, "rs" + C, 15, m * 16, half=True, ist=16, name="qs")
+
+    def send(t, kind, src, s0, s1, dst, d0, d1):
+        op("R", 0, [], [(src, s0, s1)], (t, dst, d0, d1, src, s0, s1, "ar_%s%d" % (kind, t)), kind="send", name="send_" + kind)
+        op("A", 0, [(dst, d0, d1)], [], "ar_%s%d" % (kind, t), kind="arr", name="arr_" + kind)
+
+    for t in range(TT):
+        n = A0 + L * t
+        for c, (j0, j1) in enumerate(CH):
+            m = j1 - j0
+            for b in (0, 1):
+                if t:
+                    act("pn", L * t + 2 * j0 + b, L * t + 2 * j1, "p", 2 * j0 + b * m, 2 * j0 + b * m + m, F.Copy, ost=2, name="pnat")
+        for x in CFG["ORD"].split():
+            k, c = x[0], int(x[1]) if len(x) > 1 else 0
+            if k == "s":
+                send(t, "p", "pn", L * t, L * t + L, "Z", n, n + L)
+                if t == 0:
+                    setup()
+            elif k == "v":
+                vstage(t, c, int(x[2]))
+            elif k == "p":
+                prep(c)
+            else:
+                {"h": hash_, "z": zstage, "E": elect, "c": choice, "m": common}[k](t, c)
+        send(t, "z", "f0s", 16 * t, 16 * t + 12, "f0l", 16 * t, 16 * t + 12)
+        send(t, "q", "qs", H * t, H * t + H, "ql", H * t, H * t + H)
+        send(t, "f", "fnat", L * t, L * t + L, "R", n, n + L)
+        for c, (j0, j1) in enumerate(CH):
+            m = j1 - j0
+            for b in (0, 1):
+                act("pc", 2 * j0 + b * m, 2 * j0 + b * m + m, "Z", n + 2 * j0 + b, n + 2 * j1, F.Identity, ist=2, scale=0.5, bias=1151.25, name="pc")
+        vs("Xh", 3712 + H * t, 3712 + H * t + H, "ql", H * t, H * t + H, -0.5, A.mult, half=True, name="Xhrec")
+        gather_v("p16", 0, L, "Xh", V, "f0l", 16 * t, 16 * t + 12, "newp", in1=("pc", 0, L), o_=A.add)
+        if t < TT - 1:
+            vs("p", 0, L, "p16", 0, L, -1024.0, A.add, half=True, name="p")
+            vc("X", 3712 + H * t, 3712 + H * t + H, "ql", H * t, H * t + H, half=True, name="Xrec")
+            parity()
+        else:
+            for c, (j0, j1) in enumerate(CH):
+                m = j1 - j0
+                for b in (0, 1):
+                    vs("yo", 2 * j0 + b, 2 * j1, "p16", 2 * j0 + b * m, 2 * j0 + b * m + m, -1024.0, A.add, ost=2, name="yo")
+        op("Y", 0, [], [("R", n, n + L)], (lambda T, q, t=t, n=n: q.dma_start(T["yr"][:, L * t:L * t + L], T["R"][:, n:n + L])), kind="store", name="yr")
+    op("Y", 0, [], [("yo", 0, L)], (lambda T, q: q.dma_start(T["yp"][:, :], T["yo"][:, :])), kind="store", name="yp")
+    return ops
+
+
+COMP = "VSPG"
+ONQ = {"R": "G", "SD": "S"}
+
+
+def meet(x, y):
+    return x[1] < y[2] and y[1] < x[2] and not (x[3] == y[3] and x[4] != y[4])
+
+
+def deps_of(ops):
+    hist, bank = {}, {}
+    for i, o in enumerate(ops):
+        raw, war = set(), set()
+        for x in o["r"]:
+            raw |= {j for (y, j, w) in hist.get(x[0], ()) if w and meet(x, y)}
+        for x in o["w"]:
+            war |= {j for (y, j, w) in hist.get(x[0], ()) if not w and meet(x, y)}
+            raw |= {j for (y, j, w) in hist.get(x[0], ()) if w and meet(x, y)}
+        for x in o["r"] + o["w"]:
+            if x[0] in PS:
+                war |= {j for e, j in bank.setdefault(x[0], {}).items() if e != o["e"]}
+        for x in o["r"]:
+            hist.setdefault(x[0], []).append((x, i, False))
+        for x in o["w"]:
+            hb = [(y, j, w) for (y, j, w) in hist.get(x[0], ()) if j == i or not (x[1] <= y[1] and y[2] <= x[2] and (x[3] == 1 or x[3:] == y[3:]))]
+            hb.append((x, i, True))
+            hist[x[0]] = hb
+        for x in o["r"] + o["w"]:
+            if x[0] in PS:
+                bank[x[0]][o["e"]] = i
+        raw.discard(i)
+        war.discard(i)
+        o["raw"], o["war"] = raw, war - raw
+
+
+def schedule(ops):
+    n = len(ops)
+    succ = [[] for _ in range(n)]
+    wake = EST["wake"]
+    for i, o in enumerate(ops):
+        al = set(o["raw"]) | set(o["war"])
+        if o["k"] == "arr":
+            al.add(i - 1)
+        o["all"] = al
+        for j in al:
+            succ[j].append(i)
+    cost = [{"send": 300.0, "load": 60.0, "store": 60.0}.get(o["k"], o["c"]) for o in ops]
+    lat = [{"load": EST["dma"], "store": EST["dma"], "send": EST["send"]}.get(o["k"], 0.0) + (4000.0 if o["n"] == "ax" else 0.0) for o in ops]
+    queue = [ONQ.get(o["e"], o["e"]) for o in ops]
+    free_war = lambda i, j: queue[j] == queue[i] and i not in ops[j]["raw"] and ops[i]["k"] == "c"
+    prio = [0.0] * n
+    for i in range(n - 1, -1, -1):
+        prio[i] = max([0.0] + [prio[j] + (0.0 if free_war(i, j) or ops[j]["k"] == "arr" else wake) for j in succ[i]]) + cost[i] + lat[i]
+    for i, o in enumerate(ops):
+        if o["w"]:
+            prio[i] += CFG["PR"].get(o["n"] + o["w"][0][0][-1], 0.0)
+    nd = [len(o["all"]) for o in ops]
+    ready = [0.0] * n
+    free = {q: 0.0 for q in "VSPGYA"}
+    avail = {q: [] for q in "VSPGYA"}
+    for i in range(n):
+        if nd[i] == 0:
+            avail[queue[i]].append(i)
+    order, busy, start, fin = [], {q: 0.0 for q in "VSPGYA"}, [0.0] * n, [0.0] * n
+    while len(order) < n:
+        best = None
+        for q in avail:
+            if avail[q]:
+                tmin = min(max(free[q], ready[i]) for i in avail[q])
+                i = max((i for i in avail[q] if max(free[q], ready[i]) <= tmin + CFG["SLACK"]), key=lambda i: prio[i])
+                st = max(free[q], ready[i])
+                if best is None or st < best[0]:
+                    best = (st, q, i)
+        st, q, i = best
+        avail[q].remove(i)
+        order.append(i)
+        start[i], fin[i] = st, st + cost[i] + lat[i]
+        if q != "A":
+            free[q] = st + cost[i]
+        busy[q] += cost[i]
+        for j in succ[i]:
+            ready[j] = max(ready[j], st if free_war(i, j) else fin[i] + (0.0 if ops[j]["k"] == "arr" else wake))
+            nd[j] -= 1
+            if nd[j] == 0:
+                avail[queue[j]].append(j)
+    return order, max(fin), busy, start, fin
+
+
+PLAN = []
+
+
+def plan():
+    if PLAN:
+        return PLAN[0]
+    ops = build()
+    deps_of(ops)
+    order, end, busy, start, fin = schedule(ops)
+    cnt = {e: 0 for e in COMP}
+    known = {q: {} for q in "VSPGY"}
+    clock, steps, nsent, nst = {}, [], 0, 0
+    for i in order:
+        o = ops[i]
+        e, k = o["e"], o["k"]
+        q = ONQ.get(e, e)
+        if k == "arr":
+            o["sem"] = (o["f"], 16)
+            clock[i] = {o["f"]: 16}
+            continue
+        cl, req = known[q], {}
+        for j in o["raw"] | o["war"]:
+            p = ops[j]
+            pq = ONQ.get(p["e"], p["e"])
+            if p["k"] in ("send", "store") or (pq == q and p["k"] == "c" and (j not in o["raw"] or q == "P")):
+                continue
+            sem, val = p["sem"]
+            if cl.get(sem, 0) < val and (sem not in req or ops[req[sem]]["sem"][1] < val):
+                req[sem] = j
+        for sem in list(req):
+            val = ops[req[sem]]["sem"][1]
+            if any(s2 != sem and clock[j2].get(sem, 0) >= val for s2, j2 in req.items()):
+                del req[sem]
+        for sem, j in req.items():
+            for a, b in clock[j].items():
+                cl[a] = max(cl.get(a, 0), b)
+        waits = sorted((sem, ops[j]["sem"][1]) for sem, j in req.items())
+        inc = None
+        if k == "c":
+            cnt[e] += 1
+            inc = ("c" + e, 1)
+            o["sem"] = ("c" + e, cnt[e])
+        elif k == "load":
+            inc = o["sem"] = ("ld_" + o["n"], 16)
+        elif k == "store":
+            nst += 1
+            inc = ("stored", 16)
+        else:
+            nsent += 1
+        if "sem" in o:
+            clock[i] = dict(cl)
+            clock[i][o["sem"][0]] = o["sem"][1]
+        steps.append((q, waits, o, inc))
+    PLAN.append((steps, cnt, nsent, nst, end, busy, ops, order, start, fin))
+    return PLAN[0]
+
+
+def rank_program(g, core, T, topo):
+    rank = T.rank_of(core)
+    if rank is None:
+        return
+    steps, cnt, nsent, nst = plan()[:4]
+    qs = {"V": g.vector, "S": g.scalar, "P": g.tensor, "G": g, "Y": g.sync}
+    for q, waits, o, inc in steps:
+        for sem, val in waits:
+            qs[q].wait_ge(T.sem[sem], int(val))
+        if o["k"] == "send":
+            t, dst, d0, d1, src, s0, s1, ar = o["f"]
+            to = T.cores[(rank + 1 + (t % 3)) % len(T.cores)]
+            rid, pid, _se = topo.addr(to)
+            g.remote_dma(T[dst][:, d0:d1], T[src][:, s0:s1], T.sem[ar], T.sem.sent, pid, rid, topo.mask(core, to))
+        elif o["k"] in ("load", "store"):
+            o["f"](T, qs[q]).then_inc(T.sem[inc[0]], 16)
+        else:
+            o["f"](T, g).then_inc(T.sem[inc[0]], 1)
+    for e in COMP:
+        g.sync.wait_ge(T.sem["c" + e], int(cnt[e]))
+    for n in LOADS:
+        g.sync.wait_ge(T.sem["ld_" + n], 16)
+    for t in range(TT):
+        for k in "pfqz":
+            g.sync.wait_ge(T.sem["ar_%s%d" % (k, t)], 16)
+    g.sync.wait_ge(T.sem.stored, 16 * nst)
+    g.wait_ge(T.sem.sent, 16 * nsent)

@@ -1,424 +1,427 @@
+import numpy as np
 from concourse.mybir import dt, AluOpType as A, ActivationFunctionType as F
 
 V, L, A0, TT = 4096, 192, 1024, 4
-H = L // 2
-XW = V + 512
-RW = A0 + TT * L
+NL, NP_ = 96, 48
+B0 = V - TT * 96
+XW = V + 16
+RW = A0 + (TT - 1) * L
 CFG = {
-    "CH": ((0, 48), (48, 96)),
-    "ZP": ("SVS", "SSV"),
-    "VP": (("VVS", "VVS"), ("VVS", "SSV")),
-    "RG": ("S", "B"),
-    "PS": (6, 4),
-    "ORD": "h0 p0 h1 p1 s z0 E0 z1 E1 v00 v01 c0 v10 m0 v11 c1 m1",
-    "SLACK": 15.0, "SPL": 1, "PR": {},
+    "PREP": "GGGGGGGVVVVVSSSS",
+    "ZG": "V.S.V",
+    "SC": ((0, 6),), "V2": ((0, 96),), "BC": ((0, 8), (8, 16)), "RS": ((0, 3),), "EL": 1,
+    "VP": ("VV.VV.SS", "VV.VV.SS"),
+    "RG": "SS.S",
+    "XREC": "V", "QC": "S", "PC": "V", "RC": "GG",
+    "BIAS": 6000.0, "SLACK": 15.0, "PR": {},
+    'BIAS': 4000, 'SLACK': 100, 'ZG': 'S.V.S', 'SC': ((0, 4), (4, 6)), 'V2': ((0, 96),), 'BC': ((0, 10), (10, 16)), 'RS': ((0, 2), (2, 3)), 'EL': 0, 'RG': 'SS.V', 'VP': ('V.V.VV.SS', 'VV.V.V.SS'), 'XREC': 'V', 'QC': 'S', 'PC': 'V', 'PREP': 'GGGGGVVVVVVSSSSS',
+    "LOADS": "Yp0 Sw0 Yz0 Sp1 Sw1 Yr0 Yx0 Ye0 Yz1 Yr1 Ye1 Yx1",
+    'BIAS': 4000, 'SLACK': 15, 'ZG': 'S.V.S', 'SC': ((0, 4), (4, 6)), 'V2': ((0, 96),), 'BC': ((0, 6), (6, 12), (12, 16)), 'RS': ((0, 2), (2, 3)), 'EL': 1, 'RG': 'SS.V', 'VP': ('V.V.VV.SS', 'V.V.V.V.S.S'), 'XREC': 'V', 'QC': 'S', 'PC': 'V', 'PREP': 'GGGGGVVVVVVSSSSS', 'RC': 'VS',
+    'PR': {'hh': -200, 'kmin': 2000, 'qs': 1000, 'send_p': 200, 'v2': -2000, 'F': -200, 'vsig': 200, 'f16': 500, 'f0scan': 200, 'e2c': 1000, 'F0': -2000, 'q': 2000, 'cb': -2000, 'vsub': -1000, 's8': -1000, 'eq': -200},
+    'BIAS': 4000, 'SLACK': 15, 'ZG': 'S.V.S', 'SC': ((0, 6),), 'V2': ((0, 96),), 'BC': ((0, 6), (6, 12), (12, 16)), 'RS': ((0, 2), (2, 3)), 'EL': 1, 'RG': 'SS.V', 'VP': ('VV.V.V.SS', 'S.V.VV.VV'), 'XREC': 'S', 'QC': 'S', 'PC': 'V', 'PREP': 'GGGGGVVVVVVSSSSS', 'RC': 'GG', 'PR': {'hh': -200, 'kmin': 2000, 'qs': 1000, 'send_p': 200, 'v2': -2000, 'F': -200, 'vsig': 200, 'f16': 500, 'f0scan': 2000, 'e2c': -2000, 'F0': -2000, 'q': 2000, 'cb': -2000, 'vsub': -1000, 's8': -1000, 'eq': -200, 'lu': -500, 'barred': -2000, 'ca': -2000, 'Zsub': 500, 'votes': -1000, 'k3': 500},
+    "TURNS": 6,
+    'BIAS': 4000, 'SLACK': 15, 'ZG': 'SS.S', 'SC': ((0, 6),), 'V2': ((0, 96),), 'BC': ((0, 4), (4, 10), (10, 16)), 'RS': ((0, 1), (1, 3)), 'EL': 0, 'RG': 'S.V.S', 'VP': ('V.V.V.V.S.S', 'VVV.VV.S'), 'XREC': 'S', 'QC': 'V', 'PC': 'S', 'PREP': 'GGGGGGVVSSSSSSSS', 'RC': 'SG', 'ONS': ('F32', 'al', 'e2L', 'e2c', 'f0l', 'f16', 'par1', 'par2'), 'PR': {},
+    "TURNS": 1,
+    'BIAS': 4000, 'SLACK': 15, 'ZG': 'SS.S', 'SC': ((0, 4), (4, 6)), 'V2': ((0, 96),), 'BC': ((0, 6), (6, 12), (12, 16)), 'RS': ((0, 1), (1, 3)), 'EL': 0, 'RG': 'S.V.S', 'VP': ('V.V.V.V.S.S', 'VVV.VV.S'), 'XREC': 'S', 'QC': 'V', 'PC': 'S', 'PREP': 'GGGGVVVVVVSSSSSS', 'RC': 'SG', 'ONS': ('F32', 'e2L', 'e2c', 'f16', 'li', 'par1', 'par2', 'q'), 'PR': {'ku': 500, 'Xrec': -500, 'e2': 500, 'Zp': -500, 'delta': -2000, 'cl': -500, 'vsub': 500, 'eq': 200, 'q': -500, 'k3': 1000, 'v2': -2000, 'k1': -2000, 'cb': -2000, 'yo': -1000, 'rscan': -500, 'rg': -1000, 'eL': -1000, 'score': -2000},
+    'BIAS': 4000, 'SLACK': 100, 'ZG': 'SSS', 'SC': ((0, 4), (4, 6)), 'V2': ((0, 96),), 'BC': ((0, 6), (6, 12), (12, 16)), 'RS': ((0, 1), (1, 3)), 'EL': 0, 'RG': 'S.SS', 'VP': ('VV.VV.SS', 'VV.V.V.SS'), 'XREC': 'V', 'QC': 'V', 'PC': 'V', 'PREP': 'GGGGVVVVVVVVVVVV', 'RC': 'SG', 'ONS': ('F32', 'e2c', 'par2'), 'PR': {'e2c': 500, 'f16': -200, 'yi': 200, 'u': -1000, 'dup_r': 1000, 'y': -500, 'vsub': 200, 'cT': -1000, 'eu': -2000, 'f0l': 1000, 'q': 2000, 'v1': 200, 'rg': -2000, 'e16': -1000},
 }
+EST = {"pe": 1.05, "fixed": {"V": 35.0, "S": 120.0, "P": 7.0, "G": 35.0}, "fac": 1.03, "gather": 1.5, "wake": 80.0, "dma": 1800.0, "send": 2300.0, "issue": 250.0, "rate": 350.0, "dissue": 60.0}
 DT = {"i": "int32", "u": "uint16", "f": "float32", "b": "bfloat16", "h": "float16"}
-ARENA = {"i": 4096, "u": 1024, "f": 2560, "b": 24576, "h": 5120}
-SCRATCH = {
-    "X": ("sbuf", [128, XW], "bfloat16"), "Xh": ("sbuf", [128, V], "bfloat16"), "Z": ("sbuf", [128, RW], "bfloat16"),
-    "R": ("sbuf", [128, RW], "float32"), "ri": ("sbuf", [128, A0], "int32"), "exi": ("sbuf", [128, L], "int32"),
-    "wi": ("sbuf", [128, 1], "int32"), "ki": ("sbuf", [128, 1], "int32"),
-    "pn": ("sbuf", [128, TT * L], "bfloat16"), "fnat": ("sbuf", [128, TT * L], "float32"), "yo": ("sbuf", [128, L], "float32"),
-    "f0s": ("sbuf", [128, TT * 16], "uint16"), "f0l": ("sbuf", [128, TT * 16], "uint16"),
-    "qs": ("sbuf", [128, TT * H], "bfloat16"), "ql": ("sbuf", [128, TT * H], "bfloat16"),
-}
+ARENA = {"i": 4096, "u": 1024, "f": 6144, "b": 28672, "h": 4096}
+SCRATCH = {"Cm": ("sbuf", [128, 2, 16, 32], "bfloat16")}
+for _s in "01":
+    SCRATCH["X" + _s] = ("sbuf", [128, XW], "bfloat16")
+    SCRATCH["Z" + _s] = ("sbuf", [128, RW], "bfloat16")
+    SCRATCH["R" + _s] = ("sbuf", [128, RW], "float32")
+    SCRATCH["dz" + _s] = ("sbuf", [128, 6, 16, 16], "bfloat16")
 for _k in ARENA:
     SCRATCH["ar_" + _k] = ("sbuf", [128, ARENA[_k]], DT[_k])
-PS = ("d0", "d1", "d2", "d3", "v1", "v2", "sc", "cm")
+PS = tuple(x + s for s in "01" for x in ("d0", "d1", "ma", "mb"))
 for _n in PS:
-    SCRATCH[_n] = ("psum", [128, 512], "float32")
-LOADS = ("p0", "wt", "km", "zp", "rt", "ax", "ex")
-SEMAPHORES = ["cV", "cS", "cP", "cG", "sent", "stored"] + ["ld_" + n for n in LOADS] + ["ar_%s%d" % (k, t) for t in range(TT) for k in "pfqz"]
-RATE = {"V": 1.0, "S": 1.0, "P": 0.5, "G": 1.0}
-EST = {"gather": 1.56, "wake": 90.0, "dma": 2200.0, "send": 2300.0}
-WHERE = {}
-TOP = {}
+    SCRATCH[_n] = ("psum", [128, 32, 16] if _n[:2] != "ma" else [128, 512], "float32")
+DSEM = ["ld_" + k + s for k in "pwzrxe" for s in "01"] + ["dup_%s%s%d" % (k, s, t) for k in "zr" for s in "01" for t in range(TT - 1)]
+ASEM = ["ar_%s%s%d" % (k, s, t) for k in "pfq" for s in "01" for t in range(TT)]
+SEMAPHORES = ["cV", "cS", "cP", "cG", "sent", "stored"] + DSEM + ASEM
+WHERE, TOP, MASKS = {}, {}, {}
+PART = {1: slice(0, 64), 2: slice(64, 128), 3: slice(0, 128)}
 
 
 def need(kind, **names):
-    q = {"i": 8, "f": 8, "b": 16, "u": 16, "h": 16}[kind]
+    q = 8 if kind in "if" else 16
     for n, w in names.items():
-        WHERE[n] = (kind, TOP.get(kind, 0))
+        WHERE[n] = (kind, TOP.get(kind, 0), w)
         TOP[kind] = TOP.get(kind, 0) + -(-w // q) * q
+        assert TOP[kind] <= ARENA[kind], kind
 
 
-def ap(T, n, lo, hi, st=1):
+def a(n, lo, hi, st=1, h=3):
+    if n in PS and n[:2] != "ma":
+        if st == 1 and lo % 16 == 0 and hi % 16 == 0:
+            return (n, (slice(lo // 16, hi // 16), slice(0, 16)), h)
+        raise ValueError((n, lo, hi, st))
+    return (n, (slice(lo, hi, st),), h)
+
+
+def nd(n, *idx):
+    return (n, idx, 3)
+
+
+def ap(T, x):
+    n, idx, h = x
     if n in WHERE:
-        k, o = WHERE[n]
-        n, lo, hi = "ar_" + k, lo + o, hi + o
-    return T[n][:, lo:hi:st] if st > 1 else T[n][:, lo:hi]
+        k, o, w = WHERE[n]
+        s = idx[0]
+        assert s.stop <= w, x
+        n, idx = "ar_" + k, (slice(s.start + o, s.stop + o, s.step),)
+    idx = tuple(slice(s.start, s.stop) if isinstance(s, slice) and s.step in (1, None) else s for s in idx)
+    return T[n][(PART[h],) + idx]
 
 
-def is32(n):
-    return WHERE[n][0] == "f" if n in WHERE else SCRATCH[n][2] == "float32"
+def dtype(n):
+    return DT[WHERE[n][0]] if n in WHERE else SCRATCH[n][2]
 
 
-def rg_(b, lo, hi, st=1):
-    return (b, lo, hi, st, lo % st)
+def cells(x):
+    key = (x[0], str(x[1]))
+    if key not in MASKS:
+        shape = [WHERE[x[0]][2]] if x[0] in WHERE else SCRATCH[x[0]][1][1:]
+        m = np.zeros(shape, bool)
+        m[x[1]] = True
+        MASKS[key] = (int(m.sum()), int.from_bytes(np.packbits(m.reshape(-1)).tobytes(), "big"))
+    return MASKS[key]
 
 
 def build():
     WHERE.clear()
     TOP.clear()
-    CH = CFG["CH"]
-    GC = EST["gather"]
-    NC = range(len(CH))
     ops = []
+    cur = [""]
 
-    def op(eng, cyc, w, r, fn, kind="c", name="", fix=0.0):
-        w, r = [x if len(x) == 5 else rg_(*x) for x in w], [x if len(x) == 5 else rg_(*x) for x in r]
-        ops.append({"e": eng, "c": cyc * 0.83 * RATE.get(eng, 1.0) + fix, "w": w, "r": r, "f": fn, "k": kind, "n": name})
+    def op(eng, cyc, w, r, fn, name="", kind="c", fix=0.0, gather=False, ni=1, by=0):
+        ops.append({"e": eng, "cy": cyc, "fx": fix, "g": gather, "ni": ni, "by": by, "w": w, "r": r, "f": fn, "k": kind, "n": name + cur[0], "s": cur[0]})
 
-    def v(n, w, r, fn, name="", half=False, fix=0.0):
-        op("V", max(64, n * (0.5 if half else 1)), w, r, fn, name=name, fix=fix)
+    def vcyc(xs):
+        two = all(dtype(x[0]) in ("bfloat16", "float16", "uint16") for x in xs)
+        return max(64, cells(xs[0])[0] * (0.5 if two else 1))
 
-    def s(n, w, r, fn, name="", fix=0.0):
-        op("S", max(64, n), w, r, fn, name=name, fix=fix)
+    def vm(o, val):
+        op("V", vcyc([o]), [o], [], lambda T, g: g.vector.memset(ap(T, o), val), "memset")
 
-    def vm(buf, lo, hi, val, st=1):
-        v(hi - lo, [(buf, lo, hi)], [], lambda T, g: g.vector.memset(ap(T, buf, lo, hi, st), val), "memset", half=True)
+    def gsel(o, i, pat, cmp_, base, cm, name="sel"):
+        op("G", 2 * cells(o)[0], [o], [i], lambda T, g: g.affine_select(ap(T, o), ap(T, i), pat, cmp_, 0.0, base, cm), name, fix=170)
 
-    def gsel(out, inp, n, pat, cmp_, base, cm, at=0):
-        op("G", 2 * n, [(out, at, at + n)], [(inp, 0, n)], lambda T, g: g.affine_select(ap(T, out, at, at + n), ap(T, inp, 0, n), pat, cmp_, 0.0, base, cm), fix=170, name="sel")
+    def giota(o, pat, base, cm):
+        kw = {} if dtype(o[0]) == "int32" else {"allow_small_or_imprecise_dtypes": True}
+        op("G", 2 * cells(o)[0], [o], [], lambda T, g: g.iota(ap(T, o), pat, base, cm, **kw), "iota", fix=130)
 
-    def giota(out, n, pat, base, cm, fl=True):
-        op("G", 2 * n, [(out, 0, n)], [], (lambda T, g: g.iota(ap(T, out, 0, n), pat, base, cm, allow_small_or_imprecise_dtypes=True)) if fl else (lambda T, g: g.iota(ap(T, out, 0, n), pat, base, cm)), fix=130, name="iota")
+    def vs(o, i, s1, op0, s2=None, op1=None, name=""):
+        col = [x for x in (s1, s2) if isinstance(x, tuple)]
 
-    def vs(out, ol, oh, inp, il, ih, s1, op0, s2=None, op1=None, half=False, ost=1, ist=1, name="", scol=None):
         def fn(T, g):
-            sc = ap(T, scol[0], scol[1], scol[1] + 1) if scol else s1
-            o, i = ap(T, out, ol, oh, ost), ap(T, inp, il, ih, ist)
+            x1, x2 = [ap(T, x) if isinstance(x, tuple) else x for x in (s1, s2)]
             if op1 is None:
-                return g.vector.tensor_scalar(o, i, sc, None, op0)
-            return g.vector.tensor_scalar(o, i, sc, s2, op0, op1)
-        v(-(-(ih - il) // ist), [(out, ol, oh, ost)], [(inp, il, ih, ist)] + ([(scol[0], scol[1], scol[1] + 1)] if scol else []), fn, name, half)
+                return g.vector.tensor_scalar(ap(T, o), ap(T, i), x1, None, op0)
+            return g.vector.tensor_scalar(ap(T, o), ap(T, i), x1, x2, op0, op1)
+        op("V", vcyc([i, o]), [o], [i] + col, fn, name)
 
-    def vc(out, ol, oh, inp, il, ih, half=False, ost=1, ist=1, name=""):
-        v(-(-(ih - il) // ist), [(out, ol, oh, ost)], [(inp, il, ih, ist)], lambda T, g: g.vector.tensor_copy(ap(T, out, ol, oh, ost), ap(T, inp, il, ih, ist)), name, half)
+    def vc(o, i, name=""):
+        op("V", vcyc([i, o]), [o], [i], lambda T, g: g.vector.tensor_copy(ap(T, o), ap(T, i)), name)
 
-    def vt(out, ol, oh, a, al, ah, b, bl, bh, o_, name=""):
-        n = ah - al
-        v(n if (a in PS or b in PS) else 2 * n, [(out, ol, oh)], [(a, al, ah), (b, bl, bh)],
-          lambda T, g: g.vector.tensor_tensor(ap(T, out, ol, oh), ap(T, a, al, ah), ap(T, b, bl, bh), o_), name)
+    def vt(o, x, y, o_, name=""):
+        n = cells(o)[0]
+        op("V", max(64, n if (x[0] in PS or y[0] in PS) else 2 * n), [o], [x, y], lambda T, g: g.vector.tensor_tensor(ap(T, o), ap(T, x), ap(T, y), o_), name)
 
-    def act(out, ol, oh, inp, il, ih, fn_, ost=1, ist=1, bias=0.0, scale=1.0, bcol=None, acc=None, name=""):
+    def scan(o, x, y, init, op0, op1, name):
+        op("V", vcyc([o, x, y]), [o], [x, y], lambda T, g: g.vector.tensor_tensor_scan(ap(T, o), ap(T, x), ap(T, y), init, op0, op1), name)
+
+    def act(o, i, fn_, bias=0.0, scale=1.0, acc=None, off=None, name=""):
+        col = [x for x in (bias, scale) if isinstance(x, tuple)]
+
         def fn(T, g):
-            kw = {"scale": scale, "bias": ap(T, bcol, 0, 1) if bcol else bias}
+            kw = {"scale": ap(T, scale) if isinstance(scale, tuple) else scale, "bias": ap(T, bias) if isinstance(bias, tuple) else bias}
             if acc:
-                kw["accum_out"] = ap(T, acc[0], acc[1], acc[1] + 1)
-            return g.scalar.activation(ap(T, out, ol, oh, ost), ap(T, inp, il, ih, ist), fn_, **kw)
-        s(-(-(ih - il) // ist), [(out, ol, oh, ost)] + ([(acc[0], acc[1], acc[1] + 1)] if acc else []), [(inp, il, ih, ist)] + ([(bcol, 0, 1)] if bcol else []), fn, name)
+                kw["accum_out"] = ap(T, acc)
+            return g.scalar.activation(ap(T, o), ap(T, i).indirect(ap(T, off)) if off else ap(T, i), fn_, **kw)
+        n = cells(o)[0]
+        op("S", n if off else max(64, n), [o] + ([acc] if acc else []), [i] + col + ([off] if off else []), fn, name, fix=65 if off else 20 if acc else 0, gather=bool(off))
 
-    def gather_v(out, ol, oh, win, wh, off, fl, fh, name, in1=None, o_=None):
+    def gv(o, win, off, name, y=None, o_=None):
         def fn(T, g):
-            ind = T[win][:, 0:wh].indirect(ap(T, off, fl, fh))
-            if in1 is None:
-                return g.vector.tensor_copy(ap(T, out, ol, oh), ind)
-            return g.vector.tensor_tensor(ap(T, out, ol, oh), ind, ap(T, *in1), o_)
-        v((oh - ol) * GC, [(out, ol, oh)], [(win, 0, wh), (off, fl, fh)] + ([in1] if in1 else []), fn, name, fix=50)
+            ind = ap(T, win).indirect(ap(T, off))
+            if y is None:
+                return g.vector.tensor_copy(ap(T, o), ind)
+            return g.vector.tensor_tensor(ap(T, o), ind, ap(T, y), o_)
+        op("V", cells(o)[0], [o], [win, off] + ([y] if y else []), fn, name, fix=50, gather=True)
 
-    def gather_s(out, ol, oh, win, wh, off, fl, fh, name):
-        s((oh - ol) * GC, [(out, ol, oh)], [(win, 0, wh), (off, fl, fh)],
-          lambda T, g: g.scalar.activation(ap(T, out, ol, oh), T[win][:, 0:wh].indirect(ap(T, off, fl, fh)), F.Copy), name, fix=65)
+    def gneg(eng, o, win, off, name):
+        if eng == "S":
+            act(o, win, F.Identity, scale=-1.0, off=off, name=name)
+        else:
+            op("V", cells(o)[0], [o], [win, off], lambda T, g: g.vector.tensor_scalar(ap(T, o), ap(T, win).indirect(ap(T, off)), -1.0, None, A.mult), name, fix=50, gather=True)
 
-    def groups(grs, name):
-        cost, w, r = 0, [], []
-        for prs, out, ol, oh, ost in grs:
-            w.append((out, ol, oh, ost))
-            for x in prs:
-                n = -(-(x[5] - x[4]) // x[6])
-                cost += max(min(64, x[2] - x[1]), n) * (4 if is32(x[3]) else 1)
-                r += [(x[0], x[1], x[2], 1), x[3:7]]
+    def copy(eng, o, i, name, add=0.0):
+        if eng == "G":
+            gsel(o, i, [[0, cells(o)[0]]], A.is_ge, 0, 0, name)
+        elif eng == "S":
+            act(o, i, F.Identity, bias=add, name=name)
+        elif add:
+            vs(o, i, add, A.add, name=name)
+        else:
+            vc(o, i, name)
+
+    def aff(o, i, mul, add, name):
+        if name in CFG["ONS"]:
+            act(o, i, F.Identity, bias=add, scale=mul, name=name)
+        elif mul == 1 and add == 0:
+            vc(o, i, name)
+        else:
+            vs(o, i, mul, A.mult, add, A.add, name=name)
+
+    def mm(prs, name, start=True, stop=True):
+        grs = prs if isinstance(prs[0], list) else [prs]
+        cost = sum(max(64, cells(x[2])[0]) * (4 if dtype(x[2][0]) == "float32" else 1) for gr in grs for x in gr)
 
         def fn(T, g):
             ins = None
-            for prs, out, ol, oh, ost in grs:
-                for y, x in enumerate(prs):
-                    ins = g.tensor.matmul(ap(T, out, ol, oh, ost), ap(T, x[0], x[1], x[2]), ap(T, x[3], x[4], x[5], x[6]), y == 0, y == len(prs) - 1)
+            for gr in grs:
+                for y, x in enumerate(gr):
+                    ins = g.tensor.matmul(ap(T, x[0]), ap(T, x[1]), ap(T, x[2]), start and y == 0, stop and y == len(gr) - 1)
             return ins
-        op("P", cost, w, sorted(set(r)), fn, name=name)
+        uniq = lambda xs: list({str(x): x for x in xs}.values())
+        op("P", cost * 0.5, uniq([x[0] for gr in grs for x in gr]), uniq([y for gr in grs for x in gr for y in x[1:]]), fn, name, ni=sum(map(len, grs)))
 
-    bank = [0]
+    def dma(q, prs, sem, name, by):
+        side = lambda T, x: ap(T, x) if isinstance(x, tuple) else x(T)
+        w, r = [x[0] for x in prs if isinstance(x[0], tuple)], [x[1] for x in prs if isinstance(x[1], tuple)]
+        op(q, 0, w, r, lambda T, q_: [q_.dma_start(side(T, o), side(T, i)) for o, i in prs], name, kind="dma", ni=len(prs), by=by)
+        ops[-1]["ds"] = sem
 
-    def dbank():
-        bank[0] = (bank[0] + 1) % 4
-        return "d%d" % bank[0]
+    def send(t, kind, dst, src):
+        sem = "ar_%s%s%d" % (kind, cur[0], t)
+        by = 128 * cells(src)[0] * (4 if dtype(src[0]) == "float32" else 2)
+        op("R", 0, [], [src], (t, [(dst, src)], sem), "send_" + kind, kind="send", by=by)
+        op("A", 0, [dst], [], sem, "arr_" + kind, kind="arr")
 
-    need("b", ones=144, tmpa=144, tmpb=144, BB=128, W8=144, W4=144, I1=128, IN=128, I8=128, IB=128, IC=128, BG=128, smax=1536, p=L, prep=L * 16)
-    need("f", ones32=128, cf=8, id32=128, up32=128, dn32=128, iot=16, iom=L, ion=H, M16=16, smin=L, pc=L, bar=1, cb=8)
-    need("h", WH=128, WL=128, J1=128, JN=128, BS=2048, Q=512, N16=TT * H, E16=L, p16=L, mk=H)
+    need("b", ones=256, w16=144, tmpa=144, BB=128, W=144, I=128, I2080=128, I4096=128, IK=128, BS=2048, Sel=256, smax=768, maskc=NL, half=NP_, IM=128, cs=1)
+    need("f", id32=128, iom=NL, M16=16, smin=NL, N32=TT * NL, pcol=1, bar=TT, cb=2 * TT, tab=8)
+    need("h", N16=TT * NL)
     need("i", ci=8, cj=8)
-    for c in NC:
-        np_ = CH[c][1] - CH[c][0]
-        nl, C = 2 * np_, str(c)
-        need("i", **{x + C: w for x, w in (("si", np_), ("ul", nl), ("uu", np_), ("uv", np_), ("ku", np_), ("li", 12), ("t1", nl), ("t3", nl), ("fe", nl), ("f", nl), ("ff", nl))})
-        need("u", **{x + C: w for x, w in (("cl", np_), ("al", 12), ("el", nl), ("e2l", nl), ("lu", np_))})
-        need("f", **{x + C: w for x, w in (("kt", nl), ("ks", nl), ("ef", nl), ("k1", nl), ("rl", np_))})
-        need("h", **{x + C: w for x, w in (("c16", nl), ("lh", 12), ("f16", nl), ("F16", nl), ("FT", nl))})
-        need("b", **{x + C: w for x, w in (("gz", 16 * np_), ("dz", 16 * nl), ("g1", 16 * nl), ("g2", 16 * nl), ("x1", 16 * nl), ("bb", nl), ("eq", 16 * np_), ("rs", 16 * np_))})
+    for s in "01":
+        need("i", **{x + s: w for x, w in (("ri", A0), ("exi", NL), ("wk", 2), ("q", NP_), ("hh", NP_), ("li", 6), ("yi", NL), ("e2", NL), ("f", NL))})
+        need("u", **{x + s: w for x, w in (("cl", NP_), ("al", 6), ("el", NL), ("e2l", NL), ("lu", NP_), ("f0l", 6))})
+        need("f", **{x + s: w for x, w in (("cf", 8), ("ul", NL), ("uu", NP_), ("ks", NL), ("eu", NL), ("k2", NL), ("Fs", TT * L), ("Fl", TT * L), ("yo", NL))})
+        need("h", **{x + s: w for x, w in (("Wm", 128), ("E16", NL), ("c16", 64), ("cT", 64), ("e16", NL), ("e2c", NL), ("F16", NL), ("f16", NL), ("pd", NL), ("p16", NL))})
+        need("b", **{x + s: w for x, w in (("p", TT * NL), ("pl", TT * NL), ("qs", TT * NL), ("ql", TT * NL), ("prep", 16 * NL), ("gz", 768), ("g1", 16 * NL),
+                                          ("g2", 16 * NL), ("x1", 16 * NL), ("sg", NL), ("s8", NL), ("nn", NL), ("eq", 768), ("rs", 768))})
+    I, W = a("I", 0, 128), lambda k: a("W", 16 - k, 144 - k)
 
-    for q, nm, buf, wid in (("Y", "p0", "pn", L), ("Y", "wt", "wi", 1), ("Y", "km", "ki", 1), ("SD", "zp", "Z", A0), ("Y", "ax", "X", V), ("SD", "rt", "ri", A0), ("Y", "ex", "exi", L)):
-        op(q, 0, [(buf, 0, wid)], [], (lambda T, q_, nm=nm, buf=buf, wid=wid: q_.dma_start(T[buf][:, 0:wid], T[nm][:, :])), kind="load", name=nm)
-    vm("ones", 0, 144, 1.0)
-    vm("ones32", 0, 128, 1.0)
-    gsel("tmpa", "ones", 128, [[-16, 8], [0, 16]], A.is_ge, 0, 1)
-    gsel("BB", "tmpa", 128, [[16, 8], [0, 16]], A.is_ge, 15, -1)
-    vs("ci", 0, 1, "wi", 0, 1, 63, A.bitwise_and)
-    vc("cf", 0, 1, "ci", 0, 1)
-    vt("cf", 1, 2, "wi", 0, 1, "ci", 0, 1, A.subtract)
-    vc("cf", 2, 3, "ki", 0, 1)
-    vs("WH", 0, 128, "BB", 0, 128, None, A.mult, scol=("cf", 1), half=True)
-    vs("WL", 0, 128, "BB", 0, 128, None, A.mult, scol=("cf", 0), half=True)
-    vs("mk", 0, H, "ones", 0, H, -1024.0, A.mult, half=True)
-    gsel("id32", "ones32", 128, [[-1, 128]], A.is_equal, 0, 1)
-    vc("I1", 0, 128, "id32", 0, 128)
-    vs("IN", 0, 128, "id32", 0, 128, -1.0, A.mult)
-    for c, (j0, j1) in enumerate(CH):
-        m = j1 - j0
-        for b in (0, 1):
-            vs("p16", 2 * j0 + b * m, 2 * j0 + b * m + m, "pn", 2 * j0 + b, 2 * j1, 1024.0, A.add, half=True, ist=2)
-        vs("p", 2 * j0, 2 * j1, "p16", 2 * j0, 2 * j1, -1024.0, A.add, half=True, name="p")
-    act("cb", 0, 4, "ones32", 0, 4, F.Sigmoid, name="table")
-
-    def setup():
-        gsel("tmpb", "ones", 144, [[-16, 9], [-1000, 16]], A.is_ge, 16, 1)
-        gsel("tmpa", "tmpb", 144, [[16, 9], [0, 16]], A.is_ge, -1, -1)
-        vs("W4", 0, 144, "tmpa", 0, 144, 4096.0, A.mult, half=True)
-        vs("J1", 0, 128, "id32", 0, 128, 1.0, A.mult)
-        giota("iom", L, [[0, L // 16], [1, 16]], 0, 0)
-        vs("smin", 0, L, "iom", 0, L, 0.0, A.is_equal, 33554432.0, A.mult)
-        giota("cj", 1, [[1, 1]], 0, 1, fl=False)
-        vs("ci", 1, 2, "cj", 0, 1, 4, A.logical_shift_right, 1, A.bitwise_and)
-        vc("cf", 4, 5, "ci", 1, 2)
-        vs("cf", 5, 6, "ci", 1, 2, -1.0, A.mult, 1.0, A.add)
-        gsel("up32", "ones32", 128, [[-1, 128]], A.is_equal, 16, 1)
-        gsel("dn32", "ones32", 128, [[-1, 128]], A.is_equal, -16, 1)
-        vs("Q", 0, 128, "id32", 0, 128, None, A.mult, scol=("cf", 5))
-        vs("Q", 384, 512, "id32", 0, 128, None, A.mult, scol=("cf", 4))
-        vs("Q", 128, 256, "up32", 0, 128, None, A.mult, scol=("cf", 5))
-        vs("Q", 256, 384, "dn32", 0, 128, None, A.mult, scol=("cf", 4))
-        vc("R", 0, A0, "ri", 0, A0, name="R")
-        vm("X", V, XW, 0.0)
-        vm("bar", 0, 1, -1280.0)
-        vs("W8", 0, 144, "tmpa", 0, 144, 8192.0, A.mult, half=True)
-        vs("BG", 0, 128, "BB", 0, 128, -4352.0, A.mult, half=True)
-        vs("IB", 0, 128, "I1", 0, 128, 1048576.0, A.mult, half=True)
-        vs("IC", 0, 128, "I1", 0, 128, -129024.0, A.mult, half=True)
-        for c, (j0, j1) in enumerate(CH):
-            m = j1 - j0
-            for b in (0, 1):
-                vs("E16", 2 * j0 + b * m, 2 * j0 + b * m + m, "exi", 2 * j0 + b, 2 * j1, -2048.0, A.add, ist=2)
-        vs("I8", 0, 128, "I1", 0, 128, 8192.0, A.mult, half=True)
-        vs("JN", 0, 128, "id32", 0, 128, -1.0, A.mult)
-        vs("ci", 2, 3, "cj", 0, 1, 15, A.bitwise_and)
-        vc("cf", 3, 4, "ci", 2, 3)
-        giota("iot", 16, [[1, 16]], 0, 0)
-        vs("M16", 0, 16, "iot", 0, 16, None, A.is_equal, scol=("cf", 3))
-        for k in range(16):
-            vs("BS", 128 * k, 128 * k + 128, "BB", 0, 128, None, A.mult, scol=("M16", k), half=True)
-        giota("ion", H, [[1, H]], -384, 0)
-        for t in range(TT):
-            vs("N16", H * t, H * t + H, "ion", 0, H, float(H * t), A.add)
-        vm("smax", 0, 1536, 1.0)
-        vm("smax", 0, 1536, 0.0, st=16)
-        for k in range(4):
-            vs("Xh", 1024 * k, 1024 * k + 1024, "X", 1024 * k, 1024 * k + 1024, -0.5, A.mult, half=True, name="Xh")
-
-    def hash_(t, c):
-        n, (j0, j1), C = A0 + L * t, CH[c], str(c)
-        a, m, o = 2 * j0, j1 - j0, 416 + j0
-        groups([([(x, 0, 128, "mk", 0, m, 1) for x in ("WH", "WL")] + [(x, 0, 128, "p16", a, a + m, 1) for x in ("WH", "WL")], "sc", o, o + m, 1)], "u")
-        vc("si" + C, 0, m, "sc", o, o + m, name="si")
-        vs("ul" + C, 0, m, "si" + C, 0, m, 4095, A.bitwise_and, name="u")
-        vt("uu" + C, 0, m, "ul" + C, 0, m, "ul" + C, 0, m, A.mult, "uu")
-        vs("ku" + C, 0, m, "ul" + C, 0, m, None, A.mult, scol=("cf", 2), name="ku")
-        vs("uv" + C, 0, m, "uu" + C, 0, m, 5, A.arith_shift_right, 4095, A.bitwise_and, name="uv")
-        vt("uu" + C, 0, m, "ku" + C, 0, m, "uv" + C, 0, m, A.add, "hh")
-        vs("si" + C, 0, m, "uu" + C, 0, m, 4095, A.bitwise_and, name="hm")
-        vs("cl" + C, 0, m, "si" + C, 0, m, n / 4096.0, A.mult, -0.5 + 2.0 ** -13, A.add, name="cl")
-        for b in (0, 1):
-            vc("c16" + C, b * m, b * m + m, "cl" + C, 0, m, half=True, name="c16")
-        vc("ul" + C, m, 2 * m, "ul" + C, 0, m, name="uB")
-
-    def prep(c):
-        j0, j1 = CH[c]
-        for k in range(16):
-            if k < CFG["PS"][c]:
-                act("prep", 32 * j0 + k, 32 * j1, "p", 2 * j0, 2 * j1, F.Copy, ost=16, name="prep")
-            else:
-                vc("prep", 32 * j0 + k, 32 * j1, "p", 2 * j0, 2 * j1, half=True, ost=16, name="prep")
-
-    def zstage(t, c):
-        n, (j0, j1), C = A0 + L * t, CH[c], str(c)
-        b, m, path = 2 * j0, j1 - j0, CFG["ZP"][c]
-        for x, pa in enumerate(path):
-            j = 16 * x
-            if pa == "S":
-                gather_s("gz" + C, 16 * j, 16 * j + 256, "Z", n, "cl" + C, j, j + 16, "Zg")
-                d = dbank()
-                groups([([("I1", 0, 128, "gz" + C, 16 * j, 16 * j + 256, 1), ("IN", 0, 128, "prep", 16 * (b + h * m + j), 16 * (b + h * m + j) + 256, 1)], d, 256 * h, 256 * h + 256, 1) for h in (0, 1)], "Zsub")
-            for h in (0, 1):
-                l = 16 * (h * m + j)
-                if pa == "S":
-                    act("dz" + C, l, l + 256, d, 256 * h, 256 * h + 256, F.Abs, name="Zabs")
-                else:
-                    gather_v("g1" + C, l, l + 256, "Z", n, "cl" + C, j, j + 16, "Zfused", in1=("prep", 16 * b + l, 16 * b + l + 256), o_=A.subtract)
-                    act("dz" + C, l, l + 256, "g1" + C, l, l + 256, F.Abs, name="Zabs")
-
-    def relay(src, so, st, out, o0, q):
-        return [([("Q", 256 * hi + 128 * gl, 256 * hi + 128 * gl + 128, src, so + st * gl, st * q, 2 * st) for gl in (0, 1)], out, o0 + hi, o0 + q, 2) for hi in (0, 1)]
-
-    def elect(t, c):
-        n, (j0, j1), C = A0 + L * t, CH[c], str(c)
-        m, o = j1 - j0, 2 * j0
-        nl = 2 * m
-        q = nl // 16
-        r0 = 208 + 16 * c
-        groups([([("W4", 16 - k, 144 - k, "dz" + C, k, nl * 16, 16) for k in range(16)] + [("J1", 0, 128, "c16" + C, 0, nl, 1)], "sc", o, o + nl, 1)], "score")
-        v(nl, [("kt" + C, 0, nl)], [("sc", o, o + nl)], lambda T, g: g.vector.transpose(ap(T, "kt" + C, 0, nl), ap(T, "sc", o, o + nl)), "kT")
-        v(nl, [("ks" + C, 0, nl)], [("kt" + C, 0, nl), ("smin", 0, nl)],
-          lambda T, g: g.vector.tensor_tensor_scan(ap(T, "ks" + C, 0, nl), ap(T, "smin", 0, nl), ap(T, "kt" + C, 0, nl), 33554432.0, A.max, A.min), "kmin")
-        vc("li" + C, 0, q, "ks" + C, 15, nl, ist=16, name="li")
-        vs("li" + C, 0, q, "li" + C, 0, q, 4095, A.bitwise_and, name="lm")
-        vc("lh" + C, 0, q, "li" + C, 0, q, name="lh")
-        groups(relay("lh" + C, 0, 1, "sc", r0, q), "relay")
-        vc("al" + C, 0, q, "sc", r0, r0 + q, name="al")
-        gather_v("el" + C, 0, nl, "R", n, "al" + C, 0, q, "eL")
-        gather_v("t1" + C, 0, nl, "R", n, "al" + C, 0, q, "eu", in1=("ul" + C, 0, nl), o_=A.mult)
-        gather_s("ef" + C, 0, nl, "R", n, "al" + C, 0, q, "ef")
-        e7 = "ef" + C
-        if t:
-            e7 = "kt" + C
-            act(e7, 0, nl, "ef" + C, 0, nl, F.Identity, bias=float(77 * t), name="e77")
-        vs("t1" + C, 0, nl, "t1" + C, 0, nl, 5, A.arith_shift_right, name="t2")
-        vt("t3" + C, 0, nl, "t1" + C, 0, nl, e7, 0, nl, A.add, "t3")
-        vs("t3" + C, 0, nl, "t3" + C, 0, nl, 4095, A.bitwise_and, name="e2")
-        vc("e2l" + C, 0, nl, "t3" + C, 0, nl, name="e2L")
-
-    def vstage(t, c, w):
-        (j0, j1), C = CH[c], str(c)
-        b, lst, gb = 2 * j0, ("el", "e2l")[w] + C, ("g1", "g2")[w] + C
-        path = CFG["VP"][c][w]
-        x = 0
-        while x < len(path):
-            if path[x] == "V":
-                y = x
-                while y < len(path) and path[y] == "V" and (y == x or not CFG["SPL"]):
-                    y += 1
-                gather_v(gb, 512 * x, 512 * y, "X", XW, lst, 32 * x, 32 * y, "votes", in1=("prep", 16 * b + 512 * x, 16 * b + 512 * y), o_=A.is_ge)
-                x = y
-            else:
-                gather_s("x1" + C, 512 * x, 512 * x + 512, "X", XW, lst, 32 * x, 32 * x + 32, "votesS")
-                d = dbank()
-                groups([([("I1", 0, 128, "x1" + C, 512 * x, 512 * x + 512, 1), ("IN", 0, 128, "prep", 16 * b + 512 * x, 16 * b + 512 * x + 512, 1)], d, 0, 512, 1)], "vsub")
-                act(gb, 512 * x, 512 * x + 512, d, 0, 512, F.Sigmoid, bias=128.0, scale=256.0, name="vsig")
-                x += 1
-
-    def choice(t, c):
-        (j0, j1), C = CH[c], str(c)
-        b = 2 * j0
-        nl = 2 * (j1 - j0)
-        o, o2 = b, 192 + b
-        groups([([("BG", 0, 128, "ones", 0, nl, 1)] + [("W8", 16 - k, 144 - k, "g1" + C, k, nl * 16, 16) for k in range(16)], "v1", o, o + nl, 1)], "v1sum")
-        act("bb" + C, 0, nl, "v1", o, o + nl, F.Sigmoid, scale=-1.0 / 32, bcol="bar", acc=("cb", c), name="barred")
-        vt("k1" + C, 0, nl, "v1", o, o + nl, "ef" + C, 0, nl, A.add, "k1")
-        groups([([("J1", 0, 128, "E16", b, b + nl, 1), ("IC", 0, 128, "ones", 0, nl, 1), ("IB", 0, 128, "bb" + C, 0, nl, 1)], "v1", o2, o2 + nl, 1)], "k3")
-        groups([([("W8", 16 - k, 144 - k, "g2" + C, k, nl * 16, 16) for k in range(16)], "v2", o, o + nl, 1)], "v2sum")
-        act("v2", o2, o2 + nl, "v2", o, o + nl, F.Relu, bias=65536.0, scale=-1.0, name="r")
-        vt("v2", o2, o2 + nl, "t3" + C, 0, nl, "v2", o2, o2 + nl, A.subtract, "k2")
-        vt("k1" + C, 0, nl, "v2", o2, o2 + nl, "k1" + C, 0, nl, A.max, "max")
-        vt("fe" + C, 0, nl, "v1", o2, o2 + nl, "k1" + C, 0, nl, A.max, "max")
-        vs("f" + C, 0, nl, "fe" + C, 0, nl, 4095, A.bitwise_and, name="f")
-        vs("f16" + C, 0, nl, "f" + C, 0, nl, -2048.0, A.add, name="f16")
-
-    def parity():
-        groups([([("ones32", 0, 128, "cb", c, c + 1, 1) for c in NC], "cm", 500, 501, 1)], "par")
-        vc("ci", 4, 5, "cm", 500, 501)
-        vs("ci", 5, 6, "ci", 4, 5, 1, A.bitwise_and)
-        vs("bar", 0, 1, "ci", 5, 6, 256.0, A.mult, -1280.0, A.add)
-
-    def common(t, c):
-        (j0, j1), C = CH[c], str(c)
-        m = j1 - j0
-        nl = 2 * m
-        per = 16 if m <= 32 else 8
-        for h in range(16 // per):
-            d = dbank()
-            groups([([("BS", 128 * k, 128 * k + 128, "f16" + C, m, nl, 1), ("JN", 0, 128, "f16" + C, 0, m, 1)], d, m * (k - per * h), m * (k - per * h) + m, 1) for k in range(per * h, per * h + per)], "bcast")
-            vs("eq" + C, m * per * h, m * per * h + m * per, d, 0, m * per, 0.0, A.is_equal, name="eq")
-        nn = ("J1", 0, 128, "N16", H * t + j0, H * t + j1, 1)
-        groups([([nn] + [("I8", 0, 128, "eq" + C, m * k, m * k + m, 1) for k in range(16)], "cm", j0, j1, 1)], "ca")
-        act("rl" + C, 0, m, "cm", j0, j1, F.Relu, scale=-1.0, bias=4096.0, name="rl")
-        vt("rl" + C, 0, m, "f" + C, 0, m, "rl" + C, 0, m, A.max, "ls")
-        vc("lu" + C, 0, m, "rl" + C, 0, m, name="lu")
-        b0 = 256 + j0
-        groups([([nn] + [("W8", 16 - k, 144 - k, "eq" + C, m * k, m * k + m, 1) for k in range(16)], "sc", b0, b0 + m, 1)], "cb")
-        way = CFG["RG"][c]
-        if way == "B":
-            gather_s("gz" + C, 0, m * 8, "X", XW, "lu" + C, 0, m // 2, "rg")
-            gather_v("gz" + C, m * 8, m * 16, "X", XW, "lu" + C, m // 2, m, "rg")
-        elif way == "S":
-            gather_s("gz" + C, 0, m * 16, "X", XW, "lu" + C, 0, m, "rg")
+    for x in CFG["LOADS"].split():
+        q, k, s = {"Y": "Y", "S": "SD"}[x[0]], x[1], x[2]
+        r0 = 64 * int(s)
+        hbm = lambda nm, c0, c1, r0=r0: lambda T: T[nm][r0:r0 + 64, c0:c1] if c1 else T[nm][r0:r0 + 64, :]
+        if k in "pe":
+            nm, buf = {"p": ("p0", "p"), "e": ("ex", "exi")}[k]
+            prs = [(a(buf + s, 0, NL, h=1 + h), hbm(nm, NL * h, NL * h + NL)) for h in (0, 1)]
+        elif k == "w":
+            prs = [(a("wk" + s, c, c + 1, h=1 + h), hbm(nm, 0, 0)) for c, nm in enumerate(("wt", "km")) for h in (0, 1)]
         else:
-            gather_v("gz" + C, 0, m * 16, "X", XW, "lu" + C, 0, m, "rg")
-        vt("fe" + C, 0, m, "cm", j0, j1, "f" + C, 0, m, A.max, "fx")
-        vt("fe" + C, m, nl, "sc", b0, b0 + m, "f" + C, m, nl, A.max, "fx")
-        vs("ff" + C, 0, nl, "fe" + C, 0, nl, 4095, A.bitwise_and, name="F")
-        vs("F16" + C, 0, nl, "ff" + C, 0, nl, -2048.0, A.add, name="F16")
-        v(nl, [("FT" + C, 0, nl)], [("F16" + C, 0, nl)], lambda T, g: g.vector.transpose(ap(T, "FT" + C, 0, nl), ap(T, "F16" + C, 0, nl)), "FT", half=True)
-        f0, q, l0 = 300 + 16 * c, nl // 16, 16 * t + j0 // 8
-        groups(relay("FT" + C, 0, 16, "cm", f0, q), "relayF")
-        vs("f0s", l0, l0 + q, "cm", f0, f0 + q, 2048.0, A.add, name="f0s")
-        for bb in (0, 1):
-            vc("fnat", L * t + 2 * j0 + bb, L * t + 2 * j1, "ff" + C, m * bb, m * bb + m, ost=2, name="fnat")
-        v(m * 16, [("rs" + C, 0, m * 16)], [("gz" + C, 0, m * 16), ("smax", 0, m * 16)],
-          lambda T, g: g.vector.tensor_tensor_scan(ap(T, "rs" + C, 0, m * 16), ap(T, "smax", 0, m * 16), ap(T, "gz" + C, 0, m * 16), 0.0, A.mult, A.max), "rscan", half=True)
-        vc("qs", H * t + j0, H * t + j1, "rs" + C, 15, m * 16, half=True, ist=16, name="qs")
+            nm, buf, w = {"z": ("zp", "Z", A0), "r": ("rt", "ri", A0), "x": ("ax", "X", V)}[k]
+            prs = [(a(buf + s, 0, w, h=1 + h), hbm(nm, 0, 0)) for h in (0, 1)]
+        dma(q, prs, "ld_" + k + s, "ld_" + k + s, 128 * {"p": 192, "e": 384, "w": 8, "z": 2048, "r": 4096, "x": 8192}[k])
+        ops[-1]["chain"] = q
 
-    def send(t, kind, src, s0, s1, dst, d0, d1):
-        op("R", 0, [], [(src, s0, s1)], (t, dst, d0, d1, src, s0, s1, "ar_%s%d" % (kind, t)), kind="send", name="send_" + kind)
-        op("A", 0, [(dst, d0, d1)], [], "ar_%s%d" % (kind, t), kind="arr", name="arr_" + kind)
+    vm(a("ones", 0, 256), 1.0)
+    vm(a("w16", 0, 144), 16384.0)
+    gsel(a("tmpa", 0, 128), a("ones", 0, 128), [[-16, 8], [0, 16]], A.is_ge, 0, 1)
+    gsel(a("BB", 0, 128), a("tmpa", 0, 128), [[16, 8], [0, 16]], A.is_ge, 15, -1)
+    gsel(I, a("ones", 0, 128), [[-1, 128]], A.is_equal, 0, 1)
+    vm(a("half", 0, NP_), -0.5)
+    if "S" in "".join(CFG["VP"]):
+        act(a("tab", 0, 4), a("ones", 0, 4), F.Sigmoid, name="table")
+    gsel(a("tmpa", 0, 144), a("w16", 0, 144), [[-16, 9], [-1000, 16]], A.is_ge, 16, 1)
+    gsel(a("W", 0, 144), a("tmpa", 0, 144), [[16, 9], [0, 16]], A.is_ge, -1, -1)
+    for gl in (0, 1):
+        vm(nd("Cm", gl, slice(0, 16), slice(16 - 16 * gl, 32 - 16 * gl)), 0.0)
+        for h in (0, 1):
+            gsel(nd("Cm", gl, slice(0, 16), slice(16 * gl + h, 16 * gl + 16, 2)), a("ones", 0, 128), [[-8, 4], [-32, 4], [-1, 8]], A.is_equal, 0, 1)
+    giota(a("iom", 0, NL), [[0, 6], [1, 16]], 0, 0)
+    vs(a("smin", 0, NL), a("iom", 0, NL), 0.0, A.is_equal, 33554432.0, A.mult)
+    for nm, val in (("id32", 4096.0), ("I2080", 2080.0), ("IK", 337920.0), ("IM", 67584.0), ("I4096", 4096.0)):
+        vs(a(nm, 0, 128), I, val, A.mult)
+    giota(a("cj", 0, 1), [[1, 1]], 0, 1)
+    vs(a("ci", 0, 1), a("cj", 0, 1), 15, A.bitwise_and)
+    vc(a("pcol", 0, 1), a("ci", 0, 1))
+    vs(a("M16", 0, 16), a("iom", 0, 16), a("pcol", 0, 1), A.is_equal)
+    vs(a("maskc", 0, NL), a("iom", 0, NL), a("pcol", 0, 1), A.not_equal, 8192.0, A.mult)
+    vs(a("maskc", 0, NL), a("maskc", 0, NL), 2048.0, A.add)
+    for k in range(16):
+        vs(a("BS", 128 * k, 128 * k + 128), a("BB", 0, 128), a("M16", k, k + 1), A.mult, -1.0, A.mult)
+    giota(a("N32", 0, TT * NL), [[96, TT], [1, NP_], [0, 2]], B0, 0)
+    vs(a("N32", 0, TT * NL, h=2), a("N32", 0, TT * NL, h=2), float(NP_), A.add)
+    vs(a("N16", 0, TT * NL), a("N32", 0, TT * NL), -1.0, A.mult, 2048.0, A.add)
+    giota(a("smax", 0, 768), [[0, 48], [4096, 16]], 0, 0)
+    gsel(a("Sel", 0, 256), a("ones", 0, 256), [[-64, 2], [0, 2], [-1, 64]], A.is_equal, 0, 1)
+    vm(a("bar", 0, 1), 57344.0)
+    for s in "01":
+        cf = lambda c: a("cf" + s, c, c + 1)
+        vs(cf(0), a("wk" + s, 0, 1), 2048.0, A.is_ge)
+        vs(cf(1), a("wk" + s, 0, 1), 2.0 ** -12, A.mult, cf(0), A.subtract)
+        vs(a("Wm" + s, 0, 128), a("BB", 0, 128), cf(1), A.mult)
+        vs(cf(2), a("wk" + s, 1, 2), 2048.0, A.is_ge, 2.0 ** 24, A.mult)
+        vs(cf(3), a("wk" + s, 1, 2), 4096.0, A.mult, cf(2), A.subtract)
+        vs(cf(4), cf(3), 0.5, A.mult)
+        vm(a("c16" + s, NP_, 64), 0.0)
+        vm(a("X" + s, V, XW), 0.0)
+        vs(a("E16" + s, 0, NL), a("exi" + s, 0, NL), -2048.0, A.add)
+        for x, e in enumerate(CFG["RC"]):
+            w = A0 // len(CFG["RC"])
+            copy(e, a("R" + s, w * x, w * x + w), a("ri" + s, w * x, w * x + w), "R")
 
-    for t in range(TT):
+    def units(spec):
+        out, x = [], 0
+        for w in spec.split("."):
+            out.append((w[0], x, x + len(w)))
+            x += len(w)
+        return out
+
+    def round_(t, s):
         n = A0 + L * t
-        for c, (j0, j1) in enumerate(CH):
-            m = j1 - j0
-            for b in (0, 1):
-                if t:
-                    act("pn", L * t + 2 * j0 + b, L * t + 2 * j1, "p", 2 * j0 + b * m, 2 * j0 + b * m + m, F.Copy, ost=2, name="pnat")
-        for x in CFG["ORD"].split():
-            k, c = x[0], int(x[1]) if len(x) > 1 else 0
-            if k == "s":
-                send(t, "p", "pn", L * t, L * t + L, "Z", n, n + L)
-                if t == 0:
-                    setup()
-            elif k == "v":
-                vstage(t, c, int(x[2]))
-            elif k == "p":
-                prep(c)
+        b = lambda nm, lo, hi, st=1: a(nm + s, lo, hi, st)
+        lanes = lambda nm, st=1, ph=0: a(nm + s, ph, NL, st)
+        p = lambda st=1, ph=0: b("p", NL * t + ph, NL * t + NL, st)
+        bank = [0]
+
+        def dbank():
+            bank[0] ^= 1
+            return "d%d" % bank[0] + s
+        send(t, "p", b("pl", NL * t, NL * t + NL), p())
+        ps, v = b("ma", 0, NP_), lanes("ul", 2)
+        mm([(ps, b("Wm", 0, 128), p(2)), (ps, I, a("half", 0, NP_))], "u")
+        aff(b("q", 0, NP_), ps, 1.0, 2.0 ** -13, "q")
+        vt(v, ps, b("q", 0, NP_), A.subtract, "v")
+        act(b("uu", 0, NP_), v, F.Square, bias=2048.0, scale=4096.0, name="uu")
+        act(b("ma", 48, 96), v, F.Identity, bias=b("cf", 4, 5), scale=b("cf", 3, 4), name="ku")
+        act(lanes("ul", 2, 1), v, F.Identity, name="udup")
+        aff(b("q", 0, NP_), b("uu", 0, NP_), 1.0 / 32, -0.375, "r")
+        vt(b("hh", 0, NP_), b("ma", 48, 96), b("q", 0, NP_), A.add, "hh")
+        vs(b("hh", 0, NP_), b("hh", 0, NP_), 4095, A.bitwise_and, name="hm")
+        aff(b("cl", 0, NP_), b("hh", 0, NP_), n / 4096.0, -0.5 + 2.0 ** -13, "cl")
+        for k, e in enumerate(CFG["PREP"]):
+            copy(e, b("prep", k, 16 * NL, 16), p(), "prep")
+        aff(b("c16", 0, NP_), b("cl", 0, NP_), 1.0, 0.0, "c16")
+        op("V", 64, [b("cT", 0, 64)], [b("c16", 0, 64)], lambda T, g: g.vector.transpose(ap(T, b("cT", 0, 64)), ap(T, b("c16", 0, 64))), "cT")
+        key = b("ma", 96, 192)
+        mm([(key, I, a("iom0", 0, NL))] + [(b("ma", 96 + 16 * hi, 112 + 16 * hi), nd("Cm", gl, slice(hi % 4 * 4, hi % 4 * 4 + 4), slice(0, 32)), b("cT", 32 * (hi // 4) + 16 * gl, 32 * (hi // 4) + 16 * gl + 16))
+                                          for hi in range(6) for gl in (0, 1)], "keyc", stop=False)
+        for x, d in enumerate(("d0", "d1", "mb")):
+            mm([(a(d + s, 0, 512), I, b("prep", 512 * x, 512 * x + 512))], "Zp", stop=False)
+        for e, x0, x1 in units(CFG["ZG"]):
+            gneg(e, b("gz", 256 * x0, 256 * x1), b("Z", 0, n), b("cl", 16 * x0, 16 * x1), "Zg")
+        for x, d in enumerate(("d0", "d1", "mb")):
+            mm([(nd(d + s, slice(h, 32, 2), slice(0, 16)), I, b("gz", 256 * x, 256 * x + 256)) for h in (0, 1)], "Zsub", start=False)
+            act(nd("dz" + s, slice(2 * x, 2 * x + 2), slice(0, 16), slice(0, 16)), a(d + s, 0, 512), F.Abs, scale=0.25, name="Zabs")
+        for h0, h1 in CFG["SC"]:
+            mm([(b("ma", 96 + 16 * h0, 96 + 16 * h1), W(lo), nd("dz" + s, slice(h0, h1), lo, slice(0, 16))) for lo in range(16)], "score", start=False, stop=h1 == 6)
+        scan(lanes("ks"), a("smin", 0, NL), key, 33554432.0, A.max, A.min, "kmin")
+        aff(b("li", 0, 6), lanes("ks", 16, 15), 1.0, 0.0, "li")
+        vs(b("li", 0, 6), b("li", 0, 6), 4095, A.bitwise_and, name="lm")
+        aff(b("al", 0, 6), b("li", 0, 6), 1.0, 0.0, "al")
+        act(lanes("e16"), b("R", 0, n), F.Identity, bias=-2048.0, off=b("al", 0, 6), name="e16")
+        if CFG["EL"]:
+            gv(lanes("el"), b("R", 0, n), b("al", 0, 6), "eL")
+        gv(lanes("eu"), b("R", 0, n), b("al", 0, 6), "eu", lanes("ul"), A.mult)
+        if not CFG["EL"]:
+            aff(lanes("el"), lanes("e16"), 1.0, 2048.0, "eL")
+        y = b("mb", 0, NL)
+        mm([(y, a("id32", 0, 128), lanes("eu")), (y, a("I2080", 0, 128), lanes("e16"))], "y")
+        aff(lanes("yi"), y, 1.0, 65536.0 + 2464 * t, "yi")
+        vs(lanes("e2"), lanes("yi"), 5, A.arith_shift_right, 4095, A.bitwise_and, name="e2")
+        aff(lanes("e2l"), lanes("e2"), 1.0, 0.0, "e2L")
+        aff(lanes("e2c"), lanes("e2l"), 1.0, -2048.0, "e2c")
+        v1, k3, v2 = b("ma", 192, 288), b("ma", 288, 384), b("mb", 96, 192)
+        for w, (lst, gb) in enumerate((("el", "g1"), ("e2l", "g2"))):
+            for e, x0, x1 in units(CFG["VP"][w]):
+                c0, c1 = 256 * x0, 256 * x1
+                if e == "V":
+                    gv(b(gb, c0, c1), b("X", 0, V), b(lst, 16 * x0, 16 * x1), "votes", b("prep", c0, c1), A.is_ge)
+                else:
+                    act(b("x1", c0, c1), b("X", 0, V), F.Identity, scale=-1.0, off=b(lst, 16 * x0, 16 * x1), name="votesS")
+                    d = a(dbank(), 0, c1 - c0)
+                    mm([(d, I, b("prep", c0, c1)), (d, I, b("x1", c0, c1))], "vsub")
+                    act(b(gb, c0, c1), d, F.Sigmoid, bias=128.0, scale=-256.0, name="vsig")
+            if w == 0:
+                mm([(v1, I, lanes("e16"))] + [(v1, W(k), b(gb, k, 16 * NL, 16)) for k in range(16)], "v1")
+                act(lanes("s8"), v1, F.Sign, scale=-1.0, bias=139264.0, name="s8")
+                act(lanes("sg"), v1, F.Sign, scale=-1.0, bias=a("bar", t, t + 1), acc=a("cb", 2 * t + int(s), 2 * t + int(s) + 1), name="barred")
+                act(lanes("k2"), v1, F.Identity, bias=59392.0, name="k1")
+                mm([(k3, I, lanes("E16")), (k3, a("IK", 0, 128), lanes("sg"))], "k3")
+                vt(lanes("k2"), k3, lanes("k2"), A.max, "m13")
+                if s == "1" and t < TT - 1:
+                    par = b("ma", 500, 501)
+                    act(a("cs", 0, 1), a("cb", 2 * t, 2 * t + 1), F.Identity, bias=a("cb", 2 * t + 1, 2 * t + 2), name="par")
+                    mm([(par, a("ones", 0, 128), a("cs", 0, 1))], "par")
+                    aff(a("ci", 4, 5), par, 1.0, 0.0, "par1")
+                    vs(a("ci", 5, 6), a("ci", 4, 5), 1, A.arith_shift_right, 1, A.bitwise_and, name="par")
+                    aff(a("bar", t + 1, t + 2), a("ci", 5, 6), 16384.0, 57344.0, "par2")
             else:
-                {"h": hash_, "z": zstage, "E": elect, "c": choice, "m": common}[k](t, c)
-        send(t, "z", "f0s", 16 * t, 16 * t + 12, "f0l", 16 * t, 16 * t + 12)
-        send(t, "q", "qs", H * t, H * t + H, "ql", H * t, H * t + H)
-        send(t, "f", "fnat", L * t, L * t + L, "R", n, n + L)
-        for c, (j0, j1) in enumerate(CH):
-            m = j1 - j0
-            for b in (0, 1):
-                act("pc", 2 * j0 + b * m, 2 * j0 + b * m + m, "Z", n + 2 * j0 + b, n + 2 * j1, F.Identity, ist=2, scale=0.5, bias=1151.25, name="pc")
-        vs("Xh", 3712 + H * t, 3712 + H * t + H, "ql", H * t, H * t + H, -0.5, A.mult, half=True, name="Xhrec")
-        gather_v("p16", 0, L, "Xh", V, "f0l", 16 * t, 16 * t + 12, "newp", in1=("pc", 0, L), o_=A.add)
+                for l0, l1 in CFG["V2"]:
+                    o = b("mb", 96 + l0, 96 + l1)
+                    mm([(o, I, b("e2c", l0, l1))] + [(o, W(k), b(gb, 16 * l0 + k, 16 * l1, 16)) for k in range(16)] + [(o, a("IM", 0, 128), b("s8", l0, l1))], "v2")
+        vt(lanes("f"), v2, lanes("k2"), A.max, "m2")
+        vs(lanes("f"), lanes("f"), 4095, A.bitwise_and, name="f")
+        aff(lanes("f16"), lanes("f"), 1.0, -2048.0, "f16")
+        ca, cb, lu, fn_ = b("ma", 384, 432), b("mb", 192, 240), b("ma", 432, 480), b("mb", 336, 432)
+        for k0, k1 in CFG["BC"]:
+            d = dbank()
+            mm([[(a(d, 48 * k, 48 * k + 48), a("BS", 128 * (k0 + k), 128 * (k0 + k) + 128), lanes("f16", 2, 1)), (a(d, 48 * k, 48 * k + 48), I, lanes("f16", 2))] for k in range(k1 - k0)], "bcast")
+            vs(b("eq", 48 * k0, 48 * k1), a(d, 0, 48 * (k1 - k0)), 0.0, A.is_equal, name="eq")
+        for k0, k1 in CFG["BC"]:
+            mm([(ca, I, b("eq", 48 * k, 48 * k + 48)) for k in range(k0, k1)], "ca", start=k0 == 0, stop=k1 == 16)
+        act(lanes("nn", 2), ca, F.Relu, bias=1.0, scale=-1.0, name="nn")
+        mm([(lu, I, lanes("f16", 2)), (lu, a("I4096", 0, 128), lanes("nn", 2))], "lu")
+        vs(b("lu", 0, NP_), lu, 2048.0, A.add, 4096.0, A.min, name="lu")
+        mm([[(cb, W(k), b("eq", 48 * k, 48 * k + 48)) for k in range(16)], [(fn_, I, lanes("f16")), (fn_, I, a("N16", NL * t, NL * t + NL))]], "cb")
+        act(lanes("nn", 2, 1), cb, F.Relu, bias=1.0, scale=-1.0, name="nnB")
+        for e, x0, x1 in units(CFG["RG"]):
+            if e == "V":
+                gv(b("gz", 256 * x0, 256 * x1), b("X", 0, XW), b("lu", 16 * x0, 16 * x1), "rg")
+            else:
+                act(b("gz", 256 * x0, 256 * x1), b("X", 0, XW), F.Identity, off=b("lu", 16 * x0, 16 * x1), name="rg")
+        Fs = b("Fs", L * t, L * t + NL)
+        vt(fn_, fn_, lanes("nn"), A.mult, "delta")
+        vt(lanes("F16"), fn_, a("N16", NL * t, NL * t + NL), A.subtract, "F")
+        aff(Fs, lanes("F16"), 1.0, 2048.0, "F32")
+        f0 = b("ma", 0, NL)
+        mm([(f0, I, a("maskc", 0, NL)), (f0, a("BS", 0, 128), lanes("F16"))], "F0")
+        scan(b("Fs", L * t + NL, L * t + L), a("smin", 0, NL), f0, 33554432.0, A.max, A.min, "f0scan")
+        send(t, "f", b("Fl", L * t, L * t + L), b("Fs", L * t, L * t + L))
+        for x0, x1 in CFG["RS"]:
+            scan(b("rs", 256 * x0, 256 * x1), a("smax", 0, 256 * (x1 - x0)), b("gz", 256 * x0, 256 * x1), 0.0, A.min, A.max, "rscan")
+        d = dbank()
+        mm([[(a(d, 48 * h, 48 * h + 48), a("Sel", 128 * h, 128 * h + 128), b("rs", 15, 768, 16))] for h in (0, 1)], "Q")
+        copy(CFG["QC"], b("qs", NL * t, NL * t + NL), a(d, 0, NL), "qs")
+        send(t, "q", b("ql", NL * t, NL * t + NL), b("qs", NL * t, NL * t + NL))
         if t < TT - 1:
-            vs("p", 0, L, "p16", 0, L, -1024.0, A.add, half=True, name="p")
-            vc("X", 3712 + H * t, 3712 + H * t + H, "ql", H * t, H * t + H, half=True, name="Xrec")
-            parity()
+            for k, tab, src, c0, by in (("z", "Z", "pl", NL * t, 2), ("r", "R", "Fl", L * t, 4)):
+                dma("Y", [(a(tab + s, n + NL * h, n + NL * h + NL, h=1 + h2), a(src + s, c0, c0 + NL, h=1 + h)) for h in (0, 1) for h2 in (0, 1)], "dup_%s%s%d" % (k, s, t), "dup_" + k, 256 * NL * by)
+        r0 = 64 * int(s)
+        dma("Y", [(lambda T, h=h: T["yr"][r0:r0 + 64, L * t + NL * h:L * t + NL * h + NL], a("Fl" + s, L * t, L * t + NL, h=1 + h)) for h in (0, 1)], None, "yr", 128 * NL * 4)
+        aff(b("f0l", 0, 6), b("Fl", L * t + NL + 15, L * t + L, 16), -1.0, 4096.0, "f0l")
+        copy(CFG["XREC"], b("X", B0 + 96 * t, B0 + 96 * t + 96), b("ql", NL * t, NL * t + NL), "Xrec")
+        gv(lanes("pd"), b("X", 0, V), b("f0l", 0, 6), "newp", b("pl", NL * t, NL * t + NL), A.subtract)
+        aff(lanes("p16"), lanes("pd"), -0.5, 1663.25, "p16")
+        if t < TT - 1:
+            copy(CFG["PC"], b("p", NL * t + NL, NL * t + 2 * NL), lanes("p16"), "p", add=-1536.0)
         else:
-            for c, (j0, j1) in enumerate(CH):
-                m = j1 - j0
-                for b in (0, 1):
-                    vs("yo", 2 * j0 + b, 2 * j1, "p16", 2 * j0 + b * m, 2 * j0 + b * m + m, -1024.0, A.add, ost=2, name="yo")
-        op("Y", 0, [], [("R", n, n + L)], (lambda T, q, t=t, n=n: q.dma_start(T["yr"][:, L * t:L * t + L], T["R"][:, n:n + L])), kind="store", name="yr")
-    op("Y", 0, [], [("yo", 0, L)], (lambda T, q: q.dma_start(T["yp"][:, :], T["yo"][:, :])), kind="store", name="yp")
+            vs(lanes("yo"), lanes("p16"), -1536.0, A.add, name="yo")
+            dma("Y", [(lambda T, h=h: T["yp"][r0:r0 + 64, NL * h:NL * h + NL], a("yo" + s, 0, NL, h=1 + h)) for h in (0, 1)], None, "yp", 128 * NL * 4)
+
+    need("b", iom0=NL)
+    vm(a("iom0", 0, NL), 0.0)
+    for t in range(TT):
+        for s in "01":
+            cur[0] = s
+            round_(t, s)
     return ops
 
 
@@ -426,34 +429,35 @@ COMP = "VSPG"
 ONQ = {"R": "G", "SD": "S"}
 
 
-def meet(x, y):
-    return x[1] < y[2] and y[1] < x[2] and not (x[3] == y[3] and x[4] != y[4])
-
-
 def deps_of(ops):
-    hist, bank = {}, {}
+    hist, bank, chain = {}, {}, {}
     for i, o in enumerate(ops):
         raw, war = set(), set()
-        for x in o["r"]:
-            raw |= {j for (y, j, w) in hist.get(x[0], ()) if w and meet(x, y)}
-        for x in o["w"]:
-            war |= {j for (y, j, w) in hist.get(x[0], ()) if not w and meet(x, y)}
-            raw |= {j for (y, j, w) in hist.get(x[0], ()) if w and meet(x, y)}
-        for x in o["r"] + o["w"]:
-            if x[0] in PS:
-                war |= {j for e, j in bank.setdefault(x[0], {}).items() if e != o["e"]}
-        for x in o["r"]:
-            hist.setdefault(x[0], []).append((x, i, False))
-        for x in o["w"]:
-            hb = [(y, j, w) for (y, j, w) in hist.get(x[0], ()) if j == i or not (x[1] <= y[1] and y[2] <= x[2] and (x[3] == 1 or x[3:] == y[3:]))]
-            hb.append((x, i, True))
-            hist[x[0]] = hb
-        for x in o["r"] + o["w"]:
-            if x[0] in PS:
-                bank[x[0]][o["e"]] = i
+        rd, wr = [(x[0], x[2], cells(x)[1]) for x in o["r"]], [(x[0], x[2], cells(x)[1]) for x in o["w"]]
+        for n, h, m in rd:
+            raw |= {j for (h2, m2, j, w) in hist.get(n, ()) if w and h & h2 and m & m2}
+        for n, h, m in wr:
+            raw |= {j for (h2, m2, j, w) in hist.get(n, ()) if h & h2 and m & m2}
+        banks = {x[0] for x in rd + wr if x[0] in PS}
+        for n in banks:
+            war |= set(bank.setdefault(n, {}).values())
+        if "chain" in o:
+            war |= set(chain.get(o["chain"], ()))
+            chain[o["chain"]] = [i]
+        for n, h, m in rd:
+            hist.setdefault(n, []).append((h, m, i, False))
+        for n, h, m in wr:
+            hist[n] = [y for y in hist.get(n, ()) if y[2] == i or y[0] & ~h or y[1] & ~m] + [(h, m, i, True)]
+        for n in banks:
+            bank[n][o["e"]] = i
         raw.discard(i)
         war.discard(i)
         o["raw"], o["war"] = raw, war - raw
+
+
+def no_wait(p, o, j):
+    same = ONQ.get(p["e"], p["e"]) == ONQ.get(o["e"], o["e"])
+    return same and ("chain" in o and "chain" in p or p["k"] == "c" and (j not in o["raw"] and p["e"] != "G" or o["e"] == "P"))
 
 
 def schedule(ops):
@@ -461,30 +465,25 @@ def schedule(ops):
     succ = [[] for _ in range(n)]
     wake = EST["wake"]
     for i, o in enumerate(ops):
-        al = set(o["raw"]) | set(o["war"])
-        if o["k"] == "arr":
-            al.add(i - 1)
-        o["all"] = al
-        for j in al:
+        o["all"] = o["raw"] | o["war"] | ({i - 1} if o["k"] == "arr" else set())
+        for j in o["all"]:
             succ[j].append(i)
-    cost = [{"send": 300.0, "load": 60.0, "store": 60.0}.get(o["k"], o["c"]) for o in ops]
-    lat = [{"load": EST["dma"], "store": EST["dma"], "send": EST["send"]}.get(o["k"], 0.0) + (4000.0 if o["n"] == "ax" else 0.0) for o in ops]
+    cost = [{"send": EST["issue"], "dma": EST["dissue"] * o["ni"], "arr": 0.0}.get(o["k"], (o["cy"] * 0.83 * (EST["gather"] if o["g"] else 1) + o["fx"]) * EST["fac"] * (EST["pe"] if o["e"] == "P" else 1) + EST["fixed"][o["e"]] * o["ni"] if o["k"] == "c" else 0.0) for o in ops]
+    lat = [{"dma": EST["dma"], "send": EST["send"]}.get(o["k"], 0.0) + o["by"] / EST["rate"] for o in ops]
     queue = [ONQ.get(o["e"], o["e"]) for o in ops]
-    free_war = lambda i, j: queue[j] == queue[i] and i not in ops[j]["raw"] and ops[i]["k"] == "c"
     prio = [0.0] * n
     for i in range(n - 1, -1, -1):
-        prio[i] = max([0.0] + [prio[j] + (0.0 if free_war(i, j) or ops[j]["k"] == "arr" else wake) for j in succ[i]]) + cost[i] + lat[i]
-    for i, o in enumerate(ops):
-        if o["w"]:
-            prio[i] += CFG["PR"].get(o["n"] + o["w"][0][0][-1], 0.0)
-    nd = [len(o["all"]) for o in ops]
+        tail = CFG["BIAS"] if ops[i]["s"] == "0" else 0.0
+        prio[i] = max([tail + cost[i] + lat[i]] + [prio[j] + (cost[i] if no_wait(ops[i], ops[j], i) else cost[i] + lat[i] + (0.0 if ops[j]["k"] == "arr" else wake)) for j in succ[i]])
+    prio = [prio[i] + CFG["PR"].get(o["n"][:-1], 0.0) for i, o in enumerate(ops)]
+    nd_ = [len(o["all"]) for o in ops]
     ready = [0.0] * n
     free = {q: 0.0 for q in "VSPGYA"}
     avail = {q: [] for q in "VSPGYA"}
     for i in range(n):
-        if nd[i] == 0:
+        if nd_[i] == 0:
             avail[queue[i]].append(i)
-    order, busy, start, fin = [], {q: 0.0 for q in "VSPGYA"}, [0.0] * n, [0.0] * n
+    order, pipe, fin, start = [], 0.0, [0.0] * n, [0.0] * n
     while len(order) < n:
         best = None
         for q in avail:
@@ -497,16 +496,45 @@ def schedule(ops):
         st, q, i = best
         avail[q].remove(i)
         order.append(i)
-        start[i], fin[i] = st, st + cost[i] + lat[i]
+        fin[i] = st + cost[i] + lat[i]
+        if ops[i]["k"] == "dma":
+            pipe = max(pipe, st + cost[i]) + ops[i]["by"] / EST["rate"]
+            fin[i] = pipe + EST["dma"]
         if q != "A":
             free[q] = st + cost[i]
-        busy[q] += cost[i]
         for j in succ[i]:
-            ready[j] = max(ready[j], st if free_war(i, j) else fin[i] + (0.0 if ops[j]["k"] == "arr" else wake))
-            nd[j] -= 1
-            if nd[j] == 0:
+            ready[j] = max(ready[j], st if no_wait(ops[i], ops[j], i) else fin[i] + (0.0 if ops[j]["k"] == "arr" else wake))
+            nd_[j] -= 1
+            if nd_[j] == 0:
                 avail[queue[j]].append(j)
-    return order, max(fin), busy, start, fin
+        start[i] = st
+    lat = [fin[i] - start[i] - cost[i] for i in range(n)]
+    lag = lambda i, j: cost[i] + (0.0 if no_wait(ops[i], ops[j], i) else lat[i] + (0.0 if ops[j]["k"] == "arr" else wake))
+    fwd = [[(i, lag(i, j)) for i in ops[j]["all"]] for j in range(n)]
+    bwd = [[(j, cost[j] + lag(i, j) - cost[i]) for j in succ[i]] for i in range(n)]
+
+    def place(seq, pred, first):
+        at, used = [0.0] * n, {q: [] for q in free}
+        for i in seq:
+            t, u, c = max([first[i]] + [at[j] + d for j, d in pred[i]]), used[queue[i]], cost[i]
+            lo, hi = 0, len(u)
+            while lo < hi:
+                mid = (lo + hi) // 2
+                lo, hi = (mid + 1, hi) if u[mid][1] <= t else (lo, mid)
+            while lo < len(u) and u[lo][0] < t + c:
+                t, lo = max(t, u[lo][1]), lo + 1
+            if c:
+                u.insert(lo, (t, t + c))
+            at[i] = t
+        return at
+    span = lambda at: max(at[i] + cost[i] + lat[i] for i in range(n))
+    best = start
+    for _ in range(CFG["TURNS"]):
+        back = place(sorted(range(n), key=lambda i: (-start[i] - cost[i], -i)), bwd, lat)
+        start = place(sorted(range(n), key=lambda i: (-back[i] - cost[i], i)), fwd, [0.0] * n)
+        if span(start) < span(best):
+            best = start
+    return sorted(range(n), key=lambda i: (best[i], i)), span(best)
 
 
 PLAN = []
@@ -517,10 +545,10 @@ def plan():
         return PLAN[0]
     ops = build()
     deps_of(ops)
-    order, end, busy, start, fin = schedule(ops)
+    order, end = schedule(ops)
     cnt = {e: 0 for e in COMP}
     known = {q: {} for q in "VSPGY"}
-    clock, steps, nsent, nst = {}, [], 0, 0
+    clock, steps, nsent, nst, dsem = {}, [], 0, 0, {}
     for i in order:
         o = ops[i]
         e, k = o["e"], o["k"]
@@ -532,8 +560,7 @@ def plan():
         cl, req = known[q], {}
         for j in o["raw"] | o["war"]:
             p = ops[j]
-            pq = ONQ.get(p["e"], p["e"])
-            if p["k"] in ("send", "store") or (pq == q and p["k"] == "c" and (j not in o["raw"] or q == "P")):
+            if no_wait(p, o, j):
                 continue
             sem, val = p["sem"]
             if cl.get(sem, 0) < val and (sem not in req or ops[req[sem]]["sem"][1] < val):
@@ -543,26 +570,28 @@ def plan():
             if any(s2 != sem and clock[j2].get(sem, 0) >= val for s2, j2 in req.items()):
                 del req[sem]
         for sem, j in req.items():
-            for a, b in clock[j].items():
-                cl[a] = max(cl.get(a, 0), b)
+            for x, y in clock[j].items():
+                cl[x] = max(cl.get(x, 0), y)
         waits = sorted((sem, ops[j]["sem"][1]) for sem, j in req.items())
         inc = None
         if k == "c":
             cnt[e] += 1
-            inc = ("c" + e, 1)
-            o["sem"] = ("c" + e, cnt[e])
-        elif k == "load":
-            inc = o["sem"] = ("ld_" + o["n"], 16)
-        elif k == "store":
-            nst += 1
-            inc = ("stored", 16)
+            inc = "c" + e
+            o["sem"] = (inc, cnt[e])
+        elif k == "dma" and o["ds"]:
+            inc = o["ds"]
+            o["sem"] = (inc, 16 * o["ni"])
+            dsem[inc] = 16 * o["ni"]
+        elif k == "dma":
+            nst += o["ni"]
+            inc = "stored"
         else:
             nsent += 1
         if "sem" in o:
             clock[i] = dict(cl)
             clock[i][o["sem"][0]] = o["sem"][1]
         steps.append((q, waits, o, inc))
-    PLAN.append((steps, cnt, nsent, nst, end, busy, ops, order, start, fin))
+    PLAN.append((steps, cnt, nsent, nst, dsem, end))
     return PLAN[0]
 
 
@@ -570,26 +599,26 @@ def rank_program(g, core, T, topo):
     rank = T.rank_of(core)
     if rank is None:
         return
-    steps, cnt, nsent, nst = plan()[:4]
+    steps, cnt, nsent, nst, dsem = plan()[:5]
     qs = {"V": g.vector, "S": g.scalar, "P": g.tensor, "G": g, "Y": g.sync}
     for q, waits, o, inc in steps:
         for sem, val in waits:
             qs[q].wait_ge(T.sem[sem], int(val))
         if o["k"] == "send":
-            t, dst, d0, d1, src, s0, s1, ar = o["f"]
+            t, prs, ar = o["f"]
             to = T.cores[(rank + 1 + (t % 3)) % len(T.cores)]
             rid, pid, _se = topo.addr(to)
-            g.remote_dma(T[dst][:, d0:d1], T[src][:, s0:s1], T.sem[ar], T.sem.sent, pid, rid, topo.mask(core, to))
-        elif o["k"] in ("load", "store"):
-            o["f"](T, qs[q]).then_inc(T.sem[inc[0]], 16)
+            g.remote_dma(ap(T, prs[0][0]), ap(T, prs[0][1]), T.sem[ar], T.sem.sent, pid, rid, topo.mask(core, to))
+        elif o["k"] == "dma":
+            for ins in o["f"](T, qs[q]):
+                ins.then_inc(T.sem[inc], 16)
         else:
-            o["f"](T, g).then_inc(T.sem[inc[0]], 1)
+            o["f"](T, g).then_inc(T.sem[inc], 1)
     for e in COMP:
         g.sync.wait_ge(T.sem["c" + e], int(cnt[e]))
-    for n in LOADS:
-        g.sync.wait_ge(T.sem["ld_" + n], 16)
-    for t in range(TT):
-        for k in "pfqz":
-            g.sync.wait_ge(T.sem["ar_%s%d" % (k, t)], 16)
+    for sem in DSEM:
+        g.sync.wait_ge(T.sem[sem], dsem[sem])
+    for sem in ASEM:
+        g.sync.wait_ge(T.sem[sem], 16)
     g.sync.wait_ge(T.sem.stored, 16 * nst)
     g.wait_ge(T.sem.sent, 16 * nsent)

@@ -24,8 +24,9 @@ CFG = {
     "TURNS": 1,
     'BIAS': 4000, 'SLACK': 15, 'ZG': 'SS.S', 'SC': ((0, 4), (4, 6)), 'V2': ((0, 96),), 'BC': ((0, 6), (6, 12), (12, 16)), 'RS': ((0, 1), (1, 3)), 'EL': 0, 'RG': 'S.V.S', 'VP': ('V.V.V.V.S.S', 'VVV.VV.S'), 'XREC': 'S', 'QC': 'V', 'PC': 'S', 'PREP': 'GGGGVVVVVVSSSSSS', 'RC': 'SG', 'ONS': ('F32', 'e2L', 'e2c', 'f16', 'li', 'par1', 'par2', 'q'), 'PR': {'ku': 500, 'Xrec': -500, 'e2': 500, 'Zp': -500, 'delta': -2000, 'cl': -500, 'vsub': 500, 'eq': 200, 'q': -500, 'k3': 1000, 'v2': -2000, 'k1': -2000, 'cb': -2000, 'yo': -1000, 'rscan': -500, 'rg': -1000, 'eL': -1000, 'score': -2000},
     'BIAS': 4000, 'SLACK': 100, 'ZG': 'SSS', 'SC': ((0, 4), (4, 6)), 'V2': ((0, 96),), 'BC': ((0, 6), (6, 12), (12, 16)), 'RS': ((0, 1), (1, 3)), 'EL': 0, 'RG': 'S.SS', 'VP': ('VV.VV.SS', 'VV.V.V.SS'), 'XREC': 'V', 'QC': 'V', 'PC': 'V', 'PREP': 'GGGGVVVVVVVVVVVV', 'RC': 'SG', 'ONS': ('F32', 'e2c', 'par2'), 'PR': {'e2c': 500, 'f16': -200, 'yi': 200, 'u': -1000, 'dup_r': 1000, 'y': -500, 'vsub': 200, 'cT': -1000, 'eu': -2000, 'f0l': 1000, 'q': 2000, 'v1': 200, 'rg': -2000, 'e16': -1000},
+    'BIAS': 4000, 'SLACK': 100, 'ZG': 'V.S.V', 'SC': ((0, 4), (4, 6)), 'V2': ((0, 96),), 'BC': ((0, 8), (8, 16)), 'RS': ((0, 1), (1, 2), (2, 3)), 'EL': 1, 'RG': 'SS.V', 'VP': ('SS.VV.VV', 'SS.VV.VV'), 'XREC': 'V', 'QC': 'S', 'PC': 'V', 'PREP': 'GGGVVVVVVVSSSSSS', 'RC': 'SG', 'ONS': ('F32', 'c16', 'par2'), 'TURNS': 1, 'PR': {'cb': -500, 'Zabs': -500, 'v2': -2000, 'u': 2000, 'yo': -500, 'lu': -2000, 'li': -200, 'votesS': -2000, 'score': -500, 'rscan': 500},
 }
-EST = {"pe": 1.05, "fixed": {"V": 35.0, "S": 120.0, "P": 7.0, "G": 35.0}, "fac": 1.03, "gather": 1.5, "wake": 80.0, "dma": 1800.0, "send": 2300.0, "issue": 250.0, "rate": 350.0, "dissue": 60.0}
+EST = {"pe": 1.05, "fixed": {"V": 0.0, "S": 0.0, "P": 0.0, "G": 0.0}, "fac": 1.05, "gather": 1.5, "wake": 200.0, "dma": 1800.0, "send": 1200.0, "issue": 250.0, "rate": 300.0, "dissue": 500.0}
 DT = {"i": "int32", "u": "uint16", "f": "float32", "b": "bfloat16", "h": "float16"}
 ARENA = {"i": 4096, "u": 1024, "f": 6144, "b": 28672, "h": 4096}
 SCRATCH = {"Cm": ("sbuf", [128, 2, 16, 32], "bfloat16")}

@@ -25,6 +25,7 @@ CFG = {
     'BIAS': 4000, 'SLACK': 15, 'ZG': 'SS.S', 'SC': ((0, 4), (4, 6)), 'V2': ((0, 96),), 'BC': ((0, 6), (6, 12), (12, 16)), 'RS': ((0, 1), (1, 3)), 'EL': 0, 'RG': 'S.V.S', 'VP': ('V.V.V.V.S.S', 'VVV.VV.S'), 'XREC': 'S', 'QC': 'V', 'PC': 'S', 'PREP': 'GGGGVVVVVVSSSSSS', 'RC': 'SG', 'ONS': ('F32', 'e2L', 'e2c', 'f16', 'li', 'par1', 'par2', 'q'), 'PR': {'ku': 500, 'Xrec': -500, 'e2': 500, 'Zp': -500, 'delta': -2000, 'cl': -500, 'vsub': 500, 'eq': 200, 'q': -500, 'k3': 1000, 'v2': -2000, 'k1': -2000, 'cb': -2000, 'yo': -1000, 'rscan': -500, 'rg': -1000, 'eL': -1000, 'score': -2000},
     'BIAS': 4000, 'SLACK': 100, 'ZG': 'SSS', 'SC': ((0, 4), (4, 6)), 'V2': ((0, 96),), 'BC': ((0, 6), (6, 12), (12, 16)), 'RS': ((0, 1), (1, 3)), 'EL': 0, 'RG': 'S.SS', 'VP': ('VV.VV.SS', 'VV.V.V.SS'), 'XREC': 'V', 'QC': 'V', 'PC': 'V', 'PREP': 'GGGGVVVVVVVVVVVV', 'RC': 'SG', 'ONS': ('F32', 'e2c', 'par2'), 'PR': {'e2c': 500, 'f16': -200, 'yi': 200, 'u': -1000, 'dup_r': 1000, 'y': -500, 'vsub': 200, 'cT': -1000, 'eu': -2000, 'f0l': 1000, 'q': 2000, 'v1': 200, 'rg': -2000, 'e16': -1000},
     'BIAS': 4000, 'SLACK': 100, 'ZG': 'V.S.V', 'SC': ((0, 4), (4, 6)), 'V2': ((0, 96),), 'BC': ((0, 8), (8, 16)), 'RS': ((0, 1), (1, 2), (2, 3)), 'EL': 1, 'RG': 'SS.V', 'VP': ('SS.VV.VV', 'SS.VV.VV'), 'XREC': 'V', 'QC': 'S', 'PC': 'V', 'PREP': 'GGGVVVVVVVSSSSSS', 'RC': 'SG', 'ONS': ('F32', 'c16', 'par2'), 'TURNS': 1, 'PR': {'cb': -500, 'Zabs': -500, 'v2': -2000, 'u': 2000, 'yo': -500, 'lu': -2000, 'li': -200, 'votesS': -2000, 'score': -500, 'rscan': 500},
+    'BIAS': 4000, 'SLACK': 100, 'ZG': 'V.S.V', 'SC': ((0, 4), (4, 6)), 'V2': ((0, 96),), 'BC': ((0, 8), (8, 16)), 'RS': ((0, 1), (1, 3)), 'EL': 1, 'RG': 'S.V.S', 'VP': ('SS.VV.VV', 'SS.VV.VV'), 'XREC': 'VVVS', 'QC': 'S', 'PREP': 'GGGVVVVVVVSSSSSS', 'RC': 'GGGG', 'TURNS': 1, 'ONS': ('F32', 'c16', 'cl', 'e2c', 'p', 'par1', 'par2', 'pc'), 'PR': {'m13': 2000, 'ca': 200, 'k3': 2000, 'e2L': -2000, 'f0l': -500, 'par': -500, 'votesS': -1000, 'hh': 500, 'qs': -200, 'rg': -2000, 'c16': 500, 'uu': 2000, 'fa': 500, 'votes': -2000, 'nnB': -500},
 }
 EST = {"pe": 1.05, "fixed": {"V": 0.0, "S": 0.0, "P": 0.0, "G": 0.0}, "fac": 1.05, "gather": 1.5, "wake": 200.0, "dma": 1800.0, "send": 1200.0, "issue": 250.0, "rate": 300.0, "dissue": 500.0}
 DT = {"i": "int32", "u": "uint16", "f": "float32", "b": "bfloat16", "h": "float16"}
@@ -170,8 +171,8 @@ def build():
         else:
             vc(o, i, name)
 
-    def aff(o, i, mul, add, name):
-        if name in CFG["ONS"]:
+    def aff(o, i, mul, add, name, eng=None):
+        if eng == "S" or name in CFG["ONS"]:
             act(o, i, F.Identity, bias=add, scale=mul, name=name)
         elif mul == 1 and add == 0:
             vc(o, i, name)
@@ -203,16 +204,16 @@ def build():
         op("R", 0, [], [src], (t, [(dst, src)], sem), "send_" + kind, kind="send", by=by)
         op("A", 0, [dst], [], sem, "arr_" + kind, kind="arr")
 
-    need("b", ones=256, w16=144, tmpa=144, BB=128, W=144, I=128, I2080=128, I4096=128, IK=128, BS=2048, Sel=256, smax=768, maskc=NL, half=NP_, IM=128, cs=1)
-    need("f", id32=128, iom=NL, M16=16, smin=NL, N32=TT * NL, pcol=1, bar=TT, cb=2 * TT, tab=8)
+    need("b", ones=256, w16=144, tmpa=144, BB=128, W=144, I=128, IK=128, BS=2048, smax=768, maskc=NL, half=NP_, c1536=NP_, c2048=NP_, IM=128, cs=1)
+    need("f", iom=NL, M16=16, smin=NL, N32=TT * NL, pcol=1, bar=TT, cb=2 * TT, tab=8)
     need("h", N16=TT * NL)
     need("i", ci=8, cj=8)
     for s in "01":
-        need("i", **{x + s: w for x, w in (("ri", A0), ("exi", NL), ("wk", 2), ("q", NP_), ("hh", NP_), ("li", 6), ("yi", NL), ("e2", NL), ("f", NL))})
+        need("i", **{x + s: w for x, w in (("ri", A0), ("exi", NL), ("wk", 4), ("q", NP_), ("r", NP_), ("hh", NP_), ("ks", NL), ("li", 6), ("yi", NL), ("e2", NL))})
         need("u", **{x + s: w for x, w in (("cl", NP_), ("al", 6), ("el", NL), ("e2l", NL), ("lu", NP_), ("f0l", 6))})
-        need("f", **{x + s: w for x, w in (("cf", 8), ("ul", NL), ("uu", NP_), ("ks", NL), ("eu", NL), ("k2", NL), ("Fs", TT * L), ("Fl", TT * L), ("yo", NL))})
-        need("h", **{x + s: w for x, w in (("Wm", 128), ("E16", NL), ("c16", 64), ("cT", 64), ("e16", NL), ("e2c", NL), ("F16", NL), ("f16", NL), ("pd", NL), ("p16", NL))})
-        need("b", **{x + s: w for x, w in (("p", TT * NL), ("pl", TT * NL), ("qs", TT * NL), ("ql", TT * NL), ("prep", 16 * NL), ("gz", 768), ("g1", 16 * NL),
+        need("f", **{x + s: w for x, w in (("cf", 8), ("v", NP_), ("ul", NL), ("uu", NP_), ("eu", NL), ("ed", NL), ("k2", NL), ("pc", NL), ("Fs", TT * L), ("Fl", TT * L), ("yo", NL))})
+        need("h", **{x + s: w for x, w in (("Wm", 128), ("WH", 128), ("WL", 128), ("E16", NL), ("c16", 64), ("cT", 64), ("e16", NL), ("e2c", NL), ("F16", NL), ("f16", NL), ("p2", NL))})
+        need("b", **{x + s: w for x, w in (("p", TT * NL), ("pl", TT * NL), ("qs", TT * NP_), ("ql", TT * NP_), ("kb", NL), ("nt", NP_), ("prep", 16 * NL), ("gz", 768), ("g1", 16 * NL),
                                           ("g2", 16 * NL), ("x1", 16 * NL), ("sg", NL), ("s8", NL), ("nn", NL), ("eq", 768), ("rs", 768))})
     I, W = a("I", 0, 128), lambda k: a("W", 16 - k, 144 - k)
 
@@ -237,6 +238,8 @@ def build():
     gsel(a("BB", 0, 128), a("tmpa", 0, 128), [[16, 8], [0, 16]], A.is_ge, 15, -1)
     gsel(I, a("ones", 0, 128), [[-1, 128]], A.is_equal, 0, 1)
     vm(a("half", 0, NP_), -0.5)
+    vm(a("c1536", 0, NP_), -1536.0)
+    vm(a("c2048", 0, NP_), 2048.0)
     if "S" in "".join(CFG["VP"]):
         act(a("tab", 0, 4), a("ones", 0, 4), F.Sigmoid, name="table")
     gsel(a("tmpa", 0, 144), a("w16", 0, 144), [[-16, 9], [-1000, 16]], A.is_ge, 16, 1)
@@ -247,7 +250,7 @@ def build():
             gsel(nd("Cm", gl, slice(0, 16), slice(16 * gl + h, 16 * gl + 16, 2)), a("ones", 0, 128), [[-8, 4], [-32, 4], [-1, 8]], A.is_equal, 0, 1)
     giota(a("iom", 0, NL), [[0, 6], [1, 16]], 0, 0)
     vs(a("smin", 0, NL), a("iom", 0, NL), 0.0, A.is_equal, 33554432.0, A.mult)
-    for nm, val in (("id32", 4096.0), ("I2080", 2080.0), ("IK", 337920.0), ("IM", 67584.0), ("I4096", 4096.0)):
+    for nm, val in (("IK", 1327104.0), ("IM", 1048576.0)):
         vs(a(nm, 0, 128), I, val, A.mult)
     giota(a("cj", 0, 1), [[1, 1]], 0, 1)
     vs(a("ci", 0, 1), a("cj", 0, 1), 15, A.bitwise_and)
@@ -261,7 +264,6 @@ def build():
     vs(a("N32", 0, TT * NL, h=2), a("N32", 0, TT * NL, h=2), float(NP_), A.add)
     vs(a("N16", 0, TT * NL), a("N32", 0, TT * NL), -1.0, A.mult, 2048.0, A.add)
     giota(a("smax", 0, 768), [[0, 48], [4096, 16]], 0, 0)
-    gsel(a("Sel", 0, 256), a("ones", 0, 256), [[-64, 2], [0, 2], [-1, 64]], A.is_equal, 0, 1)
     vm(a("bar", 0, 1), 57344.0)
     for s in "01":
         cf = lambda c: a("cf" + s, c, c + 1)
@@ -271,6 +273,11 @@ def build():
         vs(cf(2), a("wk" + s, 1, 2), 2048.0, A.is_ge, 2.0 ** 24, A.mult)
         vs(cf(3), a("wk" + s, 1, 2), 4096.0, A.mult, cf(2), A.subtract)
         vs(cf(4), cf(3), 0.5, A.mult)
+        vs(a("wk" + s, 2, 3), a("wk" + s, 0, 1), 63, A.bitwise_and)
+        vs(cf(5), a("wk" + s, 2, 3), -2.0 ** -13, A.mult)
+        vs(cf(6), cf(1), -0.5, A.mult, cf(5), A.subtract)
+        vs(a("WL" + s, 0, 128), a("BB", 0, 128), cf(5), A.mult)
+        vs(a("WH" + s, 0, 128), a("BB", 0, 128), cf(6), A.mult)
         vm(a("c16" + s, NP_, 64), 0.0)
         vm(a("X" + s, V, XW), 0.0)
         vs(a("E16" + s, 0, NL), a("exi" + s, 0, NL), -2048.0, A.add)
@@ -296,19 +303,27 @@ def build():
             bank[0] ^= 1
             return "d%d" % bank[0] + s
         send(t, "p", b("pl", NL * t, NL * t + NL), p())
-        ps, v = b("ma", 0, NP_), lanes("ul", 2)
-        mm([(ps, b("Wm", 0, 128), p(2)), (ps, I, a("half", 0, NP_))], "u")
+        ps, v = b("ma", 0, NP_), b("v", 0, NP_)
+        if t:
+            mm([(ps, b("Wm", 0, 128), a("c1536", 0, NP_)), (ps, I, a("half", 0, NP_))], "uc", stop=False)
+            mm([(ps, b("WH", 0, 128), lanes("p2", 2)), (ps, b("WL", 0, 128), lanes("p2", 2))], "u", start=False)
+        else:
+            mm([(ps, I, a("half", 0, NP_)), (ps, b("Wm", 0, 128), p(2))], "u")
         aff(b("q", 0, NP_), ps, 1.0, 2.0 ** -13, "q")
         vt(v, ps, b("q", 0, NP_), A.subtract, "v")
         act(b("uu", 0, NP_), v, F.Square, bias=2048.0, scale=4096.0, name="uu")
         act(b("ma", 48, 96), v, F.Identity, bias=b("cf", 4, 5), scale=b("cf", 3, 4), name="ku")
-        act(lanes("ul", 2, 1), v, F.Identity, name="udup")
-        aff(b("q", 0, NP_), b("uu", 0, NP_), 1.0 / 32, -0.375, "r")
-        vt(b("hh", 0, NP_), b("ma", 48, 96), b("q", 0, NP_), A.add, "hh")
+        for h in (0, 1):
+            aff(lanes("ul", 2, h), v, 4096.0, 0.0, "udup")
+        aff(b("r", 0, NP_), b("uu", 0, NP_), 1.0 / 32, -0.375, "r")
+        vt(b("hh", 0, NP_), b("ma", 48, 96), b("r", 0, NP_), A.add, "hh")
         vs(b("hh", 0, NP_), b("hh", 0, NP_), 4095, A.bitwise_and, name="hm")
         aff(b("cl", 0, NP_), b("hh", 0, NP_), n / 4096.0, -0.5 + 2.0 ** -13, "cl")
         for k, e in enumerate(CFG["PREP"]):
-            copy(e, b("prep", k, 16 * NL, 16), p(), "prep")
+            if e == "G" or t == 0:
+                copy(e, b("prep", k, 16 * NL, 16), p(), "prep")
+            else:
+                aff(b("prep", k, 16 * NL, 16), lanes("p2"), -0.5, -1536.0, "prep", e)
         aff(b("c16", 0, NP_), b("cl", 0, NP_), 1.0, 0.0, "c16")
         op("V", 64, [b("cT", 0, 64)], [b("c16", 0, 64)], lambda T, g: g.vector.transpose(ap(T, b("cT", 0, 64)), ap(T, b("c16", 0, 64))), "cT")
         key = b("ma", 96, 192)
@@ -324,18 +339,16 @@ def build():
         for h0, h1 in CFG["SC"]:
             mm([(b("ma", 96 + 16 * h0, 96 + 16 * h1), W(lo), nd("dz" + s, slice(h0, h1), lo, slice(0, 16))) for lo in range(16)], "score", start=False, stop=h1 == 6)
         scan(lanes("ks"), a("smin", 0, NL), key, 33554432.0, A.max, A.min, "kmin")
-        aff(b("li", 0, 6), lanes("ks", 16, 15), 1.0, 0.0, "li")
-        vs(b("li", 0, 6), b("li", 0, 6), 4095, A.bitwise_and, name="lm")
+        vs(b("li", 0, 6), lanes("ks", 16, 15), 4095, A.bitwise_and, name="lm")
         aff(b("al", 0, 6), b("li", 0, 6), 1.0, 0.0, "al")
+        act(lanes("ed"), b("R", 0, n), F.Identity, scale=2080.0, bias=2464.0 * t - 4194304.0, off=b("al", 0, 6), name="ed")
         act(lanes("e16"), b("R", 0, n), F.Identity, bias=-2048.0, off=b("al", 0, 6), name="e16")
         if CFG["EL"]:
             gv(lanes("el"), b("R", 0, n), b("al", 0, 6), "eL")
         gv(lanes("eu"), b("R", 0, n), b("al", 0, 6), "eu", lanes("ul"), A.mult)
         if not CFG["EL"]:
             aff(lanes("el"), lanes("e16"), 1.0, 2048.0, "eL")
-        y = b("mb", 0, NL)
-        mm([(y, a("id32", 0, 128), lanes("eu")), (y, a("I2080", 0, 128), lanes("e16"))], "y")
-        aff(lanes("yi"), y, 1.0, 65536.0 + 2464 * t, "yi")
+        vt(lanes("yi"), lanes("eu"), lanes("ed"), A.add, "yi")
         vs(lanes("e2"), lanes("yi"), 5, A.arith_shift_right, 4095, A.bitwise_and, name="e2")
         aff(lanes("e2l"), lanes("e2"), 1.0, 0.0, "e2L")
         aff(lanes("e2c"), lanes("e2l"), 1.0, -2048.0, "e2c")
@@ -354,7 +367,7 @@ def build():
                 mm([(v1, I, lanes("e16"))] + [(v1, W(k), b(gb, k, 16 * NL, 16)) for k in range(16)], "v1")
                 act(lanes("s8"), v1, F.Sign, scale=-1.0, bias=139264.0, name="s8")
                 act(lanes("sg"), v1, F.Sign, scale=-1.0, bias=a("bar", t, t + 1), acc=a("cb", 2 * t + int(s), 2 * t + int(s) + 1), name="barred")
-                act(lanes("k2"), v1, F.Identity, bias=59392.0, name="k1")
+                act(lanes("k2"), v1, F.Identity, bias=1040384.0, name="k1")
                 mm([(k3, I, lanes("E16")), (k3, a("IK", 0, 128), lanes("sg"))], "k3")
                 vt(lanes("k2"), k3, lanes("k2"), A.max, "m13")
                 if s == "1" and t < TT - 1:
@@ -368,19 +381,20 @@ def build():
                 for l0, l1 in CFG["V2"]:
                     o = b("mb", 96 + l0, 96 + l1)
                     mm([(o, I, b("e2c", l0, l1))] + [(o, W(k), b(gb, 16 * l0 + k, 16 * l1, 16)) for k in range(16)] + [(o, a("IM", 0, 128), b("s8", l0, l1))], "v2")
-        vt(lanes("f"), v2, lanes("k2"), A.max, "m2")
-        vs(lanes("f"), lanes("f"), 4095, A.bitwise_and, name="f")
-        aff(lanes("f16"), lanes("f"), 1.0, -2048.0, "f16")
+        vt(lanes("kb"), v2, lanes("k2"), A.max, "m2")
+        vt(b("mb", 0, NL), v2, lanes("k2"), A.max, "m2")
+        vt(lanes("f16"), b("mb", 0, NL), lanes("kb"), A.subtract, "f16")
         ca, cb, lu, fn_ = b("ma", 384, 432), b("mb", 192, 240), b("ma", 432, 480), b("mb", 336, 432)
         for k0, k1 in CFG["BC"]:
             d = dbank()
             mm([[(a(d, 48 * k, 48 * k + 48), a("BS", 128 * (k0 + k), 128 * (k0 + k) + 128), lanes("f16", 2, 1)), (a(d, 48 * k, 48 * k + 48), I, lanes("f16", 2))] for k in range(k1 - k0)], "bcast")
             vs(b("eq", 48 * k0, 48 * k1), a(d, 0, 48 * (k1 - k0)), 0.0, A.is_equal, name="eq")
+        mm([(lu, I, lanes("f16", 2)), (lu, I, a("c2048", 0, NP_))], "fa")
         for k0, k1 in CFG["BC"]:
             mm([(ca, I, b("eq", 48 * k, 48 * k + 48)) for k in range(k0, k1)], "ca", start=k0 == 0, stop=k1 == 16)
-        act(lanes("nn", 2), ca, F.Relu, bias=1.0, scale=-1.0, name="nn")
-        mm([(lu, I, lanes("f16", 2)), (lu, a("I4096", 0, 128), lanes("nn", 2))], "lu")
-        vs(b("lu", 0, NP_), lu, 2048.0, A.add, 4096.0, A.min, name="lu")
+        vs(b("nt", 0, NP_), ca, 0.0, A.is_equal, 4096.0, A.mult, name="nt")
+        vt(b("lu", 0, NP_), lu, b("nt", 0, NP_), A.max, "lu")
+        aff(lanes("nn", 2), b("nt", 0, NP_), 2.0 ** -12, 0.0, "nn")
         mm([[(cb, W(k), b("eq", 48 * k, 48 * k + 48)) for k in range(16)], [(fn_, I, lanes("f16")), (fn_, I, a("N16", NL * t, NL * t + NL))]], "cb")
         act(lanes("nn", 2, 1), cb, F.Relu, bias=1.0, scale=-1.0, name="nnB")
         for e, x0, x1 in units(CFG["RG"]):
@@ -398,23 +412,23 @@ def build():
         send(t, "f", b("Fl", L * t, L * t + L), b("Fs", L * t, L * t + L))
         for x0, x1 in CFG["RS"]:
             scan(b("rs", 256 * x0, 256 * x1), a("smax", 0, 256 * (x1 - x0)), b("gz", 256 * x0, 256 * x1), 0.0, A.min, A.max, "rscan")
-        d = dbank()
-        mm([[(a(d, 48 * h, 48 * h + 48), a("Sel", 128 * h, 128 * h + 128), b("rs", 15, 768, 16))] for h in (0, 1)], "Q")
-        copy(CFG["QC"], b("qs", NL * t, NL * t + NL), a(d, 0, NL), "qs")
-        send(t, "q", b("ql", NL * t, NL * t + NL), b("qs", NL * t, NL * t + NL))
+        copy(CFG["QC"], b("qs", NP_ * t, NP_ * t + NP_), b("rs", 15, 768, 16), "qs")
+        send(t, "q", b("ql", NP_ * t, NP_ * t + NP_), b("qs", NP_ * t, NP_ * t + NP_))
         if t < TT - 1:
             for k, tab, src, c0, by in (("z", "Z", "pl", NL * t, 2), ("r", "R", "Fl", L * t, 4)):
                 dma("Y", [(a(tab + s, n + NL * h, n + NL * h + NL, h=1 + h2), a(src + s, c0, c0 + NL, h=1 + h)) for h in (0, 1) for h2 in (0, 1)], "dup_%s%s%d" % (k, s, t), "dup_" + k, 256 * NL * by)
         r0 = 64 * int(s)
         dma("Y", [(lambda T, h=h: T["yr"][r0:r0 + 64, L * t + NL * h:L * t + NL * h + NL], a("Fl" + s, L * t, L * t + NL, h=1 + h)) for h in (0, 1)], None, "yr", 128 * NL * 4)
         aff(b("f0l", 0, 6), b("Fl", L * t + NL + 15, L * t + L, 16), -1.0, 4096.0, "f0l")
-        copy(CFG["XREC"], b("X", B0 + 96 * t, B0 + 96 * t + 96), b("ql", NL * t, NL * t + NL), "Xrec")
-        gv(lanes("pd"), b("X", 0, V), b("f0l", 0, 6), "newp", b("pl", NL * t, NL * t + NL), A.subtract)
-        aff(lanes("p16"), lanes("pd"), -0.5, 1663.25, "p16")
+        for x, e in enumerate(CFG["XREC"]):
+            c0 = B0 + 96 * t + NP_ * (x % 2)
+            copy(e, a("X" + s, c0, c0 + NP_, h=1 + x // 2), a("ql" + s, NP_ * t, NP_ * t + NP_, h=1 + x % 2), "Xrec")
+        aff(lanes("pc"), b("pl", NL * t, NL * t + NL), 1.0, 3326.5, "pc")
+        gv(lanes("p2"), b("X", 0, V), b("f0l", 0, 6), "newp", lanes("pc"), A.subtract)
         if t < TT - 1:
-            copy(CFG["PC"], b("p", NL * t + NL, NL * t + 2 * NL), lanes("p16"), "p", add=-1536.0)
+            aff(b("p", NL * t + NL, NL * t + 2 * NL), lanes("p2"), -0.5, -1536.0, "p")
         else:
-            vs(lanes("yo"), lanes("p16"), -1536.0, A.add, name="yo")
+            aff(lanes("yo"), lanes("p2"), -0.5, -1536.0, "yo")
             dma("Y", [(lambda T, h=h: T["yp"][r0:r0 + 64, NL * h:NL * h + NL], a("yo" + s, 0, NL, h=1 + h)) for h in (0, 1)], None, "yp", 128 * NL * 4)
 
     need("b", iom0=NL)

@@ -4,7 +4,8 @@ from concourse.mybir import dt, AluOpType as A, ActivationFunctionType as F
 V, L, A0, TT = 4096, 192, 1024, 4
 NL, NP_ = 96, 48
 B0 = V - TT * 96
-XW = V + 16
+XO = TT * 96
+XV, XW = XO + V, XO + V + 16
 RW = A0 + (TT - 1) * L
 CFG = {
     "PREP": "GGGGGGGVVVVVSSSS",
@@ -26,10 +27,19 @@ CFG = {
     'BIAS': 4000, 'SLACK': 100, 'ZG': 'SSS', 'SC': ((0, 4), (4, 6)), 'V2': ((0, 96),), 'BC': ((0, 6), (6, 12), (12, 16)), 'RS': ((0, 1), (1, 3)), 'EL': 0, 'RG': 'S.SS', 'VP': ('VV.VV.SS', 'VV.V.V.SS'), 'XREC': 'V', 'QC': 'V', 'PC': 'V', 'PREP': 'GGGGVVVVVVVVVVVV', 'RC': 'SG', 'ONS': ('F32', 'e2c', 'par2'), 'PR': {'e2c': 500, 'f16': -200, 'yi': 200, 'u': -1000, 'dup_r': 1000, 'y': -500, 'vsub': 200, 'cT': -1000, 'eu': -2000, 'f0l': 1000, 'q': 2000, 'v1': 200, 'rg': -2000, 'e16': -1000},
     'BIAS': 4000, 'SLACK': 100, 'ZG': 'V.S.V', 'SC': ((0, 4), (4, 6)), 'V2': ((0, 96),), 'BC': ((0, 8), (8, 16)), 'RS': ((0, 1), (1, 2), (2, 3)), 'EL': 1, 'RG': 'SS.V', 'VP': ('SS.VV.VV', 'SS.VV.VV'), 'XREC': 'V', 'QC': 'S', 'PC': 'V', 'PREP': 'GGGVVVVVVVSSSSSS', 'RC': 'SG', 'ONS': ('F32', 'c16', 'par2'), 'TURNS': 1, 'PR': {'cb': -500, 'Zabs': -500, 'v2': -2000, 'u': 2000, 'yo': -500, 'lu': -2000, 'li': -200, 'votesS': -2000, 'score': -500, 'rscan': 500},
     'BIAS': 4000, 'SLACK': 100, 'ZG': 'V.S.V', 'SC': ((0, 4), (4, 6)), 'V2': ((0, 96),), 'BC': ((0, 8), (8, 16)), 'RS': ((0, 1), (1, 3)), 'EL': 1, 'RG': 'S.V.S', 'VP': ('SS.VV.VV', 'SS.VV.VV'), 'XREC': 'VVVS', 'QC': 'S', 'PREP': 'GGGVVVVVVVSSSSSS', 'RC': 'GGGG', 'TURNS': 1, 'ONS': ('F32', 'c16', 'cl', 'e2c', 'p', 'par1', 'par2', 'pc'), 'PR': {'m13': 2000, 'ca': 200, 'k3': 2000, 'e2L': -2000, 'f0l': -500, 'par': -500, 'votesS': -1000, 'hh': 500, 'qs': -200, 'rg': -2000, 'c16': 500, 'uu': 2000, 'fa': 500, 'votes': -2000, 'nnB': -500},
+    "QV": 0, "ZD": 0, "ZZ": 0, "VS": 1, "XREC": "VSVS", "ONS": ('F32', 'c16', 'e2c', 'nn', 'par2'), "LAM": 1.0, "TEMP": 0.0, "SHAKES": 0, "SEED": 0, "BU": 0, "LOADS": "Yp0 Sw0 Yk0 Sz0 Yr0 Yx0 Yp1 Yw1 Yk1 Yz1 Ye0 Yr1 Yx1 Ye1",
+    'BIAS': 4000, 'SLACK': 50, 'ZG': 'V.S.V', 'SC': ((0, 4), (4, 6)), 'V2': ((0, 96),), 'BC': ((0, 3), (3, 10), (10, 16)), 'RS': ((0, 1), (1, 3)), 'EL': 1, 'RG': 'S.V.S', 'VP': ('SS.S.V.VV', 'S.V.VV.VV'), 'XREC': 'VVVV', 'QC': 'S', 'PREP': 'GGGGVVVVVVVVVVVV', 'RC': 'GG', 'TURNS': 1, 'ONS': ('F32', 'c16', 'cl', 'eL', 'p', 'par2', 'pc', 'r', 'udup', 'yo'), 'VS': 1, 'LOADS': 'Yp0 Sw0 Yz0 Sk0 Yr0 Sw1 Yx0 Yp1 Yk1 Yz1 Yr1 Ye0 Yx1 Ye1', 'PR': {'eL': 2000, 'par1': 2000, 'barred': 1000, 'k3': 1000, 'Xrec': -500},
+    'BIAS': 4000, 'SLACK': 50, 'ZG': 'V.S.V', 'SC': ((0, 4), (4, 6)), 'V2': ((0, 96),), 'BC': ((0, 3), (3, 10), (10, 16)), 'RS': ((0, 1), (1, 3)), 'EL': 2, 'RG': 'S.V.S', 'VP': ('SS.S.V.VV', 'S.V.VV.VV'), 'XREC': 'VVVV', 'QC': 'S', 'PREP': 'GGGGVVVVVVVVVVVV', 'RC': 'GS', 'TURNS': 1, 'ONS': ('F32', 'c16', 'eL', 'nn', 'p', 'par1', 'par2', 'pc', 'r', 'udup', 'yo'), 'VS': 1, 'LOADS': 'Yw Sp Yk Sz0 Yr0 Yz1 Yx0 Ye Yr1 Yx1', 'PR': {'eL': 2000, 'par1': 2000, 'barred': 1000, 'k3': 1000, 'Xrec': -500, 'qs': 500, 'yp': 500, 'vp': 2000, 'ku': -500, 'v': -2000, 'eu': 1000},
+    'BIAS': 4000, 'SLACK': 50, 'ZG': 'VV.SS.VV', "ZP": ((0, 2), (2, 4), (4, 6)), 'SC': ((0, 4), (4, 6)), 'V2': ((0, 96),), 'BC': ((0, 10), (10, 16)), 'RS': ((0, 2), (2, 6)), 'EL': 2, 'RG': 'SS.VV.SS', 'VP': ('SS.S.V.VV', 'S.V.VV.VV'), 'XREC': 'VSVS', 'QC': 'S', 'PREP': 'GGGGVVVVSSSSSSSS', 'RC': 'GS', 'TURNS': 1, 'ONS': ('F32', 'al', 'c16', 'e16', 'e2c', 'eL', 'f0l', 'par1', 'par2', 'pc', 'udup', 'yo'), 'VS': 1, 'LOADS': 'Yw Sp Yk Sz0 Yr0 Yz1 Yx0 Ye Yr1 Yx1', 'PR': {'eL': 2000, 'par1': 2000, 'barred': 1000, 'k3': 1000, 'Xrec': -500, 'qs': 500, 'yp': 500, 'vp': 2000, 'ku': 200, 'v': -2000, 'eu': 1000, 'kf': 200, 'votes': -200, 'v2': -2000, 'nt': 1000, 'kmin': -200},
+    'BIAS': 4000, 'SLACK': 50, 'ZG': 'VV.VV.SS', 'SC': ((0, 4), (4, 6)), 'V2': ((0, 96),), 'BC': ((0, 10), (10, 16)), 'RS': ((0, 2), (2, 6)), 'EL': 2, 'RG': 'SS.VV.SS', 'VP': ('SS.S.V.VV', 'S.V.VV.VV'), 'XREC': 'VVSS', 'QC': 'S', 'PREP': 'GGGGVVVVVVSSSSSS', 'RC': 'SS', 'TURNS': 1, 'ONS': ('F32', 'al', 'c16', 'e16', 'e2c', 'eL', 'f0l', 'fa', 'par1', 'par2', 'udup', 'yo'), 'VS': 0, 'LOADS': 'Yw Sp Yk Sz0 Yr0 Yz1 Yx0 Ye Yr1 Yx1', 'ZP': ((0, 2), (2, 4), (4, 6)), 'PR': {'Zp': 500, 'cb': 200, 'v1': -500, 'Xrec': 2000, 'f0m': 1000, 'hh': -2000, 'k1': 1000, 'q': -2000, 'dup_z': 500, 'kn': 200},
+    'BC': ((0, 7), (7, 13), (13, 16)), 'RS': ((0, 2), (2, 4), (4, 6)), 'QC': 'V', 'ONS': ('F32', 'al', 'c16', 'e16', 'e2c', 'eL', 'f0l', 'fa', 'par2', 'udup', 'yo'), 'PR': {'Zp': 500, 'cb': 200, 'v1': -500, 'Xrec': 2000, 'f0m': -2000, 'hh': -2000, 'k1': 1000, 'q': -2000, 'dup_z': 500, 'kn': 200, 'Zg': -1000, 'kf': -2000, 'send_q': 1000, 'eL': -2000, 'qs': 2000, 'nnB': 2000, 'eq': 200},
+    'SLACK': 15, 'SC': ((0, 3), (3, 6)), 'RS': ((0, 2), (2, 6)), 'ONS': ('F32', 'al', 'c16', 'c16G', 'e16', 'e2c', 'eL', 'fa', 'par1', 'par2', 'udup', 'yo'), 'PR': {'Zp': 500, 'cb': 200, 'v1': -500, 'Xrec': 2000, 'f0m': 500, 'hh': -2000, 'k1': 1000, 'q': 1000, 'dup_z': 500, 'kn': 200, 'Zg': -500, 'kf': -2000, 'send_q': 1000, 'eL': -2000, 'qs': 2000, 'nnB': 2000, 'eq': 200, 'cT': 200, 's8': -500},
+    "XC": "", 'EL': 1, 'RC': 'VS', 'ONS': ('al', 'c16', 'e16', 'e2c', 'eL', 'fa', 'par1', 'par2', 'pc', 'udup'), 'VS': 0, 'LOADS': 'Yw Sp Yk Sz0 Yz1 Yr Yx0 Ye Yx1', 'PR': {'Zp': -500, 'cb': 200, 'v1': 500, 'Xrec': 2000, 'f0m': 500, 'hh': -2000, 'k1': 1000, 'q': 1000, 'dup_z': 500, 'kn': -200, 'Zg': -500, 'kf': -2000, 'send_q': 1000, 'eL': -2000, 'qs': 2000, 'nnB': 2000, 'eq': 200, 'cT': 200, 's8': -500, 'pc': -2000, 'F0': -500, 'ku': -500, 'e16': -200, 'keyc': -2000, 'Zabs': 200},
+    'BIAS': 4000, 'SLACK': 15, 'ZG': 'S.VV.SS.V', 'SC': ((0, 3), (3, 6)), 'V2': ((0, 96),), 'BC': ((0, 7), (7, 13), (13, 16)), 'RS': ((0, 2), (2, 6)), 'EL': 2, 'RG': 'SS.VV.SS', 'VP': ('SS.S.V.VV', 'S.V.VV.VV'), 'XREC': 'VVSS', 'PREP': 'GGGGVVVVVVSSSSSS', 'RC': 'SSSV', 'TURNS': 1, 'ONS': ('E16', 'F32', 'al', 'c16G', 'cl', 'e2c', 'f0l', 'fa', 'par1', 'par2', 'pc', 'udup'), 'VS': 0, 'LOADS': 'Yw Sp Yk Sz0 Yr Yz1 Yx0 Ye Yx1', 'ZP': ((0, 2), (2, 4), (4, 6)), 'PR': {'send_q': 1000, 'send_z': 500, 'ed': 1000, 'votes': -500, 'eu': 500, 'f0scan': -500, 'Xrec': -2000, 'F0': 2000, 'cb': -200, 'barred': 500, 'votesS': -500, 'e2L': 500, 'e2': 500},
 }
-EST = {"pe": 1.05, "fixed": {"V": 0.0, "S": 0.0, "P": 0.0, "G": 0.0}, "fac": 1.05, "gather": 1.5, "wake": 200.0, "dma": 1800.0, "send": 1200.0, "issue": 250.0, "rate": 300.0, "dissue": 500.0}
+EST = {"pe": 1.06, "fixed": {"V": 0.0, "S": 10.0, "P": 0.0, "G": 60.0}, "fac": 1.03, "gather": 1.5, "wake": 215.0, "dma": 1800.0, "send": 1200.0, "issue": 250.0, "rate": 240.0, "dissue": 400.0}
 DT = {"i": "int32", "u": "uint16", "f": "float32", "b": "bfloat16", "h": "float16"}
-ARENA = {"i": 4096, "u": 1024, "f": 6144, "b": 28672, "h": 4096}
+ARENA = {"i": 4096, "u": 2048, "f": 6144, "b": 32768, "h": 4096}
 SCRATCH = {"Cm": ("sbuf", [128, 2, 16, 32], "bfloat16")}
 for _s in "01":
     SCRATCH["X" + _s] = ("sbuf", [128, XW], "bfloat16")
@@ -41,8 +51,8 @@ for _k in ARENA:
 PS = tuple(x + s for s in "01" for x in ("d0", "d1", "ma", "mb"))
 for _n in PS:
     SCRATCH[_n] = ("psum", [128, 32, 16] if _n[:2] != "ma" else [128, 512], "float32")
-DSEM = ["ld_" + k + s for k in "pwzrxe" for s in "01"] + ["dup_%s%s%d" % (k, s, t) for k in "zr" for s in "01" for t in range(TT - 1)]
-ASEM = ["ar_%s%s%d" % (k, s, t) for k in "pfq" for s in "01" for t in range(TT)]
+DSEM = ["ld_" + k for k in "pwker"] + ["ld_" + k + s for k in "zx" for s in "01"] + ["dup_%s%s%d" % (k, s, t) for k in "zr" for s in "01" for t in range(TT - 1)]
+ASEM = ["ar_%s%s%d" % (k, s, t) for k in "pfqz" for s in "01" for t in range(TT)]
 SEMAPHORES = ["cV", "cS", "cP", "cG", "sent", "stored"] + DSEM + ASEM
 WHERE, TOP, MASKS = {}, {}, {}
 PART = {1: slice(0, 64), 2: slice(64, 128), 3: slice(0, 128)}
@@ -97,10 +107,12 @@ def build():
     WHERE.clear()
     TOP.clear()
     ops = []
-    cur = [""]
+    cur, seen = [""], {}
 
     def op(eng, cyc, w, r, fn, name="", kind="c", fix=0.0, gather=False, ni=1, by=0):
         ops.append({"e": eng, "cy": cyc, "fx": fix, "g": gather, "ni": ni, "by": by, "w": w, "r": r, "f": fn, "k": kind, "n": name + cur[0], "s": cur[0]})
+        seen[name] = seen.get(name, 0) + 1
+        ops[-1]["id"] = (name, cur[0], seen[name])
 
     def vcyc(xs):
         two = all(dtype(x[0]) in ("bfloat16", "float16", "uint16") for x in xs)
@@ -172,7 +184,9 @@ def build():
             vc(o, i, name)
 
     def aff(o, i, mul, add, name, eng=None):
-        if eng == "S" or name in CFG["ONS"]:
+        if name + "G" in CFG["ONS"]:
+            copy("G", o, i, name)
+        elif eng == "S" or name in CFG["ONS"]:
             act(o, i, F.Identity, bias=add, scale=mul, name=name)
         elif mul == 1 and add == 0:
             vc(o, i, name)
@@ -204,32 +218,30 @@ def build():
         op("R", 0, [], [src], (t, [(dst, src)], sem), "send_" + kind, kind="send", by=by)
         op("A", 0, [dst], [], sem, "arr_" + kind, kind="arr")
 
-    need("b", ones=256, w16=144, tmpa=144, BB=128, W=144, I=128, IK=128, BS=2048, smax=768, maskc=NL, half=NP_, c1536=NP_, c2048=NP_, IM=128, cs=1)
+    need("b", ones=256, w16=144, tmpa=144, BB=128, W=144, I=128, IK=128, BS=2048, smax=768, maskc=NL, half=NL, c1536=NL, c4096=NP_, cbig=NP_, eps=NP_, s2=NL, s4=4 * NP_, IM=128, IN=128, BS4=128, cpar=NL, NJ=NL, ramp=NL, cs=1)
     need("f", iom=NL, M16=16, smin=NL, N32=TT * NL, pcol=1, bar=TT, cb=2 * TT, tab=8)
     need("h", N16=TT * NL)
-    need("i", ci=8, cj=8)
+    need("i", ci=8, cj=8, wtn=1, kmn=1, exn=L, rtn=A0)
+    need("b", p0n=L)
     for s in "01":
-        need("i", **{x + s: w for x, w in (("ri", A0), ("exi", NL), ("wk", 4), ("q", NP_), ("r", NP_), ("hh", NP_), ("ks", NL), ("li", 6), ("yi", NL), ("e2", NL))})
-        need("u", **{x + s: w for x, w in (("cl", NP_), ("al", 6), ("el", NL), ("e2l", NL), ("lu", NP_), ("f0l", 6))})
-        need("f", **{x + s: w for x, w in (("cf", 8), ("v", NP_), ("ul", NL), ("uu", NP_), ("eu", NL), ("ed", NL), ("k2", NL), ("pc", NL), ("Fs", TT * L), ("Fl", TT * L), ("yo", NL))})
+        need("i", **{x + s: w for x, w in (("wk", 4), ("ki", 2), ("q", NP_), ("r", NP_), ("hh", NP_), ("h4", 4 * NP_), ("ks", NL), ("li", 6), ("yi", NL), ("e2", NL))})
+        need("u", **{x + s: w for x, w in (("cl", NP_), ("al", 6), ("el", NL), ("e2l", NL), ("lu", NP_), ("zs", TT * 16), ("zl", TT * 16))})
+        need("b", **{x + s: w for x, w in (("qs", TT * NL), ("lo", NL), ("hi", NL))})
+        need("f", **{x + s: w for x, w in (("cf", 8), ("v", NL), ("ul", NL), ("uu", 4 * NP_), ("fa", NP_), ("eu", NL), ("ed", NL), ("k2", NL), ("pc", NL), ("f0", NL), ("Fs", TT * NL), ("Fl", TT * NL), ("yo", NL))})
         need("h", **{x + s: w for x, w in (("Wm", 128), ("WH", 128), ("WL", 128), ("E16", NL), ("c16", 64), ("cT", 64), ("e16", NL), ("e2c", NL), ("F16", NL), ("f16", NL), ("p2", NL))})
-        need("b", **{x + s: w for x, w in (("p", TT * NL), ("pl", TT * NL), ("qs", TT * NP_), ("ql", TT * NP_), ("kb", NL), ("nt", NP_), ("prep", 16 * NL), ("gz", 768), ("g1", 16 * NL),
-                                          ("g2", 16 * NL), ("x1", 16 * NL), ("sg", NL), ("s8", NL), ("nn", NL), ("eq", 768), ("rs", 768))})
+        need("b", **{x + s: w for x, w in (("p", TT * NL), ("pl", TT * NL), ("kb", NL), ("nt", NP_), ("prep", 16 * NL), ("gz", 768), ("g1", 16 * NL),
+                                          ("g2", 16 * NL), ("x1", 32 * NL), ("sg", NL), ("s8", NL), ("nn", NL), ("eq", 768), ("rs", 768))})
     I, W = a("I", 0, 128), lambda k: a("W", 16 - k, 144 - k)
 
     for x in CFG["LOADS"].split():
-        q, k, s = {"Y": "Y", "S": "SD"}[x[0]], x[1], x[2]
-        r0 = 64 * int(s)
-        hbm = lambda nm, c0, c1, r0=r0: lambda T: T[nm][r0:r0 + 64, c0:c1] if c1 else T[nm][r0:r0 + 64, :]
-        if k in "pe":
-            nm, buf = {"p": ("p0", "p"), "e": ("ex", "exi")}[k]
-            prs = [(a(buf + s, 0, NL, h=1 + h), hbm(nm, NL * h, NL * h + NL)) for h in (0, 1)]
-        elif k == "w":
-            prs = [(a("wk" + s, c, c + 1, h=1 + h), hbm(nm, 0, 0)) for c, nm in enumerate(("wt", "km")) for h in (0, 1)]
+        q, k, s = {"Y": "Y", "S": "SD"}[x[0]], x[1], x[2:]
+        if not s:
+            nm, w = {"p": ("p0", L), "e": ("ex", L), "w": ("wt", 1), "k": ("km", 1), "r": ("rt", A0)}[k]
+            prs = [(a(nm + "n", 0, w), lambda T, nm=nm: T[nm][:, :])]
         else:
-            nm, buf, w = {"z": ("zp", "Z", A0), "r": ("rt", "ri", A0), "x": ("ax", "X", V)}[k]
-            prs = [(a(buf + s, 0, w, h=1 + h), hbm(nm, 0, 0)) for h in (0, 1)]
-        dma(q, prs, "ld_" + k + s, "ld_" + k + s, 128 * {"p": 192, "e": 384, "w": 8, "z": 2048, "r": 4096, "x": 8192}[k])
+            nm, buf, c0, c1 = {"z": ("zp", "Z", 0, A0), "x": ("ax", "X", XO, XV)}[k]
+            prs = [(a(buf + s, c0, c1, h=1 + h), lambda T, nm=nm, r0=64 * int(s): T[nm][r0:r0 + 64, :]) for h in (0, 1)]
+        dma(q, prs, "ld_" + k + s, "ld_" + k + s, (64 * len(prs) if s else 128) * {"p": 384, "e": 768, "w": 4, "k": 4, "z": 2048, "r": 4096, "x": 8192}[k])
         ops[-1]["chain"] = q
 
     vm(a("ones", 0, 256), 1.0)
@@ -237,9 +249,15 @@ def build():
     gsel(a("tmpa", 0, 128), a("ones", 0, 128), [[-16, 8], [0, 16]], A.is_ge, 0, 1)
     gsel(a("BB", 0, 128), a("tmpa", 0, 128), [[16, 8], [0, 16]], A.is_ge, 15, -1)
     gsel(I, a("ones", 0, 128), [[-1, 128]], A.is_equal, 0, 1)
-    vm(a("half", 0, NP_), -0.5)
-    vm(a("c1536", 0, NP_), -1536.0)
-    vm(a("c2048", 0, NP_), 2048.0)
+    vm(a("half", 0, NL), -0.5)
+    vm(a("c1536", 0, NL), -1536.0)
+    vm(a("c4096", 0, NP_), 4096.0)
+    vm(a("cbig", 0, NP_), 12582912.0)
+    vm(a("eps", 0, NP_), 2.0 ** -13)
+    for k, val in enumerate((0.0, -1.0)):
+        vm(a("s2", k, NL, 2), val)
+    for k, val in enumerate((0.0, 1.0 / 32, 1.0, 1.0)):
+        vm(a("s4", k, 4 * NP_, 4), val)
     if "S" in "".join(CFG["VP"]):
         act(a("tab", 0, 4), a("ones", 0, 4), F.Sigmoid, name="table")
     gsel(a("tmpa", 0, 144), a("w16", 0, 144), [[-16, 9], [-1000, 16]], A.is_ge, 16, 1)
@@ -250,14 +268,19 @@ def build():
             gsel(nd("Cm", gl, slice(0, 16), slice(16 * gl + h, 16 * gl + 16, 2)), a("ones", 0, 128), [[-8, 4], [-32, 4], [-1, 8]], A.is_equal, 0, 1)
     giota(a("iom", 0, NL), [[0, 6], [1, 16]], 0, 0)
     vs(a("smin", 0, NL), a("iom", 0, NL), 0.0, A.is_equal, 33554432.0, A.mult)
-    for nm, val in (("IK", 1327104.0), ("IM", 1048576.0)):
+    for nm, val in (("IK", 1327104.0), ("IM", 1048576.0), ("IN", -1.0)):
         vs(a(nm, 0, 128), I, val, A.mult)
     giota(a("cj", 0, 1), [[1, 1]], 0, 1)
     vs(a("ci", 0, 1), a("cj", 0, 1), 15, A.bitwise_and)
     vc(a("pcol", 0, 1), a("ci", 0, 1))
     vs(a("M16", 0, 16), a("iom", 0, 16), a("pcol", 0, 1), A.is_equal)
-    vs(a("maskc", 0, NL), a("iom", 0, NL), a("pcol", 0, 1), A.not_equal, 8192.0, A.mult)
-    vs(a("maskc", 0, NL), a("maskc", 0, NL), 2048.0, A.add)
+    giota(a("ramp", 0, NL), [[-16, 6], [0, 16]], 0, 0)
+    vs(a("maskc", 0, NL), a("iom", 0, NL), a("pcol", 0, 1), A.not_equal, 256.0, A.mult)
+    vt(a("ramp", 0, NL), a("ramp", 0, NL), a("maskc", 0, NL), A.add)
+    vs(a("maskc", 0, NL), a("ramp", 0, NL), 16384.0, A.mult)
+    vm(a("cpar", 0, NL, 2), 8192.0)
+    vm(a("cpar", 1, NL, 2), -8192.0)
+    vs(a("BS4", 0, 128), a("BB", 0, 128), a("M16", 0, 1), A.mult, -16384.0, A.mult)
     for k in range(16):
         vs(a("BS", 128 * k, 128 * k + 128), a("BB", 0, 128), a("M16", k, k + 1), A.mult, -1.0, A.mult)
     giota(a("N32", 0, TT * NL), [[96, TT], [1, NP_], [0, 2]], B0, 0)
@@ -267,23 +290,34 @@ def build():
     vm(a("bar", 0, 1), 57344.0)
     for s in "01":
         cf = lambda c: a("cf" + s, c, c + 1)
+        for h in (0, 1):
+            vc(a("wk" + s, 0, 1, h=1 + h), a("wtn", 0, 1, h=1 + int(s)))
+            vc(a("ki" + s, 0, 1, h=1 + h), a("kmn", 0, 1, h=1 + int(s)))
+            copy("S", a("p" + s, 0, NL, h=1 + h), a("p0n", NL * h, NL * h + NL, h=1 + int(s)), "p0")
+            aff(a("E16" + s, 0, NL, h=1 + h), a("exn", NL * h, NL * h + NL, h=1 + int(s)), 1.0, -2048.0, "E16")
         vs(cf(0), a("wk" + s, 0, 1), 2048.0, A.is_ge)
         vs(cf(1), a("wk" + s, 0, 1), 2.0 ** -12, A.mult, cf(0), A.subtract)
         vs(a("Wm" + s, 0, 128), a("BB", 0, 128), cf(1), A.mult)
-        vs(cf(2), a("wk" + s, 1, 2), 2048.0, A.is_ge, 2.0 ** 24, A.mult)
-        vs(cf(3), a("wk" + s, 1, 2), 4096.0, A.mult, cf(2), A.subtract)
-        vs(cf(4), cf(3), 0.5, A.mult)
+        vs(cf(2), a("ki" + s, 0, 1), 1920.0, A.is_ge, 2.0 ** 24, A.mult)
+        vs(cf(7), a("ki" + s, 0, 1), 128.0, A.add, 4096.0, A.mult)
+        vs(cf(3), cf(7), cf(2), A.subtract)
+        vs(a("ki" + s, 1, 2), a("ki" + s, 0, 1), 1, A.bitwise_and)
+        vs(cf(4), a("ki" + s, 1, 2), 2048.0, A.mult, -12582912.0, A.add)
+        vm(a("uu" + s, 1, 4 * NP_, 4), -0.375)
+        vm(a("uu" + s, 2, 4 * NP_, 4), 12582912.0)
         vs(a("wk" + s, 2, 3), a("wk" + s, 0, 1), 63, A.bitwise_and)
         vs(cf(5), a("wk" + s, 2, 3), -2.0 ** -13, A.mult)
         vs(cf(6), cf(1), -0.5, A.mult, cf(5), A.subtract)
         vs(a("WL" + s, 0, 128), a("BB", 0, 128), cf(5), A.mult)
         vs(a("WH" + s, 0, 128), a("BB", 0, 128), cf(6), A.mult)
         vm(a("c16" + s, NP_, 64), 0.0)
-        vm(a("X" + s, V, XW), 0.0)
-        vs(a("E16" + s, 0, NL), a("exi" + s, 0, NL), -2048.0, A.add)
+        vm(a("X" + s, XV, XW), 0.0)
         for x, e in enumerate(CFG["RC"]):
             w = A0 // len(CFG["RC"])
-            copy(e, a("R" + s, w * x, w * x + w), a("ri" + s, w * x, w * x + w), "R")
+            for h in (0, 1):
+                copy(e, a("R" + s, w * x, w * x + w, h=1 + h), a("rtn", w * x, w * x + w, h=1 + int(s)), "R")
+
+    vs(a("NJ", 0, NL), a("N32", 0, NL), -float(B0), A.add)
 
     def units(spec):
         out, x = [], 0
@@ -303,21 +337,28 @@ def build():
             bank[0] ^= 1
             return "d%d" % bank[0] + s
         send(t, "p", b("pl", NL * t, NL * t + NL), p())
-        ps, v = b("ma", 0, NP_), b("v", 0, NP_)
-        if t:
-            mm([(ps, b("Wm", 0, 128), a("c1536", 0, NP_)), (ps, I, a("half", 0, NP_))], "uc", stop=False)
-            mm([(ps, b("WH", 0, 128), lanes("p2", 2)), (ps, b("WL", 0, 128), lanes("p2", 2))], "u", start=False)
+        both, ps, pq = b("ma", 0, NL), b("ma", 1, NL, 2), b("ma", 0, NL, 2)
+        if CFG["QV"]:
+            v = lanes("v", 2, 1)
+            src = [(b("WH", 0, 128), lanes("p2", 2)), (b("WL", 0, 128), lanes("p2", 2))] if t else [(b("Wm", 0, 128), p(2))]
+            mm([(both, I, a("half", 0, NL)), (pq, I, a("eps", 0, NP_))] + [(both, b("Wm", 0, 128), a("c1536", 0, NL))] * (t > 0), "uc", stop=False)
+            mm([(o, w, r) for o in (pq, ps) for w, r in src] + [(pq, I, a("cbig", 0, NP_)), (pq, a("IN", 0, 128), a("cbig", 0, NP_))], "u", start=False)
+            scan(lanes("v"), a("s2", 0, NL), both, 0.0, A.mult, A.add, "v")
         else:
-            mm([(ps, I, a("half", 0, NP_)), (ps, b("Wm", 0, 128), p(2))], "u")
-        aff(b("q", 0, NP_), ps, 1.0, 2.0 ** -13, "q")
-        vt(v, ps, b("q", 0, NP_), A.subtract, "v")
-        act(b("uu", 0, NP_), v, F.Square, bias=2048.0, scale=4096.0, name="uu")
-        act(b("ma", 48, 96), v, F.Identity, bias=b("cf", 4, 5), scale=b("cf", 3, 4), name="ku")
+            v = b("v", 0, NP_)
+            if t:
+                mm([(ps, b("Wm", 0, 128), a("c1536", 0, NP_)), (ps, I, a("half", 0, NP_))], "uc", stop=False)
+                mm([(ps, b("WH", 0, 128), lanes("p2", 2)), (ps, b("WL", 0, 128), lanes("p2", 2))], "u", start=False)
+            else:
+                mm([(ps, I, a("half", 0, NP_)), (ps, b("Wm", 0, 128), p(2))], "u")
+            aff(b("q", 0, NP_), ps, 1.0, 2.0 ** -13, "q")
+            vt(v, ps, b("q", 0, NP_), A.subtract, "v")
+        act(b("uu", 0, 4 * NP_, 4), v, F.Square, scale=4096.0, name="uu")
+        act(b("uu", 3, 4 * NP_, 4), v, F.Identity, bias=b("cf", 4, 5), scale=b("cf", 3, 4), name="ku")
         for h in (0, 1):
             aff(lanes("ul", 2, h), v, 4096.0, 0.0, "udup")
-        aff(b("r", 0, NP_), b("uu", 0, NP_), 1.0 / 32, -0.375, "r")
-        vt(b("hh", 0, NP_), b("ma", 48, 96), b("r", 0, NP_), A.add, "hh")
-        vs(b("hh", 0, NP_), b("hh", 0, NP_), 4095, A.bitwise_and, name="hm")
+        scan(b("h4", 0, 4 * NP_), a("s4", 0, 4 * NP_), b("uu", 0, 4 * NP_), 0.0, A.mult, A.add, "hh")
+        vs(b("hh", 0, NP_), b("h4", 3, 4 * NP_, 4), 4095, A.bitwise_and, name="hm")
         aff(b("cl", 0, NP_), b("hh", 0, NP_), n / 4096.0, -0.5 + 2.0 ** -13, "cl")
         for k, e in enumerate(CFG["PREP"]):
             if e == "G" or t == 0:
@@ -329,39 +370,53 @@ def build():
         key = b("ma", 96, 192)
         mm([(key, I, a("iom0", 0, NL))] + [(b("ma", 96 + 16 * hi, 112 + 16 * hi), nd("Cm", gl, slice(hi % 4 * 4, hi % 4 * 4 + 4), slice(0, 32)), b("cT", 32 * (hi // 4) + 16 * gl, 32 * (hi // 4) + 16 * gl + 16))
                                           for hi in range(6) for gl in (0, 1)], "keyc", stop=False)
-        for x, d in enumerate(("d0", "d1", "mb")):
-            mm([(a(d + s, 0, 512), I, b("prep", 512 * x, 512 * x + 512))], "Zp", stop=False)
         for e, x0, x1 in units(CFG["ZG"]):
-            gneg(e, b("gz", 256 * x0, 256 * x1), b("Z", 0, n), b("cl", 16 * x0, 16 * x1), "Zg")
-        for x, d in enumerate(("d0", "d1", "mb")):
-            mm([(nd(d + s, slice(h, 32, 2), slice(0, 16)), I, b("gz", 256 * x, 256 * x + 256)) for h in (0, 1)], "Zsub", start=False)
-            act(nd("dz" + s, slice(2 * x, 2 * x + 2), slice(0, 16), slice(0, 16)), a(d + s, 0, 512), F.Abs, scale=0.25, name="Zabs")
+            gneg(e, b("gz", 128 * x0, 128 * x1), b("Z", 0, n), b("cl", 8 * x0, 8 * x1), "Zg")
+        for y, (x0, x1) in enumerate(CFG["ZP"]):
+            d, w = ("d0", "d1", "mb")[y % 3] + s, x1 - x0
+            if y < CFG["ZD"]:
+                pp = b("p", NL * t + 16 * x0, NL * t + 16 * x1)
+                mm([(a(d, 0, 256 * w), a("zero", 0, 128), a("BS", 0, 256 * w))] * CFG["ZZ"] + [(nd(d, slice(0, 16 * w), m), I, pp) for m in range(16)], "Zp", stop=False)
+            else:
+                mm([(a(d, 0, 256 * w), I, b("prep", 256 * x0, 256 * x1))], "Zp", stop=False)
+            mm([(nd(d, slice(h, 16 * w, 2), slice(0, 16)), I, b("gz", 128 * x0, 128 * x1)) for h in (0, 1)], "Zsub", start=False)
+            act(nd("dz" + s, slice(x0, x1), slice(0, 16), slice(0, 16)), a(d, 0, 256 * w), F.Abs, scale=0.25, name="Zabs")
         for h0, h1 in CFG["SC"]:
             mm([(b("ma", 96 + 16 * h0, 96 + 16 * h1), W(lo), nd("dz" + s, slice(h0, h1), lo, slice(0, 16))) for lo in range(16)], "score", start=False, stop=h1 == 6)
         scan(lanes("ks"), a("smin", 0, NL), key, 33554432.0, A.max, A.min, "kmin")
-        vs(b("li", 0, 6), lanes("ks", 16, 15), 4095, A.bitwise_and, name="lm")
-        aff(b("al", 0, 6), b("li", 0, 6), 1.0, 0.0, "al")
+        if CFG["BU"]:
+            vs(b("al", 0, 6), lanes("ks", 16, 15), 4095, A.bitwise_and, name="lm")
+        else:
+            vs(b("li", 0, 6), lanes("ks", 16, 15), 4095, A.bitwise_and, name="lm")
+            aff(b("al", 0, 6), b("li", 0, 6), 1.0, 0.0, "al")
         act(lanes("ed"), b("R", 0, n), F.Identity, scale=2080.0, bias=2464.0 * t - 4194304.0, off=b("al", 0, 6), name="ed")
-        act(lanes("e16"), b("R", 0, n), F.Identity, bias=-2048.0, off=b("al", 0, 6), name="e16")
+        if CFG["EL"] < 2:
+            act(lanes("e16"), b("R", 0, n), F.Identity, bias=-2048.0, off=b("al", 0, 6), name="e16")
         if CFG["EL"]:
             gv(lanes("el"), b("R", 0, n), b("al", 0, 6), "eL")
+        if CFG["EL"] == 2:
+            aff(lanes("e16"), lanes("el"), 1.0, -2048.0, "e16")
         gv(lanes("eu"), b("R", 0, n), b("al", 0, 6), "eu", lanes("ul"), A.mult)
         if not CFG["EL"]:
             aff(lanes("el"), lanes("e16"), 1.0, 2048.0, "eL")
         vt(lanes("yi"), lanes("eu"), lanes("ed"), A.add, "yi")
-        vs(lanes("e2"), lanes("yi"), 5, A.arith_shift_right, 4095, A.bitwise_and, name="e2")
-        aff(lanes("e2l"), lanes("e2"), 1.0, 0.0, "e2L")
+        vs(lanes("e2l" if CFG["BU"] else "e2"), lanes("yi"), 5, A.arith_shift_right, 4095, A.bitwise_and, name="e2")
+        if not CFG["BU"]:
+            aff(lanes("e2l"), lanes("e2"), 1.0, 0.0, "e2L")
         aff(lanes("e2c"), lanes("e2l"), 1.0, -2048.0, "e2c")
         v1, k3, v2 = b("ma", 192, 288), b("ma", 288, 384), b("mb", 96, 192)
         for w, (lst, gb) in enumerate((("el", "g1"), ("e2l", "g2"))):
             for e, x0, x1 in units(CFG["VP"][w]):
                 c0, c1 = 256 * x0, 256 * x1
                 if e == "V":
-                    gv(b(gb, c0, c1), b("X", 0, V), b(lst, 16 * x0, 16 * x1), "votes", b("prep", c0, c1), A.is_ge)
+                    gv(b(gb, c0, c1), b("X", XO, XV), b(lst, 16 * x0, 16 * x1), "votes", b("prep", c0, c1), A.is_ge)
                 else:
-                    act(b("x1", c0, c1), b("X", 0, V), F.Identity, scale=-1.0, off=b(lst, 16 * x0, 16 * x1), name="votesS")
+                    xs = b("x1", 1536 * w + c0, 1536 * w + c1)
+                    act(xs, b("X", XO, XV), F.Identity, scale=-1.0, off=b(lst, 16 * x0, 16 * x1), name="votesS")
                     d = a(dbank(), 0, c1 - c0)
-                    mm([(d, I, b("prep", c0, c1)), (d, I, b("x1", c0, c1))], "vsub")
+                    if CFG["VS"]:
+                        mm([(d, I, b("prep", c0, c1))], "vp", stop=False)
+                    mm([(d, I, b("prep", c0, c1))] * (1 - CFG["VS"]) + [(d, I, xs)], "vsub", start=not CFG["VS"])
                     act(b(gb, c0, c1), d, F.Sigmoid, bias=128.0, scale=-256.0, name="vsig")
             if w == 0:
                 mm([(v1, I, lanes("e16"))] + [(v1, W(k), b(gb, k, 16 * NL, 16)) for k in range(16)], "v1")
@@ -384,58 +439,69 @@ def build():
         vt(lanes("kb"), v2, lanes("k2"), A.max, "m2")
         vt(b("mb", 0, NL), v2, lanes("k2"), A.max, "m2")
         vt(lanes("f16"), b("mb", 0, NL), lanes("kb"), A.subtract, "f16")
-        ca, cb, lu, fn_ = b("ma", 384, 432), b("mb", 192, 240), b("ma", 432, 480), b("mb", 336, 432)
+        ca, cb, fn_ = b("mb", 240, 288), b("mb", 192, 240), b("mb", 336, 432)
         for k0, k1 in CFG["BC"]:
             d = dbank()
             mm([[(a(d, 48 * k, 48 * k + 48), a("BS", 128 * (k0 + k), 128 * (k0 + k) + 128), lanes("f16", 2, 1)), (a(d, 48 * k, 48 * k + 48), I, lanes("f16", 2))] for k in range(k1 - k0)], "bcast")
-            vs(b("eq", 48 * k0, 48 * k1), a(d, 0, 48 * (k1 - k0)), 0.0, A.is_equal, name="eq")
-        mm([(lu, I, lanes("f16", 2)), (lu, I, a("c2048", 0, NP_))], "fa")
+            vs(b("eq", 48 * k0, 48 * k1), a(d, 0, 48 * (k1 - k0)), 0.0, A.is_equal, 16384.0, A.mult, name="eq")
+        kf, kn = b("ma", 192, 288), b("ma", 384, 480)
+        ends = [("lo", B0 + 96 * t, -1.0), ("hi", B0 + 96 * t + 96, 1.0)][:2 - t // 3]
+        for nm, c0, sg in ends:
+            vs(lanes(nm), lanes("f16"), c0 - 2048.0, A.is_ge, sg * (B0 + 192 * t + 96), A.mult, name="ends")
+        mm([(kf, I, a("maskc", 0, NL))] + [(kf, a("BS", 0, 128), lanes(nm)) for nm in ["f16"] + [x[0] for x in ends]], "kf")
+        act(lanes("f0"), kf, F.Identity, scale=-1.0, bias=2048.0 + 96 * t + 96, name="kf")
+        mm([(kn, a("IN", 0, 128), a("maskc", 0, NL)), (kn, I, a("cpar", 0, NL)), (kn, I, a("NJ", 0, NL)),
+            (b("ma", 385, 480, 2), a("BB", 0, 128), b("eq", 0, NP_))], "kn", stop=False)
+        aff(b("fa", 0, NP_), lanes("f16", 2), 1.0, 2048.0, "fa")
         for k0, k1 in CFG["BC"]:
-            mm([(ca, I, b("eq", 48 * k, 48 * k + 48)) for k in range(k0, k1)], "ca", start=k0 == 0, stop=k1 == 16)
-        vs(b("nt", 0, NP_), ca, 0.0, A.is_equal, 4096.0, A.mult, name="nt")
-        vt(b("lu", 0, NP_), lu, b("nt", 0, NP_), A.max, "lu")
-        aff(lanes("nn", 2), b("nt", 0, NP_), 2.0 ** -12, 0.0, "nn")
+            mm([(ca, I, a("c4096", 0, NP_))] * (k0 == 0) + [(ca, a("IN", 0, 128), b("eq", 48 * k, 48 * k + 48)) for k in range(k0, k1)], "ca", start=k0 == 0, stop=k1 == 16)
+        vt(b("lu", 0, NP_), ca, b("fa", 0, NP_), A.max, "lu")
+        act(lanes("nn", 2), ca, F.Relu, scale=2.0 ** -12, name="nn")
+        mm([(b("ma", 384, 480, 2), a("BS4", 0, 128), lanes("nn", 2))], "F0", start=False)
+        scan(lanes("yi"), kn, lanes("f0"), -1.0, A.max, A.max, "f0scan")
+        vs(b("li", 0, 6), lanes("yi", 16, 15), 8191, A.bitwise_and, name="f0m")
+        aff(b("zs", 16 * t, 16 * t + 6), b("li", 0, 6), 1.0, 0.0, "f0l")
+        send(t, "z", b("zl", 16 * t, 16 * t + 6), b("zs", 16 * t, 16 * t + 6))
         mm([[(cb, W(k), b("eq", 48 * k, 48 * k + 48)) for k in range(16)], [(fn_, I, lanes("f16")), (fn_, I, a("N16", NL * t, NL * t + NL))]], "cb")
         act(lanes("nn", 2, 1), cb, F.Relu, bias=1.0, scale=-1.0, name="nnB")
         for e, x0, x1 in units(CFG["RG"]):
             if e == "V":
-                gv(b("gz", 256 * x0, 256 * x1), b("X", 0, XW), b("lu", 16 * x0, 16 * x1), "rg")
+                gv(b("gz", 128 * x0, 128 * x1), b("X", XO, XW), b("lu", 8 * x0, 8 * x1), "rg")
             else:
-                act(b("gz", 256 * x0, 256 * x1), b("X", 0, XW), F.Identity, off=b("lu", 16 * x0, 16 * x1), name="rg")
-        Fs = b("Fs", L * t, L * t + NL)
+                act(b("gz", 128 * x0, 128 * x1), b("X", XO, XW), F.Identity, off=b("lu", 8 * x0, 8 * x1), name="rg")
+        Fs = b("Fs", NL * t, NL * t + NL)
         vt(fn_, fn_, lanes("nn"), A.mult, "delta")
         vt(lanes("F16"), fn_, a("N16", NL * t, NL * t + NL), A.subtract, "F")
         aff(Fs, lanes("F16"), 1.0, 2048.0, "F32")
-        f0 = b("ma", 0, NL)
-        mm([(f0, I, a("maskc", 0, NL)), (f0, a("BS", 0, 128), lanes("F16"))], "F0")
-        scan(b("Fs", L * t + NL, L * t + L), a("smin", 0, NL), f0, 33554432.0, A.max, A.min, "f0scan")
-        send(t, "f", b("Fl", L * t, L * t + L), b("Fs", L * t, L * t + L))
+        send(t, "f", b("Fl", NL * t, NL * t + NL), Fs)
         for x0, x1 in CFG["RS"]:
-            scan(b("rs", 256 * x0, 256 * x1), a("smax", 0, 256 * (x1 - x0)), b("gz", 256 * x0, 256 * x1), 0.0, A.min, A.max, "rscan")
-        copy(CFG["QC"], b("qs", NP_ * t, NP_ * t + NP_), b("rs", 15, 768, 16), "qs")
-        send(t, "q", b("ql", NP_ * t, NP_ * t + NP_), b("qs", NP_ * t, NP_ * t + NP_))
+            scan(b("rs", 128 * x0, 128 * x1), a("smax", 0, 128 * (x1 - x0)), b("gz", 128 * x0, 128 * x1), 0.0, A.min, A.max, "rscan")
+        for x, e in enumerate(CFG["XREC"]):
+            c0 = NL * t + NP_ * (x % 2)
+            copy(e, a("qs" + s, c0, c0 + NP_, h=1 + x // 2), a("rs" + s, 15, 768, 16, h=1 + x % 2), "qs")
+        land = XO - 96 * t - 96
+        send(t, "q", b("X", land, land + 96), b("qs", NL * t, NL * t + NL))
         if t < TT - 1:
-            for k, tab, src, c0, by in (("z", "Z", "pl", NL * t, 2), ("r", "R", "Fl", L * t, 4)):
+            for k, tab, src, c0, by in (("z", "Z", "pl", NL * t, 2), ("r", "R", "Fl", NL * t, 4)):
                 dma("Y", [(a(tab + s, n + NL * h, n + NL * h + NL, h=1 + h2), a(src + s, c0, c0 + NL, h=1 + h)) for h in (0, 1) for h2 in (0, 1)], "dup_%s%s%d" % (k, s, t), "dup_" + k, 256 * NL * by)
         r0 = 64 * int(s)
-        dma("Y", [(lambda T, h=h: T["yr"][r0:r0 + 64, L * t + NL * h:L * t + NL * h + NL], a("Fl" + s, L * t, L * t + NL, h=1 + h)) for h in (0, 1)], None, "yr", 128 * NL * 4)
-        aff(b("f0l", 0, 6), b("Fl", L * t + NL + 15, L * t + L, 16), -1.0, 4096.0, "f0l")
-        for x, e in enumerate(CFG["XREC"]):
-            c0 = B0 + 96 * t + NP_ * (x % 2)
-            copy(e, a("X" + s, c0, c0 + NP_, h=1 + x // 2), a("ql" + s, NP_ * t, NP_ * t + NP_, h=1 + x % 2), "Xrec")
+        dma("Y", [(lambda T, h=h: T["yr"][r0:r0 + 64, L * t + NL * h:L * t + NL * h + NL], a("Fl" + s, NL * t, NL * t + NL, h=1 + h)) for h in (0, 1)], None, "yr", 128 * NL * 4)
         aff(lanes("pc"), b("pl", NL * t, NL * t + NL), 1.0, 3326.5, "pc")
-        gv(lanes("p2"), b("X", 0, V), b("f0l", 0, 6), "newp", lanes("pc"), A.subtract)
+        gv(lanes("p2"), b("X", land, XV), b("zl", 16 * t, 16 * t + 6), "newp", lanes("pc"), A.subtract)
         if t < TT - 1:
+            aff(b("X", XO + B0 + 96 * t, XO + B0 + 96 * t + 96), b("X", land, land + 96), 1.0, 0.0, "Xrec")
             aff(b("p", NL * t + NL, NL * t + 2 * NL), lanes("p2"), -0.5, -1536.0, "p")
         else:
             aff(lanes("yo"), lanes("p2"), -0.5, -1536.0, "yo")
-            dma("Y", [(lambda T, h=h: T["yp"][r0:r0 + 64, NL * h:NL * h + NL], a("yo" + s, 0, NL, h=1 + h)) for h in (0, 1)], None, "yp", 128 * NL * 4)
+            for h, q in enumerate(("Y", "SD")):
+                dma(q, [(lambda T, h=h: T["yp"][r0:r0 + 64, NL * h:NL * h + NL], a("yo" + s, 0, NL, h=1 + h))], None, "yp", 64 * NL * 4)
 
     need("b", iom0=NL)
     vm(a("iom0", 0, NL), 0.0)
     for t in range(TT):
         for s in "01":
             cur[0] = s
+            seen.clear()
             round_(t, s)
     return ops
 
@@ -468,6 +534,15 @@ def deps_of(ops):
         raw.discard(i)
         war.discard(i)
         o["raw"], o["war"] = raw, war - raw
+    above = []
+    for i, o in enumerate(ops):
+        pre = [(j, no_wait(ops[j], o, j)) for j in o["raw"] | o["war"] | ({i - 1} if o["k"] == "arr" else set())]
+        implied = whole = 0
+        for j, free in pre:
+            whole |= above[j] | 1 << j
+            implied |= 0 if free else above[j]
+        above.append(whole)
+        o["pre"] = [(j, free) for j, free in pre if ops[j]["k"] != "c" or not implied >> j & 1]
 
 
 def no_wait(p, o, j):
@@ -480,18 +555,17 @@ def schedule(ops):
     succ = [[] for _ in range(n)]
     wake = EST["wake"]
     for i, o in enumerate(ops):
-        o["all"] = o["raw"] | o["war"] | ({i - 1} if o["k"] == "arr" else set())
-        for j in o["all"]:
-            succ[j].append(i)
+        for j, free in o["pre"]:
+            succ[j].append((i, free, 0.0 if o["k"] == "arr" else wake))
     cost = [{"send": EST["issue"], "dma": EST["dissue"] * o["ni"], "arr": 0.0}.get(o["k"], (o["cy"] * 0.83 * (EST["gather"] if o["g"] else 1) + o["fx"]) * EST["fac"] * (EST["pe"] if o["e"] == "P" else 1) + EST["fixed"][o["e"]] * o["ni"] if o["k"] == "c" else 0.0) for o in ops]
     lat = [{"dma": EST["dma"], "send": EST["send"]}.get(o["k"], 0.0) + o["by"] / EST["rate"] for o in ops]
     queue = [ONQ.get(o["e"], o["e"]) for o in ops]
     prio = [0.0] * n
     for i in range(n - 1, -1, -1):
         tail = CFG["BIAS"] if ops[i]["s"] == "0" else 0.0
-        prio[i] = max([tail + cost[i] + lat[i]] + [prio[j] + (cost[i] if no_wait(ops[i], ops[j], i) else cost[i] + lat[i] + (0.0 if ops[j]["k"] == "arr" else wake)) for j in succ[i]])
+        prio[i] = max([tail + cost[i] + lat[i]] + [prio[j] + cost[i] + (0.0 if fr else lat[i] + w) for j, fr, w in succ[i]])
     prio = [prio[i] + CFG["PR"].get(o["n"][:-1], 0.0) for i, o in enumerate(ops)]
-    nd_ = [len(o["all"]) for o in ops]
+    nd_ = [len(o["pre"]) for o in ops]
     ready = [0.0] * n
     free = {q: 0.0 for q in "VSPGYA"}
     avail = {q: [] for q in "VSPGYA"}
@@ -517,16 +591,18 @@ def schedule(ops):
             fin[i] = pipe + EST["dma"]
         if q != "A":
             free[q] = st + cost[i]
-        for j in succ[i]:
-            ready[j] = max(ready[j], st if no_wait(ops[i], ops[j], i) else fin[i] + (0.0 if ops[j]["k"] == "arr" else wake))
+        for j, fr, w in succ[i]:
+            ready[j] = max(ready[j], st if fr else fin[i] + w)
             nd_[j] -= 1
             if nd_[j] == 0:
                 avail[queue[j]].append(j)
         start[i] = st
     lat = [fin[i] - start[i] - cost[i] for i in range(n)]
-    lag = lambda i, j: cost[i] + (0.0 if no_wait(ops[i], ops[j], i) else lat[i] + (0.0 if ops[j]["k"] == "arr" else wake))
-    fwd = [[(i, lag(i, j)) for i in ops[j]["all"]] for j in range(n)]
-    bwd = [[(j, cost[j] + lag(i, j) - cost[i]) for j in succ[i]] for i in range(n)]
+    bwd = [[(j, cost[j] + (0.0 if fr else lat[i] + w)) for j, fr, w in succ[i]] for i in range(n)]
+    fwd = [[] for _ in range(n)]
+    for i in range(n):
+        for j, d in bwd[i]:
+            fwd[j].append((i, d - cost[j] + cost[i]))
 
     def place(seq, pred, first):
         at, used = [0.0] * n, {q: [] for q in free}
@@ -549,6 +625,21 @@ def schedule(ops):
         start = place(sorted(range(n), key=lambda i: (-back[i] - cost[i], i)), fwd, [0.0] * n)
         if span(start) < span(best):
             best = start
+    rng, end = np.random.default_rng(CFG["SEED"]), span(best)
+    kinds = {}
+    kind = np.array([kinds.setdefault(o["id"], len(kinds)) for o in ops])
+    for _ in range(CFG["SHAKES"]):
+        shift = np.zeros(len(kinds))
+        for x in rng.integers(0, n, rng.integers(1, 4)):
+            shift[kind[x]] = rng.choice((-1.0, 1.0)) * rng.choice((100.0, 300.0, 700.0, 1500.0))
+        key = list(np.array(best) + shift[kind])
+        for j in range(n):
+            for i, d in fwd[j]:
+                if key[j] <= key[i]:
+                    key[j] = key[i] + 1e-3
+        start = place(sorted(range(n), key=lambda i: key[i]), fwd, [0.0] * n)
+        if span(start) + CFG["LAM"] * sum(start) / n <= end + CFG["LAM"] * sum(best) / n + CFG["TEMP"] * rng.random() * (1 - _ / CFG["SHAKES"]):
+            best, end = start, span(start)
     return sorted(range(n), key=lambda i: (best[i], i)), span(best)
 
 

import numpy as np
from concourse.mybir import dt, AluOpType as A, ActivationFunctionType as F

V, L, A0, TT = 4096, 192, 1024, 4
NL, NP_ = 96, 48
B0 = V - TT * 96
XO = TT * 96
XV, XW = XO + V, XO + V + 16
RW = A0 + (TT - 1) * L
CFG = {
    "PREP": "GGGGGGGVVVVVSSSS",
    "ZG": "V.S.V",
    "SC": ((0, 6),), "V2": ((0, 96),), "BC": ((0, 8), (8, 16)), "RS": ((0, 3),), "EL": 1,
    "VP": ("VV.VV.SS", "VV.VV.SS"),
    "RG": "SS.S",
    "XREC": "V", "QC": "S", "PC": "V", "RC": "GG",
    "BIAS": 6000.0, "SLACK": 15.0, "PR": {},
    'BIAS': 4000, 'SLACK': 100, 'ZG': 'S.V.S', 'SC': ((0, 4), (4, 6)), 'V2': ((0, 96),), 'BC': ((0, 10), (10, 16)), 'RS': ((0, 2), (2, 3)), 'EL': 0, 'RG': 'SS.V', 'VP': ('V.V.VV.SS', 'VV.V.V.SS'), 'XREC': 'V', 'QC': 'S', 'PC': 'V', 'PREP': 'GGGGGVVVVVVSSSSS',
    "LOADS": "Yp0 Sw0 Yz0 Sp1 Sw1 Yr0 Yx0 Ye0 Yz1 Yr1 Ye1 Yx1",
    'BIAS': 4000, 'SLACK': 15, 'ZG': 'S.V.S', 'SC': ((0, 4), (4, 6)), 'V2': ((0, 96),), 'BC': ((0, 6), (6, 12), (12, 16)), 'RS': ((0, 2), (2, 3)), 'EL': 1, 'RG': 'SS.V', 'VP': ('V.V.VV.SS', 'V.V.V.V.S.S'), 'XREC': 'V', 'QC': 'S', 'PC': 'V', 'PREP': 'GGGGGVVVVVVSSSSS', 'RC': 'VS',
    'PR': {'hh': -200, 'kmin': 2000, 'qs': 1000, 'send_p': 200, 'v2': -2000, 'F': -200, 'vsig': 200, 'f16': 500, 'f0scan': 200, 'e2c': 1000, 'F0': -2000, 'q': 2000, 'cb': -2000, 'vsub': -1000, 's8': -1000, 'eq': -200},
    'BIAS': 4000, 'SLACK': 15, 'ZG': 'S.V.S', 'SC': ((0, 6),), 'V2': ((0, 96),), 'BC': ((0, 6), (6, 12), (12, 16)), 'RS': ((0, 2), (2, 3)), 'EL': 1, 'RG': 'SS.V', 'VP': ('VV.V.V.SS', 'S.V.VV.VV'), 'XREC': 'S', 'QC': 'S', 'PC': 'V', 'PREP': 'GGGGGVVVVVVSSSSS', 'RC': 'GG', 'PR': {'hh': -200, 'kmin': 2000, 'qs': 1000, 'send_p': 200, 'v2': -2000, 'F': -200, 'vsig': 200, 'f16': 500, 'f0scan': 2000, 'e2c': -2000, 'F0': -2000, 'q': 2000, 'cb': -2000, 'vsub': -1000, 's8': -1000, 'eq': -200, 'lu': -500, 'barred': -2000, 'ca': -2000, 'Zsub': 500, 'votes': -1000, 'k3': 500},
    "TURNS": 6,
    'BIAS': 4000, 'SLACK': 15, 'ZG': 'SS.S', 'SC': ((0, 6),), 'V2': ((0, 96),), 'BC': ((0, 4), (4, 10), (10, 16)), 'RS': ((0, 1), (1, 3)), 'EL': 0, 'RG': 'S.V.S', 'VP': ('V.V.V.V.S.S', 'VVV.VV.S'), 'XREC': 'S', 'QC': 'V', 'PC': 'S', 'PREP': 'GGGGGGVVSSSSSSSS', 'RC': 'SG', 'ONS': ('F32', 'al', 'e2L', 'e2c', 'f0l', 'f16', 'par1', 'par2'), 'PR': {},
    "TURNS": 1,
    'BIAS': 4000, 'SLACK': 15, 'ZG': 'SS.S', 'SC': ((0, 4), (4, 6)), 'V2': ((0, 96),), 'BC': ((0, 6), (6, 12), (12, 16)), 'RS': ((0, 1), (1, 3)), 'EL': 0, 'RG': 'S.V.S', 'VP': ('V.V.V.V.S.S', 'VVV.VV.S'), 'XREC': 'S', 'QC': 'V', 'PC': 'S', 'PREP': 'GGGGVVVVVVSSSSSS', 'RC': 'SG', 'ONS': ('F32', 'e2L', 'e2c', 'f16', 'li', 'par1', 'par2', 'q'), 'PR': {'ku': 500, 'Xrec': -500, 'e2': 500, 'Zp': -500, 'delta': -2000, 'cl': -500, 'vsub': 500, 'eq': 200, 'q': -500, 'k3': 1000, 'v2': -2000, 'k1': -2000, 'cb': -2000, 'yo': -1000, 'rscan': -500, 'rg': -1000, 'eL': -1000, 'score': -2000},
    'BIAS': 4000, 'SLACK': 100, 'ZG': 'SSS', 'SC': ((0, 4), (4, 6)), 'V2': ((0, 96),), 'BC': ((0, 6), (6, 12), (12, 16)), 'RS': ((0, 1), (1, 3)), 'EL': 0, 'RG': 'S.SS', 'VP': ('VV.VV.SS', 'VV.V.V.SS'), 'XREC': 'V', 'QC': 'V', 'PC': 'V', 'PREP': 'GGGGVVVVVVVVVVVV', 'RC': 'SG', 'ONS': ('F32', 'e2c', 'par2'), 'PR': {'e2c': 500, 'f16': -200, 'yi': 200, 'u': -1000, 'dup_r': 1000, 'y': -500, 'vsub': 200, 'cT': -1000, 'eu': -2000, 'f0l': 1000, 'q': 2000, 'v1': 200, 'rg': -2000, 'e16': -1000},
    'BIAS': 4000, 'SLACK': 100, 'ZG': 'V.S.V', 'SC': ((0, 4), (4, 6)), 'V2': ((0, 96),), 'BC': ((0, 8), (8, 16)), 'RS': ((0, 1), (1, 2), (2, 3)), 'EL': 1, 'RG': 'SS.V', 'VP': ('SS.VV.VV', 'SS.VV.VV'), 'XREC': 'V', 'QC': 'S', 'PC': 'V', 'PREP': 'GGGVVVVVVVSSSSSS', 'RC': 'SG', 'ONS': ('F32', 'c16', 'par2'), 'TURNS': 1, 'PR': {'cb': -500, 'Zabs': -500, 'v2': -2000, 'u': 2000, 'yo': -500, 'lu': -2000, 'li': -200, 'votesS': -2000, 'score': -500, 'rscan': 500},
    'BIAS': 4000, 'SLACK': 100, 'ZG': 'V.S.V', 'SC': ((0, 4), (4, 6)), 'V2': ((0, 96),), 'BC': ((0, 8), (8, 16)), 'RS': ((0, 1), (1, 3)), 'EL': 1, 'RG': 'S.V.S', 'VP': ('SS.VV.VV', 'SS.VV.VV'), 'XREC': 'VVVS', 'QC': 'S', 'PREP': 'GGGVVVVVVVSSSSSS', 'RC': 'GGGG', 'TURNS': 1, 'ONS': ('F32', 'c16', 'cl', 'e2c', 'p', 'par1', 'par2', 'pc'), 'PR': {'m13': 2000, 'ca': 200, 'k3': 2000, 'e2L': -2000, 'f0l': -500, 'par': -500, 'votesS': -1000, 'hh': 500, 'qs': -200, 'rg': -2000, 'c16': 500, 'uu': 2000, 'fa': 500, 'votes': -2000, 'nnB': -500},
    "QV": 0, "ZD": 0, "ZZ": 0, "VS": 1, "XREC": "VSVS", "ONS": ('F32', 'c16', 'e2c', 'nn', 'par2'), "LAM": 1.0, "TEMP": 0.0, "SHAKES": 0, "SEED": 0, "BU": 0, "LOADS": "Yp0 Sw0 Yk0 Sz0 Yr0 Yx0 Yp1 Yw1 Yk1 Yz1 Ye0 Yr1 Yx1 Ye1",
    'BIAS': 4000, 'SLACK': 50, 'ZG': 'V.S.V', 'SC': ((0, 4), (4, 6)), 'V2': ((0, 96),), 'BC': ((0, 3), (3, 10), (10, 16)), 'RS': ((0, 1), (1, 3)), 'EL': 1, 'RG': 'S.V.S', 'VP': ('SS.S.V.VV', 'S.V.VV.VV'), 'XREC': 'VVVV', 'QC': 'S', 'PREP': 'GGGGVVVVVVVVVVVV', 'RC': 'GG', 'TURNS': 1, 'ONS': ('F32', 'c16', 'cl', 'eL', 'p', 'par2', 'pc', 'r', 'udup', 'yo'), 'VS': 1, 'LOADS': 'Yp0 Sw0 Yz0 Sk0 Yr0 Sw1 Yx0 Yp1 Yk1 Yz1 Yr1 Ye0 Yx1 Ye1', 'PR': {'eL': 2000, 'par1': 2000, 'barred': 1000, 'k3': 1000, 'Xrec': -500},
    'BIAS': 4000, 'SLACK': 50, 'ZG': 'V.S.V', 'SC': ((0, 4), (4, 6)), 'V2': ((0, 96),), 'BC': ((0, 3), (3, 10), (10, 16)), 'RS': ((0, 1), (1, 3)), 'EL': 2, 'RG': 'S.V.S', 'VP': ('SS.S.V.VV', 'S.V.VV.VV'), 'XREC': 'VVVV', 'QC': 'S', 'PREP': 'GGGGVVVVVVVVVVVV', 'RC': 'GS', 'TURNS': 1, 'ONS': ('F32', 'c16', 'eL', 'nn', 'p', 'par1', 'par2', 'pc', 'r', 'udup', 'yo'), 'VS': 1, 'LOADS': 'Yw Sp Yk Sz0 Yr0 Yz1 Yx0 Ye Yr1 Yx1', 'PR': {'eL': 2000, 'par1': 2000, 'barred': 1000, 'k3': 1000, 'Xrec': -500, 'qs': 500, 'yp': 500, 'vp': 2000, 'ku': -500, 'v': -2000, 'eu': 1000},
    'BIAS': 4000, 'SLACK': 50, 'ZG': 'VV.SS.VV', "ZP": ((0, 2), (2, 4), (4, 6)), 'SC': ((0, 4), (4, 6)), 'V2': ((0, 96),), 'BC': ((0, 10), (10, 16)), 'RS': ((0, 2), (2, 6)), 'EL': 2, 'RG': 'SS.VV.SS', 'VP': ('SS.S.V.VV', 'S.V.VV.VV'), 'XREC': 'VSVS', 'QC': 'S', 'PREP': 'GGGGVVVVSSSSSSSS', 'RC': 'GS', 'TURNS': 1, 'ONS': ('F32', 'al', 'c16', 'e16', 'e2c', 'eL', 'f0l', 'par1', 'par2', 'pc', 'udup', 'yo'), 'VS': 1, 'LOADS': 'Yw Sp Yk Sz0 Yr0 Yz1 Yx0 Ye Yr1 Yx1', 'PR': {'eL': 2000, 'par1': 2000, 'barred': 1000, 'k3': 1000, 'Xrec': -500, 'qs': 500, 'yp': 500, 'vp': 2000, 'ku': 200, 'v': -2000, 'eu': 1000, 'kf': 200, 'votes': -200, 'v2': -2000, 'nt': 1000, 'kmin': -200},
    'BIAS': 4000, 'SLACK': 50, 'ZG': 'VV.VV.SS', 'SC': ((0, 4), (4, 6)), 'V2': ((0, 96),), 'BC': ((0, 10), (10, 16)), 'RS': ((0, 2), (2, 6)), 'EL': 2, 'RG': 'SS.VV.SS', 'VP': ('SS.S.V.VV', 'S.V.VV.VV'), 'XREC': 'VVSS', 'QC': 'S', 'PREP': 'GGGGVVVVVVSSSSSS', 'RC': 'SS', 'TURNS': 1, 'ONS': ('F32', 'al', 'c16', 'e16', 'e2c', 'eL', 'f0l', 'fa', 'par1', 'par2', 'udup', 'yo'), 'VS': 0, 'LOADS': 'Yw Sp Yk Sz0 Yr0 Yz1 Yx0 Ye Yr1 Yx1', 'ZP': ((0, 2), (2, 4), (4, 6)), 'PR': {'Zp': 500, 'cb': 200, 'v1': -500, 'Xrec': 2000, 'f0m': 1000, 'hh': -2000, 'k1': 1000, 'q': -2000, 'dup_z': 500, 'kn': 200},
    'BC': ((0, 7), (7, 13), (13, 16)), 'RS': ((0, 2), (2, 4), (4, 6)), 'QC': 'V', 'ONS': ('F32', 'al', 'c16', 'e16', 'e2c', 'eL', 'f0l', 'fa', 'par2', 'udup', 'yo'), 'PR': {'Zp': 500, 'cb': 200, 'v1': -500, 'Xrec': 2000, 'f0m': -2000, 'hh': -2000, 'k1': 1000, 'q': -2000, 'dup_z': 500, 'kn': 200, 'Zg': -1000, 'kf': -2000, 'send_q': 1000, 'eL': -2000, 'qs': 2000, 'nnB': 2000, 'eq': 200},
    'SLACK': 15, 'SC': ((0, 3), (3, 6)), 'RS': ((0, 2), (2, 6)), 'ONS': ('F32', 'al', 'c16', 'c16G', 'e16', 'e2c', 'eL', 'fa', 'par1', 'par2', 'udup', 'yo'), 'PR': {'Zp': 500, 'cb': 200, 'v1': -500, 'Xrec': 2000, 'f0m': 500, 'hh': -2000, 'k1': 1000, 'q': 1000, 'dup_z': 500, 'kn': 200, 'Zg': -500, 'kf': -2000, 'send_q': 1000, 'eL': -2000, 'qs': 2000, 'nnB': 2000, 'eq': 200, 'cT': 200, 's8': -500},
    "XC": "", 'EL': 1, 'RC': 'VS', 'ONS': ('al', 'c16', 'e16', 'e2c', 'eL', 'fa', 'par1', 'par2', 'pc', 'udup'), 'VS': 0, 'LOADS': 'Yw Sp Yk Sz0 Yz1 Yr Yx0 Ye Yx1', 'PR': {'Zp': -500, 'cb': 200, 'v1': 500, 'Xrec': 2000, 'f0m': 500, 'hh': -2000, 'k1': 1000, 'q': 1000, 'dup_z': 500, 'kn': -200, 'Zg': -500, 'kf': -2000, 'send_q': 1000, 'eL': -2000, 'qs': 2000, 'nnB': 2000, 'eq': 200, 'cT': 200, 's8': -500, 'pc': -2000, 'F0': -500, 'ku': -500, 'e16': -200, 'keyc': -2000, 'Zabs': 200},
    'BIAS': 4000, 'SLACK': 15, 'ZG': 'S.VV.SS.V', 'SC': ((0, 3), (3, 6)), 'V2': ((0, 96),), 'BC': ((0, 7), (7, 13), (13, 16)), 'RS': ((0, 2), (2, 6)), 'EL': 2, 'RG': 'SS.VV.SS', 'VP': ('SS.S.V.VV', 'S.V.VV.VV'), 'XREC': 'VVSS', 'PREP': 'GGGGVVVVVVSSSSSS', 'RC': 'SSSV', 'TURNS': 1, 'ONS': ('E16', 'F32', 'al', 'c16G', 'cl', 'e2c', 'f0l', 'fa', 'par1', 'par2', 'pc', 'udup'), 'VS': 0, 'LOADS': 'Yw Sp Yk Sz0 Yr Yz1 Yx0 Ye Yx1', 'ZP': ((0, 2), (2, 4), (4, 6)), 'PR': {'send_q': 1000, 'send_z': 500, 'ed': 1000, 'votes': -500, 'eu': 500, 'f0scan': -500, 'Xrec': -2000, 'F0': 2000, 'cb': -200, 'barred': 500, 'votesS': -500, 'e2L': 500, 'e2': 500},
}
EST = {"pe": 1.06, "fixed": {"V": 0.0, "S": 10.0, "P": 0.0, "G": 60.0}, "fac": 1.03, "gather": 1.5, "wake": 215.0, "dma": 1800.0, "send": 1200.0, "issue": 250.0, "rate": 240.0, "dissue": 400.0}
DT = {"i": "int32", "u": "uint16", "f": "float32", "b": "bfloat16", "h": "float16"}
ARENA = {"i": 4096, "u": 2048, "f": 6144, "b": 32768, "h": 4096}
SCRATCH = {"Cm": ("sbuf", [128, 2, 16, 32], "bfloat16")}
for _s in "01":
    SCRATCH["X" + _s] = ("sbuf", [128, XW], "bfloat16")
    SCRATCH["Z" + _s] = ("sbuf", [128, RW], "bfloat16")
    SCRATCH["R" + _s] = ("sbuf", [128, RW], "float32")
    SCRATCH["dz" + _s] = ("sbuf", [128, 6, 16, 16], "bfloat16")
for _k in ARENA:
    SCRATCH["ar_" + _k] = ("sbuf", [128, ARENA[_k]], DT[_k])
PS = tuple(x + s for s in "01" for x in ("d0", "d1", "ma", "mb"))
for _n in PS:
    SCRATCH[_n] = ("psum", [128, 32, 16] if _n[:2] != "ma" else [128, 512], "float32")
DSEM = ["ld_" + k for k in "pwker"] + ["ld_" + k + s for k in "zx" for s in "01"] + ["dup_%s%s%d" % (k, s, t) for k in "zr" for s in "01" for t in range(TT - 1)]
ASEM = ["ar_%s%s%d" % (k, s, t) for k in "pfqz" for s in "01" for t in range(TT)]
SEMAPHORES = ["cV", "cS", "cP", "cG", "sent", "stored"] + DSEM + ASEM
WHERE, TOP, MASKS = {}, {}, {}
PART = {1: slice(0, 64), 2: slice(64, 128), 3: slice(0, 128)}


def need(kind, **names):
    q = 8 if kind in "if" else 16
    for n, w in names.items():
        WHERE[n] = (kind, TOP.get(kind, 0), w)
        TOP[kind] = TOP.get(kind, 0) + -(-w // q) * q
        assert TOP[kind] <= ARENA[kind], kind


def a(n, lo, hi, st=1, h=3):
    if n in PS and n[:2] != "ma":
        if st == 1 and lo % 16 == 0 and hi % 16 == 0:
            return (n, (slice(lo // 16, hi // 16), slice(0, 16)), h)
        raise ValueError((n, lo, hi, st))
    return (n, (slice(lo, hi, st),), h)


def nd(n, *idx):
    return (n, idx, 3)


def ap(T, x):
    n, idx, h = x
    if n in WHERE:
        k, o, w = WHERE[n]
        s = idx[0]
        assert s.stop <= w, x
        n, idx = "ar_" + k, (slice(s.start + o, s.stop + o, s.step),)
    idx = tuple(slice(s.start, s.stop) if isinstance(s, slice) and s.step in (1, None) else s for s in idx)
    return T[n][(PART[h],) + idx]


def dtype(n):
    return DT[WHERE[n][0]] if n in WHERE else SCRATCH[n][2]


def cells(x):
    key = (x[0], str(x[1]))
    if key not in MASKS:
        shape = [WHERE[x[0]][2]] if x[0] in WHERE else SCRATCH[x[0]][1][1:]
        m = np.zeros(shape, bool)
        m[x[1]] = True
        MASKS[key] = (int(m.sum()), int.from_bytes(np.packbits(m.reshape(-1)).tobytes(), "big"))
    return MASKS[key]


def build():
    WHERE.clear()
    TOP.clear()
    ops = []
    cur, seen = [""], {}

    def op(eng, cyc, w, r, fn, name="", kind="c", fix=0.0, gather=False, ni=1, by=0):
        ops.append({"e": eng, "cy": cyc, "fx": fix, "g": gather, "ni": ni, "by": by, "w": w, "r": r, "f": fn, "k": kind, "n": name + cur[0], "s": cur[0]})
        seen[name] = seen.get(name, 0) + 1
        ops[-1]["id"] = (name, cur[0], seen[name])

    def vcyc(xs):
        two = all(dtype(x[0]) in ("bfloat16", "float16", "uint16") for x in xs)
        return max(64, cells(xs[0])[0] * (0.5 if two else 1))

    def vm(o, val):
        op("V", vcyc([o]), [o], [], lambda T, g: g.vector.memset(ap(T, o), val), "memset")

    def gsel(o, i, pat, cmp_, base, cm, name="sel"):
        op("G", 2 * cells(o)[0], [o], [i], lambda T, g: g.affine_select(ap(T, o), ap(T, i), pat, cmp_, 0.0, base, cm), name, fix=170)

    def giota(o, pat, base, cm):
        kw = {} if dtype(o[0]) == "int32" else {"allow_small_or_imprecise_dtypes": True}
        op("G", 2 * cells(o)[0], [o], [], lambda T, g: g.iota(ap(T, o), pat, base, cm, **kw), "iota", fix=130)

    def vs(o, i, s1, op0, s2=None, op1=None, name=""):
        col = [x for x in (s1, s2) if isinstance(x, tuple)]

        def fn(T, g):
            x1, x2 = [ap(T, x) if isinstance(x, tuple) else x for x in (s1, s2)]
            if op1 is None:
                return g.vector.tensor_scalar(ap(T, o), ap(T, i), x1, None, op0)
            return g.vector.tensor_scalar(ap(T, o), ap(T, i), x1, x2, op0, op1)
        op("V", vcyc([i, o]), [o], [i] + col, fn, name)

    def vc(o, i, name=""):
        op("V", vcyc([i, o]), [o], [i], lambda T, g: g.vector.tensor_copy(ap(T, o), ap(T, i)), name)

    def vt(o, x, y, o_, name=""):
        n = cells(o)[0]
        op("V", max(64, n if (x[0] in PS or y[0] in PS) else 2 * n), [o], [x, y], lambda T, g: g.vector.tensor_tensor(ap(T, o), ap(T, x), ap(T, y), o_), name)

    def scan(o, x, y, init, op0, op1, name):
        op("V", vcyc([o, x, y]), [o], [x, y], lambda T, g: g.vector.tensor_tensor_scan(ap(T, o), ap(T, x), ap(T, y), init, op0, op1), name)

    def act(o, i, fn_, bias=0.0, scale=1.0, acc=None, off=None, name=""):
        col = [x for x in (bias, scale) if isinstance(x, tuple)]

        def fn(T, g):
            kw = {"scale": ap(T, scale) if isinstance(scale, tuple) else scale, "bias": ap(T, bias) if isinstance(bias, tuple) else bias}
            if acc:
                kw["accum_out"] = ap(T, acc)
            return g.scalar.activation(ap(T, o), ap(T, i).indirect(ap(T, off)) if off else ap(T, i), fn_, **kw)
        n = cells(o)[0]
        op("S", n if off else max(64, n), [o] + ([acc] if acc else []), [i] + col + ([off] if off else []), fn, name, fix=65 if off else 20 if acc else 0, gather=bool(off))

    def gv(o, win, off, name, y=None, o_=None):
        def fn(T, g):
            ind = ap(T, win).indirect(ap(T, off))
            if y is None:
                return g.vector.tensor_copy(ap(T, o), ind)
            return g.vector.tensor_tensor(ap(T, o), ind, ap(T, y), o_)
        op("V", cells(o)[0], [o], [win, off] + ([y] if y else []), fn, name, fix=50, gather=True)

    def gneg(eng, o, win, off, name):
        if eng == "S":
            act(o, win, F.Identity, scale=-1.0, off=off, name=name)
        else:
            op("V", cells(o)[0], [o], [win, off], lambda T, g: g.vector.tensor_scalar(ap(T, o), ap(T, win).indirect(ap(T, off)), -1.0, None, A.mult), name, fix=50, gather=True)

    def copy(eng, o, i, name, add=0.0):
        if eng == "G":
            gsel(o, i, [[0, cells(o)[0]]], A.is_ge, 0, 0, name)
        elif eng == "S":
            act(o, i, F.Identity, bias=add, name=name)
        elif add:
            vs(o, i, add, A.add, name=name)
        else:
            vc(o, i, name)

    def aff(o, i, mul, add, name, eng=None):
        if name + "G" in CFG["ONS"]:
            copy("G", o, i, name)
        elif eng == "S" or name in CFG["ONS"]:
            act(o, i, F.Identity, bias=add, scale=mul, name=name)
        elif mul == 1 and add == 0:
            vc(o, i, name)
        else:
            vs(o, i, mul, A.mult, add, A.add, name=name)

    def mm(prs, name, start=True, stop=True):
        grs = prs if isinstance(prs[0], list) else [prs]
        cost = sum(max(64, cells(x[2])[0]) * (4 if dtype(x[2][0]) == "float32" else 1) for gr in grs for x in gr)

        def fn(T, g):
            ins = None
            for gr in grs:
                for y, x in enumerate(gr):
                    ins = g.tensor.matmul(ap(T, x[0]), ap(T, x[1]), ap(T, x[2]), start and y == 0, stop and y == len(gr) - 1)
            return ins
        uniq = lambda xs: list({str(x): x for x in xs}.values())
        op("P", cost * 0.5, uniq([x[0] for gr in grs for x in gr]), uniq([y for gr in grs for x in gr for y in x[1:]]), fn, name, ni=sum(map(len, grs)))

    def dma(q, prs, sem, name, by):
        side = lambda T, x: ap(T, x) if isinstance(x, tuple) else x(T)
        w, r = [x[0] for x in prs if isinstance(x[0], tuple)], [x[1] for x in prs if isinstance(x[1], tuple)]
        op(q, 0, w, r, lambda T, q_: [q_.dma_start(side(T, o), side(T, i)) for o, i in prs], name, kind="dma", ni=len(prs), by=by)
        ops[-1]["ds"] = sem

    def send(t, kind, dst, src):
        sem = "ar_%s%s%d" % (kind, cur[0], t)
        by = 128 * cells(src)[0] * (4 if dtype(src[0]) == "float32" else 2)
        op("R", 0, [], [src], (t, [(dst, src)], sem), "send_" + kind, kind="send", by=by)
        op("A", 0, [dst], [], sem, "arr_" + kind, kind="arr")

    need("b", ones=256, w16=144, tmpa=144, BB=128, W=144, I=128, IK=128, BS=2048, smax=768, maskc=NL, half=NL, c1536=NL, c4096=NP_, cbig=NP_, eps=NP_, s2=NL, s4=4 * NP_, IM=128, IN=128, BS4=128, cpar=NL, NJ=NL, ramp=NL, cs=1)
    need("f", iom=NL, M16=16, smin=NL, N32=TT * NL, pcol=1, bar=TT, cb=2 * TT, tab=8)
    need("h", N16=TT * NL)
    need("i", ci=8, cj=8, wtn=1, kmn=1, exn=L, rtn=A0)
    need("b", p0n=L)
    for s in "01":
        need("i", **{x + s: w for x, w in (("wk", 4), ("ki", 2), ("q", NP_), ("r", NP_), ("hh", NP_), ("h4", 4 * NP_), ("ks", NL), ("li", 6), ("yi", NL), ("e2", NL))})
        need("u", **{x + s: w for x, w in (("cl", NP_), ("al", 6), ("el", NL), ("e2l", NL), ("lu", NP_), ("zs", TT * 16), ("zl", TT * 16))})
        need("b", **{x + s: w for x, w in (("qs", TT * NL), ("lo", NL), ("hi", NL))})
        need("f", **{x + s: w for x, w in (("cf", 8), ("v", NL), ("ul", NL), ("uu", 4 * NP_), ("fa", NP_), ("eu", NL), ("ed", NL), ("k2", NL), ("pc", NL), ("f0", NL), ("Fs", TT * NL), ("Fl", TT * NL), ("yo", NL))})
        need("h", **{x + s: w for x, w in (("Wm", 128), ("WH", 128), ("WL", 128), ("E16", NL), ("c16", 64), ("cT", 64), ("e16", NL), ("e2c", NL), ("F16", NL), ("f16", NL), ("p2", NL))})
        need("b", **{x + s: w for x, w in (("p", TT * NL), ("pl", TT * NL), ("kb", NL), ("nt", NP_), ("prep", 16 * NL), ("gz", 768), ("g1", 16 * NL),
                                          ("g2", 16 * NL), ("x1", 32 * NL), ("sg", NL), ("s8", NL), ("nn", NL), ("eq", 768), ("rs", 768))})
    I, W = a("I", 0, 128), lambda k: a("W", 16 - k, 144 - k)

    for x in CFG["LOADS"].split():
        q, k, s = {"Y": "Y", "S": "SD"}[x[0]], x[1], x[2:]
        if not s:
            nm, w = {"p": ("p0", L), "e": ("ex", L), "w": ("wt", 1), "k": ("km", 1), "r": ("rt", A0)}[k]
            prs = [(a(nm + "n", 0, w), lambda T, nm=nm: T[nm][:, :])]
        else:
            nm, buf, c0, c1 = {"z": ("zp", "Z", 0, A0), "x": ("ax", "X", XO, XV)}[k]
            prs = [(a(buf + s, c0, c1, h=1 + h), lambda T, nm=nm, r0=64 * int(s): T[nm][r0:r0 + 64, :]) for h in (0, 1)]
        dma(q, prs, "ld_" + k + s, "ld_" + k + s, (64 * len(prs) if s else 128) * {"p": 384, "e": 768, "w": 4, "k": 4, "z": 2048, "r": 4096, "x": 8192}[k])
        ops[-1]["chain"] = q

    vm(a("ones", 0, 256), 1.0)
    vm(a("w16", 0, 144), 16384.0)
    gsel(a("tmpa", 0, 128), a("ones", 0, 128), [[-16, 8], [0, 16]], A.is_ge, 0, 1)
    gsel(a("BB", 0, 128), a("tmpa", 0, 128), [[16, 8], [0, 16]], A.is_ge, 15, -1)
    gsel(I, a("ones", 0, 128), [[-1, 128]], A.is_equal, 0, 1)
    vm(a("half", 0, NL), -0.5)
    vm(a("c1536", 0, NL), -1536.0)
    vm(a("c4096", 0, NP_), 4096.0)
    vm(a("cbig", 0, NP_), 12582912.0)
    vm(a("eps", 0, NP_), 2.0 ** -13)
    for k, val in enumerate((0.0, -1.0)):
        vm(a("s2", k, NL, 2), val)
    for k, val in enumerate((0.0, 1.0 / 32, 1.0, 1.0)):
        vm(a("s4", k, 4 * NP_, 4), val)
    if "S" in "".join(CFG["VP"]):
        act(a("tab", 0, 4), a("ones", 0, 4), F.Sigmoid, name="table")
    gsel(a("tmpa", 0, 144), a("w16", 0, 144), [[-16, 9], [-1000, 16]], A.is_ge, 16, 1)
    gsel(a("W", 0, 144), a("tmpa", 0, 144), [[16, 9], [0, 16]], A.is_ge, -1, -1)
    for gl in (0, 1):
        vm(nd("Cm", gl, slice(0, 16), slice(16 - 16 * gl, 32 - 16 * gl)), 0.0)
        for h in (0, 1):
            gsel(nd("Cm", gl, slice(0, 16), slice(16 * gl + h, 16 * gl + 16, 2)), a("ones", 0, 128), [[-8, 4], [-32, 4], [-1, 8]], A.is_equal, 0, 1)
    giota(a("iom", 0, NL), [[0, 6], [1, 16]], 0, 0)
    vs(a("smin", 0, NL), a("iom", 0, NL), 0.0, A.is_equal, 33554432.0, A.mult)
    for nm, val in (("IK", 1327104.0), ("IM", 1048576.0), ("IN", -1.0)):
        vs(a(nm, 0, 128), I, val, A.mult)
    giota(a("cj", 0, 1), [[1, 1]], 0, 1)
    vs(a("ci", 0, 1), a("cj", 0, 1), 15, A.bitwise_and)
    vc(a("pcol", 0, 1), a("ci", 0, 1))
    vs(a("M16", 0, 16), a("iom", 0, 16), a("pcol", 0, 1), A.is_equal)
    giota(a("ramp", 0, NL), [[-16, 6], [0, 16]], 0, 0)
    vs(a("maskc", 0, NL), a("iom", 0, NL), a("pcol", 0, 1), A.not_equal, 256.0, A.mult)
    vt(a("ramp", 0, NL), a("ramp", 0, NL), a("maskc", 0, NL), A.add)
    vs(a("maskc", 0, NL), a("ramp", 0, NL), 16384.0, A.mult)
    vm(a("cpar", 0, NL, 2), 8192.0)
    vm(a("cpar", 1, NL, 2), -8192.0)
    vs(a("BS4", 0, 128), a("BB", 0, 128), a("M16", 0, 1), A.mult, -16384.0, A.mult)
    for k in range(16):
        vs(a("BS", 128 * k, 128 * k + 128), a("BB", 0, 128), a("M16", k, k + 1), A.mult, -1.0, A.mult)
    giota(a("N32", 0, TT * NL), [[96, TT], [1, NP_], [0, 2]], B0, 0)
    vs(a("N32", 0, TT * NL, h=2), a("N32", 0, TT * NL, h=2), float(NP_), A.add)
    vs(a("N16", 0, TT * NL), a("N32", 0, TT * NL), -1.0, A.mult, 2048.0, A.add)
    giota(a("smax", 0, 768), [[0, 48], [4096, 16]], 0, 0)
    vm(a("bar", 0, 1), 57344.0)
    for s in "01":
        cf = lambda c: a("cf" + s, c, c + 1)
        for h in (0, 1):
            vc(a("wk" + s, 0, 1, h=1 + h), a("wtn", 0, 1, h=1 + int(s)))
            vc(a("ki" + s, 0, 1, h=1 + h), a("kmn", 0, 1, h=1 + int(s)))
            copy("S", a("p" + s, 0, NL, h=1 + h), a("p0n", NL * h, NL * h + NL, h=1 + int(s)), "p0")
            aff(a("E16" + s, 0, NL, h=1 + h), a("exn", NL * h, NL * h + NL, h=1 + int(s)), 1.0, -2048.0, "E16")
        vs(cf(0), a("wk" + s, 0, 1), 2048.0, A.is_ge)
        vs(cf(1), a("wk" + s, 0, 1), 2.0 ** -12, A.mult, cf(0), A.subtract)
        vs(a("Wm" + s, 0, 128), a("BB", 0, 128), cf(1), A.mult)
        vs(cf(2), a("ki" + s, 0, 1), 1920.0, A.is_ge, 2.0 ** 24, A.mult)
        vs(cf(7), a("ki" + s, 0, 1), 128.0, A.add, 4096.0, A.mult)
        vs(cf(3), cf(7), cf(2), A.subtract)
        vs(a("ki" + s, 1, 2), a("ki" + s, 0, 1), 1, A.bitwise_and)
        vs(cf(4), a("ki" + s, 1, 2), 2048.0, A.mult, -12582912.0, A.add)
        vm(a("uu" + s, 1, 4 * NP_, 4), -0.375)
        vm(a("uu" + s, 2, 4 * NP_, 4), 12582912.0)
        vs(a("wk" + s, 2, 3), a("wk" + s, 0, 1), 63, A.bitwise_and)
        vs(cf(5), a("wk" + s, 2, 3), -2.0 ** -13, A.mult)
        vs(cf(6), cf(1), -0.5, A.mult, cf(5), A.subtract)
        vs(a("WL" + s, 0, 128), a("BB", 0, 128), cf(5), A.mult)
        vs(a("WH" + s, 0, 128), a("BB", 0, 128), cf(6), A.mult)
        vm(a("c16" + s, NP_, 64), 0.0)
        vm(a("X" + s, XV, XW), 0.0)
        for x, e in enumerate(CFG["RC"]):
            w = A0 // len(CFG["RC"])
            for h in (0, 1):
                copy(e, a("R" + s, w * x, w * x + w, h=1 + h), a("rtn", w * x, w * x + w, h=1 + int(s)), "R")

    vs(a("NJ", 0, NL), a("N32", 0, NL), -float(B0), A.add)

    def units(spec):
        out, x = [], 0
        for w in spec.split("."):
            out.append((w[0], x, x + len(w)))
            x += len(w)
        return out

    def round_(t, s):
        n = A0 + L * t
        b = lambda nm, lo, hi, st=1: a(nm + s, lo, hi, st)
        lanes = lambda nm, st=1, ph=0: a(nm + s, ph, NL, st)
        p = lambda st=1, ph=0: b("p", NL * t + ph, NL * t + NL, st)
        bank = [0]

        def dbank():
            bank[0] ^= 1
            return "d%d" % bank[0] + s
        send(t, "p", b("pl", NL * t, NL * t + NL), p())
        both, ps, pq = b("ma", 0, NL), b("ma", 1, NL, 2), b("ma", 0, NL, 2)
        if CFG["QV"]:
            v = lanes("v", 2, 1)
            src = [(b("WH", 0, 128), lanes("p2", 2)), (b("WL", 0, 128), lanes("p2", 2))] if t else [(b("Wm", 0, 128), p(2))]
            mm([(both, I, a("half", 0, NL)), (pq, I, a("eps", 0, NP_))] + [(both, b("Wm", 0, 128), a("c1536", 0, NL))] * (t > 0), "uc", stop=False)
            mm([(o, w, r) for o in (pq, ps) for w, r in src] + [(pq, I, a("cbig", 0, NP_)), (pq, a("IN", 0, 128), a("cbig", 0, NP_))], "u", start=False)
            scan(lanes("v"), a("s2", 0, NL), both, 0.0, A.mult, A.add, "v")
        else:
            v = b("v", 0, NP_)
            if t:
                mm([(ps, b("Wm", 0, 128), a("c1536", 0, NP_)), (ps, I, a("half", 0, NP_))], "uc", stop=False)
                mm([(ps, b("WH", 0, 128), lanes("p2", 2)), (ps, b("WL", 0, 128), lanes("p2", 2))], "u", start=False)
            else:
                mm([(ps, I, a("half", 0, NP_)), (ps, b("Wm", 0, 128), p(2))], "u")
            aff(b("q", 0, NP_), ps, 1.0, 2.0 ** -13, "q")
            vt(v, ps, b("q", 0, NP_), A.subtract, "v")
        act(b("uu", 0, 4 * NP_, 4), v, F.Square, scale=4096.0, name="uu")
        act(b("uu", 3, 4 * NP_, 4), v, F.Identity, bias=b("cf", 4, 5), scale=b("cf", 3, 4), name="ku")
        for h in (0, 1):
            aff(lanes("ul", 2, h), v, 4096.0, 0.0, "udup")
        scan(b("h4", 0, 4 * NP_), a("s4", 0, 4 * NP_), b("uu", 0, 4 * NP_), 0.0, A.mult, A.add, "hh")
        vs(b("hh", 0, NP_), b("h4", 3, 4 * NP_, 4), 4095, A.bitwise_and, name="hm")
        aff(b("cl", 0, NP_), b("hh", 0, NP_), n / 4096.0, -0.5 + 2.0 ** -13, "cl")
        for k, e in enumerate(CFG["PREP"]):
            if e == "G" or t == 0:
                copy(e, b("prep", k, 16 * NL, 16), p(), "prep")
            else:
                aff(b("prep", k, 16 * NL, 16), lanes("p2"), -0.5, -1536.0, "prep", e)
        aff(b("c16", 0, NP_), b("cl", 0, NP_), 1.0, 0.0, "c16")
        op("V", 64, [b("cT", 0, 64)], [b("c16", 0, 64)], lambda T, g: g.vector.transpose(ap(T, b("cT", 0, 64)), ap(T, b("c16", 0, 64))), "cT")
        key = b("ma", 96, 192)
        mm([(key, I, a("iom0", 0, NL))] + [(b("ma", 96 + 16 * hi, 112 + 16 * hi), nd("Cm", gl, slice(hi % 4 * 4, hi % 4 * 4 + 4), slice(0, 32)), b("cT", 32 * (hi // 4) + 16 * gl, 32 * (hi // 4) + 16 * gl + 16))
                                          for hi in range(6) for gl in (0, 1)], "keyc", stop=False)
        for e, x0, x1 in units(CFG["ZG"]):
            gneg(e, b("gz", 128 * x0, 128 * x1), b("Z", 0, n), b("cl", 8 * x0, 8 * x1), "Zg")
        for y, (x0, x1) in enumerate(CFG["ZP"]):
            d, w = ("d0", "d1", "mb")[y % 3] + s, x1 - x0
            if y < CFG["ZD"]:
                pp = b("p", NL * t + 16 * x0, NL * t + 16 * x1)
                mm([(a(d, 0, 256 * w), a("zero", 0, 128), a("BS", 0, 256 * w))] * CFG["ZZ"] + [(nd(d, slice(0, 16 * w), m), I, pp) for m in range(16)], "Zp", stop=False)
            else:
                mm([(a(d, 0, 256 * w), I, b("prep", 256 * x0, 256 * x1))], "Zp", stop=False)
            mm([(nd(d, slice(h, 16 * w, 2), slice(0, 16)), I, b("gz", 128 * x0, 128 * x1)) for h in (0, 1)], "Zsub", start=False)
            act(nd("dz" + s, slice(x0, x1), slice(0, 16), slice(0, 16)), a(d, 0, 256 * w), F.Abs, scale=0.25, name="Zabs")
        for h0, h1 in CFG["SC"]:
            mm([(b("ma", 96 + 16 * h0, 96 + 16 * h1), W(lo), nd("dz" + s, slice(h0, h1), lo, slice(0, 16))) for lo in range(16)], "score", start=False, stop=h1 == 6)
        scan(lanes("ks"), a("smin", 0, NL), key, 33554432.0, A.max, A.min, "kmin")
        if CFG["BU"]:
            vs(b("al", 0, 6), lanes("ks", 16, 15), 4095, A.bitwise_and, name="lm")
        else:
            vs(b("li", 0, 6), lanes("ks", 16, 15), 4095, A.bitwise_and, name="lm")
            aff(b("al", 0, 6), b("li", 0, 6), 1.0, 0.0, "al")
        act(lanes("ed"), b("R", 0, n), F.Identity, scale=2080.0, bias=2464.0 * t - 4194304.0, off=b("al", 0, 6), name="ed")
        if CFG["EL"] < 2:
            act(lanes("e16"), b("R", 0, n), F.Identity, bias=-2048.0, off=b("al", 0, 6), name="e16")
        if CFG["EL"]:
            gv(lanes("el"), b("R", 0, n), b("al", 0, 6), "eL")
        if CFG["EL"] == 2:
            aff(lanes("e16"), lanes("el"), 1.0, -2048.0, "e16")
        gv(lanes("eu"), b("R", 0, n), b("al", 0, 6), "eu", lanes("ul"), A.mult)
        if not CFG["EL"]:
            aff(lanes("el"), lanes("e16"), 1.0, 2048.0, "eL")
        vt(lanes("yi"), lanes("eu"), lanes("ed"), A.add, "yi")
        vs(lanes("e2l" if CFG["BU"] else "e2"), lanes("yi"), 5, A.arith_shift_right, 4095, A.bitwise_and, name="e2")
        if not CFG["BU"]:
            aff(lanes("e2l"), lanes("e2"), 1.0, 0.0, "e2L")
        aff(lanes("e2c"), lanes("e2l"), 1.0, -2048.0, "e2c")
        v1, k3, v2 = b("ma", 192, 288), b("ma", 288, 384), b("mb", 96, 192)
        for w, (lst, gb) in enumerate((("el", "g1"), ("e2l", "g2"))):
            for e, x0, x1 in units(CFG["VP"][w]):
                c0, c1 = 256 * x0, 256 * x1
                if e == "V":
                    gv(b(gb, c0, c1), b("X", XO, XV), b(lst, 16 * x0, 16 * x1), "votes", b("prep", c0, c1), A.is_ge)
                else:
                    xs = b("x1", 1536 * w + c0, 1536 * w + c1)
                    act(xs, b("X", XO, XV), F.Identity, scale=-1.0, off=b(lst, 16 * x0, 16 * x1), name="votesS")
                    d = a(dbank(), 0, c1 - c0)
                    if CFG["VS"]:
                        mm([(d, I, b("prep", c0, c1))], "vp", stop=False)
                    mm([(d, I, b("prep", c0, c1))] * (1 - CFG["VS"]) + [(d, I, xs)], "vsub", start=not CFG["VS"])
                    act(b(gb, c0, c1), d, F.Sigmoid, bias=128.0, scale=-256.0, name="vsig")
            if w == 0:
                mm([(v1, I, lanes("e16"))] + [(v1, W(k), b(gb, k, 16 * NL, 16)) for k in range(16)], "v1")
                act(lanes("s8"), v1, F.Sign, scale=-1.0, bias=139264.0, name="s8")
                act(lanes("sg"), v1, F.Sign, scale=-1.0, bias=a("bar", t, t + 1), acc=a("cb", 2 * t + int(s), 2 * t + int(s) + 1), name="barred")
                act(lanes("k2"), v1, F.Identity, bias=1040384.0, name="k1")
                mm([(k3, I, lanes("E16")), (k3, a("IK", 0, 128), lanes("sg"))], "k3")
                vt(lanes("k2"), k3, lanes("k2"), A.max, "m13")
                if s == "1" and t < TT - 1:
                    par = b("ma", 500, 501)
                    act(a("cs", 0, 1), a("cb", 2 * t, 2 * t + 1), F.Identity, bias=a("cb", 2 * t + 1, 2 * t + 2), name="par")
                    mm([(par, a("ones", 0, 128), a("cs", 0, 1))], "par")
                    aff(a("ci", 4, 5), par, 1.0, 0.0, "par1")
                    vs(a("ci", 5, 6), a("ci", 4, 5), 1, A.arith_shift_right, 1, A.bitwise_and, name="par")
                    aff(a("bar", t + 1, t + 2), a("ci", 5, 6), 16384.0, 57344.0, "par2")
            else:
                for l0, l1 in CFG["V2"]:
                    o = b("mb", 96 + l0, 96 + l1)
                    mm([(o, I, b("e2c", l0, l1))] + [(o, W(k), b(gb, 16 * l0 + k, 16 * l1, 16)) for k in range(16)] + [(o, a("IM", 0, 128), b("s8", l0, l1))], "v2")
        vt(lanes("kb"), v2, lanes("k2"), A.max, "m2")
        vt(b("mb", 0, NL), v2, lanes("k2"), A.max, "m2")
        vt(lanes("f16"), b("mb", 0, NL), lanes("kb"), A.subtract, "f16")
        ca, cb, fn_ = b("mb", 240, 288), b("mb", 192, 240), b("mb", 336, 432)
        for k0, k1 in CFG["BC"]:
            d = dbank()
            mm([[(a(d, 48 * k, 48 * k + 48), a("BS", 128 * (k0 + k), 128 * (k0 + k) + 128), lanes("f16", 2, 1)), (a(d, 48 * k, 48 * k + 48), I, lanes("f16", 2))] for k in range(k1 - k0)], "bcast")
            vs(b("eq", 48 * k0, 48 * k1), a(d, 0, 48 * (k1 - k0)), 0.0, A.is_equal, 16384.0, A.mult, name="eq")
        kf, kn = b("ma", 192, 288), b("ma", 384, 480)
        ends = [("lo", B0 + 96 * t, -1.0), ("hi", B0 + 96 * t + 96, 1.0)][:2 - t // 3]
        for nm, c0, sg in ends:
            vs(lanes(nm), lanes("f16"), c0 - 2048.0, A.is_ge, sg * (B0 + 192 * t + 96), A.mult, name="ends")
        mm([(kf, I, a("maskc", 0, NL))] + [(kf, a("BS", 0, 128), lanes(nm)) for nm in ["f16"] + [x[0] for x in ends]], "kf")
        act(lanes("f0"), kf, F.Identity, scale=-1.0, bias=2048.0 + 96 * t + 96, name="kf")
        mm([(kn, a("IN", 0, 128), a("maskc", 0, NL)), (kn, I, a("cpar", 0, NL)), (kn, I, a("NJ", 0, NL)),
            (b("ma", 385, 480, 2), a("BB", 0, 128), b("eq", 0, NP_))], "kn", stop=False)
        aff(b("fa", 0, NP_), lanes("f16", 2), 1.0, 2048.0, "fa")
        for k0, k1 in CFG["BC"]:
            mm([(ca, I, a("c4096", 0, NP_))] * (k0 == 0) + [(ca, a("IN", 0, 128), b("eq", 48 * k, 48 * k + 48)) for k in range(k0, k1)], "ca", start=k0 == 0, stop=k1 == 16)
        vt(b("lu", 0, NP_), ca, b("fa", 0, NP_), A.max, "lu")
        act(lanes("nn", 2), ca, F.Relu, scale=2.0 ** -12, name="nn")
        mm([(b("ma", 384, 480, 2), a("BS4", 0, 128), lanes("nn", 2))], "F0", start=False)
        scan(lanes("yi"), kn, lanes("f0"), -1.0, A.max, A.max, "f0scan")
        vs(b("li", 0, 6), lanes("yi", 16, 15), 8191, A.bitwise_and, name="f0m")
        aff(b("zs", 16 * t, 16 * t + 6), b("li", 0, 6), 1.0, 0.0, "f0l")
        send(t, "z", b("zl", 16 * t, 16 * t + 6), b("zs", 16 * t, 16 * t + 6))
        mm([[(cb, W(k), b("eq", 48 * k, 48 * k + 48)) for k in range(16)], [(fn_, I, lanes("f16")), (fn_, I, a("N16", NL * t, NL * t + NL))]], "cb")
        act(lanes("nn", 2, 1), cb, F.Relu, bias=1.0, scale=-1.0, name="nnB")
        for e, x0, x1 in units(CFG["RG"]):
            if e == "V":
                gv(b("gz", 128 * x0, 128 * x1), b("X", XO, XW), b("lu", 8 * x0, 8 * x1), "rg")
            else:
                act(b("gz", 128 * x0, 128 * x1), b("X", XO, XW), F.Identity, off=b("lu", 8 * x0, 8 * x1), name="rg")
        Fs = b("Fs", NL * t, NL * t + NL)
        vt(fn_, fn_, lanes("nn"), A.mult, "delta")
        vt(lanes("F16"), fn_, a("N16", NL * t, NL * t + NL), A.subtract, "F")
        aff(Fs, lanes("F16"), 1.0, 2048.0, "F32")
        send(t, "f", b("Fl", NL * t, NL * t + NL), Fs)
        for x0, x1 in CFG["RS"]:
            scan(b("rs", 128 * x0, 128 * x1), a("smax", 0, 128 * (x1 - x0)), b("gz", 128 * x0, 128 * x1), 0.0, A.min, A.max, "rscan")
        for x, e in enumerate(CFG["XREC"]):
            c0 = NL * t + NP_ * (x % 2)
            copy(e, a("qs" + s, c0, c0 + NP_, h=1 + x // 2), a("rs" + s, 15, 768, 16, h=1 + x % 2), "qs")
        land = XO - 96 * t - 96
        send(t, "q", b("X", land, land + 96), b("qs", NL * t, NL * t + NL))
        if t < TT - 1:
            for k, tab, src, c0, by in (("z", "Z", "pl", NL * t, 2), ("r", "R", "Fl", NL * t, 4)):
                dma("Y", [(a(tab + s, n + NL * h, n + NL * h + NL, h=1 + h2), a(src + s, c0, c0 + NL, h=1 + h)) for h in (0, 1) for h2 in (0, 1)], "dup_%s%s%d" % (k, s, t), "dup_" + k, 256 * NL * by)
        r0 = 64 * int(s)
        dma("Y", [(lambda T, h=h: T["yr"][r0:r0 + 64, L * t + NL * h:L * t + NL * h + NL], a("Fl" + s, NL * t, NL * t + NL, h=1 + h)) for h in (0, 1)], None, "yr", 128 * NL * 4)
        aff(lanes("pc"), b("pl", NL * t, NL * t + NL), 1.0, 3326.5, "pc")
        gv(lanes("p2"), b("X", land, XV), b("zl", 16 * t, 16 * t + 6), "newp", lanes("pc"), A.subtract)
        if t < TT - 1:
            aff(b("X", XO + B0 + 96 * t, XO + B0 + 96 * t + 96), b("X", land, land + 96), 1.0, 0.0, "Xrec")
            aff(b("p", NL * t + NL, NL * t + 2 * NL), lanes("p2"), -0.5, -1536.0, "p")
        else:
            aff(lanes("yo"), lanes("p2"), -0.5, -1536.0, "yo")
            for h, q in enumerate(("Y", "SD")):
                dma(q, [(lambda T, h=h: T["yp"][r0:r0 + 64, NL * h:NL * h + NL], a("yo" + s, 0, NL, h=1 + h))], None, "yp", 64 * NL * 4)

    need("b", iom0=NL)
    vm(a("iom0", 0, NL), 0.0)
    for t in range(TT):
        for s in "01":
            cur[0] = s
            seen.clear()
            round_(t, s)
    return ops


COMP = "VSPG"
ONQ = {"R": "G", "SD": "S"}


def deps_of(ops):
    hist, bank, chain = {}, {}, {}
    for i, o in enumerate(ops):
        raw, war = set(), set()
        rd, wr = [(x[0], x[2], cells(x)[1]) for x in o["r"]], [(x[0], x[2], cells(x)[1]) for x in o["w"]]
        for n, h, m in rd:
            raw |= {j for (h2, m2, j, w) in hist.get(n, ()) if w and h & h2 and m & m2}
        for n, h, m in wr:
            raw |= {j for (h2, m2, j, w) in hist.get(n, ()) if h & h2 and m & m2}
        banks = {x[0] for x in rd + wr if x[0] in PS}
        for n in banks:
            war |= set(bank.setdefault(n, {}).values())
        if "chain" in o:
            war |= set(chain.get(o["chain"], ()))
            chain[o["chain"]] = [i]
        for n, h, m in rd:
            hist.setdefault(n, []).append((h, m, i, False))
        for n, h, m in wr:
            hist[n] = [y for y in hist.get(n, ()) if y[2] == i or y[0] & ~h or y[1] & ~m] + [(h, m, i, True)]
        for n in banks:
            bank[n][o["e"]] = i
        raw.discard(i)
        war.discard(i)
        o["raw"], o["war"] = raw, war - raw
    above = []
    for i, o in enumerate(ops):
        pre = [(j, no_wait(ops[j], o, j)) for j in o["raw"] | o["war"] | ({i - 1} if o["k"] == "arr" else set())]
        implied = whole = 0
        for j, free in pre:
            whole |= above[j] | 1 << j
            implied |= 0 if free else above[j]
        above.append(whole)
        o["pre"] = [(j, free) for j, free in pre if ops[j]["k"] != "c" or not implied >> j & 1]


def no_wait(p, o, j):
    same = ONQ.get(p["e"], p["e"]) == ONQ.get(o["e"], o["e"])
    return same and ("chain" in o and "chain" in p or p["k"] == "c" and (j not in o["raw"] and p["e"] != "G" or o["e"] == "P"))


def schedule(ops):
    n = len(ops)
    succ = [[] for _ in range(n)]
    wake = EST["wake"]
    for i, o in enumerate(ops):
        for j, free in o["pre"]:
            succ[j].append((i, free, 0.0 if o["k"] == "arr" else wake))
    cost = [{"send": EST["issue"], "dma": EST["dissue"] * o["ni"], "arr": 0.0}.get(o["k"], (o["cy"] * 0.83 * (EST["gather"] if o["g"] else 1) + o["fx"]) * EST["fac"] * (EST["pe"] if o["e"] == "P" else 1) + EST["fixed"][o["e"]] * o["ni"] if o["k"] == "c" else 0.0) for o in ops]
    lat = [{"dma": EST["dma"], "send": EST["send"]}.get(o["k"], 0.0) + o["by"] / EST["rate"] for o in ops]
    queue = [ONQ.get(o["e"], o["e"]) for o in ops]
    prio = [0.0] * n
    for i in range(n - 1, -1, -1):
        tail = CFG["BIAS"] if ops[i]["s"] == "0" else 0.0
        prio[i] = max([tail + cost[i] + lat[i]] + [prio[j] + cost[i] + (0.0 if fr else lat[i] + w) for j, fr, w in succ[i]])
    prio = [prio[i] + CFG["PR"].get(o["n"][:-1], 0.0) for i, o in enumerate(ops)]
    nd_ = [len(o["pre"]) for o in ops]
    ready = [0.0] * n
    free = {q: 0.0 for q in "VSPGYA"}
    avail = {q: [] for q in "VSPGYA"}
    for i in range(n):
        if nd_[i] == 0:
            avail[queue[i]].append(i)
    order, pipe, fin, start = [], 0.0, [0.0] * n, [0.0] * n
    while len(order) < n:
        best = None
        for q in avail:
            if avail[q]:
                tmin = min(max(free[q], ready[i]) for i in avail[q])
                i = max((i for i in avail[q] if max(free[q], ready[i]) <= tmin + CFG["SLACK"]), key=lambda i: prio[i])
                st = max(free[q], ready[i])
                if best is None or st < best[0]:
                    best = (st, q, i)
        st, q, i = best
        avail[q].remove(i)
        order.append(i)
        fin[i] = st + cost[i] + lat[i]
        if ops[i]["k"] == "dma":
            pipe = max(pipe, st + cost[i]) + ops[i]["by"] / EST["rate"]
            fin[i] = pipe + EST["dma"]
        if q != "A":
            free[q] = st + cost[i]
        for j, fr, w in succ[i]:
            ready[j] = max(ready[j], st if fr else fin[i] + w)
            nd_[j] -= 1
            if nd_[j] == 0:
                avail[queue[j]].append(j)
        start[i] = st
    lat = [fin[i] - start[i] - cost[i] for i in range(n)]
    bwd = [[(j, cost[j] + (0.0 if fr else lat[i] + w)) for j, fr, w in succ[i]] for i in range(n)]
    fwd = [[] for _ in range(n)]
    for i in range(n):
        for j, d in bwd[i]:
            fwd[j].append((i, d - cost[j] + cost[i]))

    def place(seq, pred, first):
        at, used = [0.0] * n, {q: [] for q in free}
        for i in seq:
            t, u, c = max([first[i]] + [at[j] + d for j, d in pred[i]]), used[queue[i]], cost[i]
            lo, hi = 0, len(u)
            while lo < hi:
                mid = (lo + hi) // 2
                lo, hi = (mid + 1, hi) if u[mid][1] <= t else (lo, mid)
            while lo < len(u) and u[lo][0] < t + c:
                t, lo = max(t, u[lo][1]), lo + 1
            if c:
                u.insert(lo, (t, t + c))
            at[i] = t
        return at
    span = lambda at: max(at[i] + cost[i] + lat[i] for i in range(n))
    best = start
    for _ in range(CFG["TURNS"]):
        back = place(sorted(range(n), key=lambda i: (-start[i] - cost[i], -i)), bwd, lat)
        start = place(sorted(range(n), key=lambda i: (-back[i] - cost[i], i)), fwd, [0.0] * n)
        if span(start) < span(best):
            best = start
    rng, end = np.random.default_rng(CFG["SEED"]), span(best)
    kinds = {}
    kind = np.array([kinds.setdefault(o["id"], len(kinds)) for o in ops])
    for _ in range(CFG["SHAKES"]):
        shift = np.zeros(len(kinds))
        for x in rng.integers(0, n, rng.integers(1, 4)):
            shift[kind[x]] = rng.choice((-1.0, 1.0)) * rng.choice((100.0, 300.0, 700.0, 1500.0))
        key = list(np.array(best) + shift[kind])
        for j in range(n):
            for i, d in fwd[j]:
                if key[j] <= key[i]:
                    key[j] = key[i] + 1e-3
        start = place(sorted(range(n), key=lambda i: key[i]), fwd, [0.0] * n)
        if span(start) + CFG["LAM"] * sum(start) / n <= end + CFG["LAM"] * sum(best) / n + CFG["TEMP"] * rng.random() * (1 - _ / CFG["SHAKES"]):
            best, end = start, span(start)
    return sorted(range(n), key=lambda i: (best[i], i)), span(best)


PLAN = []


def plan():
    if PLAN:
        return PLAN[0]
    ops = build()
    deps_of(ops)
    order, end = schedule(ops)
    cnt = {e: 0 for e in COMP}
    known = {q: {} for q in "VSPGY"}
    clock, steps, nsent, nst, dsem = {}, [], 0, 0, {}
    for i in order:
        o = ops[i]
        e, k = o["e"], o["k"]
        q = ONQ.get(e, e)
        if k == "arr":
            o["sem"] = (o["f"], 16)
            clock[i] = {o["f"]: 16}
            continue
        cl, req = known[q], {}
        for j in o["raw"] | o["war"]:
            p = ops[j]
            if no_wait(p, o, j):
                continue
            sem, val = p["sem"]
            if cl.get(sem, 0) < val and (sem not in req or ops[req[sem]]["sem"][1] < val):
                req[sem] = j
        for sem in list(req):
            val = ops[req[sem]]["sem"][1]
            if any(s2 != sem and clock[j2].get(sem, 0) >= val for s2, j2 in req.items()):
                del req[sem]
        for sem, j in req.items():
            for x, y in clock[j].items():
                cl[x] = max(cl.get(x, 0), y)
        waits = sorted((sem, ops[j]["sem"][1]) for sem, j in req.items())
        inc = None
        if k == "c":
            cnt[e] += 1
            inc = "c" + e
            o["sem"] = (inc, cnt[e])
        elif k == "dma" and o["ds"]:
            inc = o["ds"]
            o["sem"] = (inc, 16 * o["ni"])
            dsem[inc] = 16 * o["ni"]
        elif k == "dma":
            nst += o["ni"]
            inc = "stored"
        else:
            nsent += 1
        if "sem" in o:
            clock[i] = dict(cl)
            clock[i][o["sem"][0]] = o["sem"][1]
        steps.append((q, waits, o, inc))
    PLAN.append((steps, cnt, nsent, nst, dsem, end))
    return PLAN[0]


def rank_program(g, core, T, topo):
    rank = T.rank_of(core)
    if rank is None:
        return
    steps, cnt, nsent, nst, dsem = plan()[:5]
    qs = {"V": g.vector, "S": g.scalar, "P": g.tensor, "G": g, "Y": g.sync}
    for q, waits, o, inc in steps:
        for sem, val in waits:
            qs[q].wait_ge(T.sem[sem], int(val))
        if o["k"] == "send":
            t, prs, ar = o["f"]
            to = T.cores[(rank + 1 + (t % 3)) % len(T.cores)]
            rid, pid, _se = topo.addr(to)
            g.remote_dma(ap(T, prs[0][0]), ap(T, prs[0][1]), T.sem[ar], T.sem.sent, pid, rid, topo.mask(core, to))
        elif o["k"] == "dma":
            for ins in o["f"](T, qs[q]):
                ins.then_inc(T.sem[inc], 16)
        else:
            o["f"](T, g).then_inc(T.sem[inc], 1)
    for e in COMP:
        g.sync.wait_ge(T.sem["c" + e], int(cnt[e]))
    for sem in DSEM:
        g.sync.wait_ge(T.sem[sem], dsem[sem])
    for sem in ASEM:
        g.sync.wait_ge(T.sem[sem], 16)
    g.sync.wait_ge(T.sem.stored, 16 * nst)
    g.wait_ge(T.sem.sent, 16 * nsent)
